import numpy as np
import ml_dtypes


def mxq(x, axis, fmt="e4m3"):
    dtype, down = {"e4m3": (ml_dtypes.float8_e4m3fn, 7), "e5m2": (ml_dtypes.float8_e5m2, 14)}[fmt]
    v = np.moveaxis(np.asarray(x, np.float32).astype(ml_dtypes.bfloat16).astype(np.float64), axis, -1)
    blocks = v.reshape(v.shape[:-1] + (-1, 32))
    amax = np.abs(blocks).max(-1, keepdims=True)
    byte = np.maximum(np.where(amax > 0, np.frexp(amax)[1] - 1 + 127, 0) - down, 1)
    scale = np.exp2(byte - 127.0)
    codes = (blocks / scale).astype(np.float32).astype(dtype).astype(np.float64)
    return np.moveaxis((codes * scale).reshape(v.shape), -1, axis)


WIDE = False


def mx_kscale(k):
    if not WIDE:
        return np.ones(k)
    levels = np.array([30, -30])
    if k % 512:
        return np.exp2(np.random.permutation(np.resize(levels, k // 32))).repeat(32)
    a = np.empty((k // 512, 16))
    for p in range(k // 512):
        a[p, :8] = np.random.permutation(np.resize(levels, 8))
        for g in range(8):
            far = levels[np.abs(levels - a[p, g]) >= 10]
            a[p, g + 8] = far[np.random.randint(len(far))]
    return np.exp2(a.ravel()).repeat(32)


BF16 = ml_dtypes.bfloat16


def bf(x):
    return np.asarray(x, np.float32).astype(BF16)


def f64(x):
    return np.asarray(x).astype(np.float64)


E2M1 = np.array([0.0, 0.5, 1.0, 1.5, 2.0, 3.0, 4.0, 6.0, -0.0, -0.5, -1.0, -1.5, -2.0, -3.0, -4.0, -6.0])


def pack_weight(w, fmt):
    k, n = w.shape
    w = f64(bf(w)).reshape(k // 32, 32, n)
    amax = np.abs(w).max(1)
    if fmt == "e4m3":
        byte = np.frexp(amax)[1] - 1 + 127 - 7
    else:
        mant, ex = np.frexp(amax / 6.0)
        byte = np.where(mant > 0.5, ex, ex - 1) + 127
    byte = np.clip(np.where(amax > 0, byte, 1), 1, 254)
    scaled = (w * np.exp2(127.0 - byte)[:, None, :]).reshape(k, n).astype(np.float32)
    by_word = np.ascontiguousarray(scaled.reshape(k // 512, 128, 4, n).transpose(0, 1, 3, 2))
    if fmt == "e4m3":
        words = by_word.astype(ml_dtypes.float8_e4m3fn).view(np.uint8)
    else:
        c = by_word.astype(ml_dtypes.float4_e2m1fn).view(np.uint8) & 0xF
        words = c[..., 0::2] | (c[..., 1::2] << 4)
    return np.ascontiguousarray(words), np.ascontiguousarray(byte.astype(np.uint8).reshape(k // 512, 16, n))


def unpack_weight(words, scales, fmt):
    g, p, n, _ = words.shape
    if fmt == "e4m3":
        vals = np.ascontiguousarray(words).view(ml_dtypes.float8_e4m3fn).astype(np.float64)
    else:
        nib = np.empty((g, p, n, 4), np.uint8)
        nib[..., 0::2] = words & 0xF
        nib[..., 1::2] = words >> 4
        vals = E2M1[nib]
    vals = vals * np.repeat(np.exp2(scales.astype(np.float64) - 127.0), 8, axis=1)[..., None]
    return vals.transpose(0, 1, 3, 2).reshape(g * 512, n)
def pack4(w):
    words, scales = pack_weight(w, "e2m1")
    return words.reshape(words.shape[0], 128, -1), scales


def unpack4(words, scales):
    return unpack_weight(words.reshape(words.shape[0], 128, -1, 2), scales, "e2m1")


T, O, F, C = 1024, 2048, 1024, 1024


def setup_inputs():
    s, u = mx_kscale(O), mx_kscale(T)
    v = np.random.standard_normal((O, F)) / np.sqrt(O) / s[:, None]
    v_words, v_scales = pack4(v)
    return {"delta": bf(0.2 * np.random.standard_normal((T, O)) * s / u[:, None]),
            "v_words": v_words,
            "v_scales": v_scales,
            "gain": bf(1 + 0.1 * np.random.standard_normal(F)),
            "x": bf(np.random.standard_normal((T, C)) * u[:, None]),
            "lo": bf(-(0.8 + 0.4 * np.random.random(T)) * u),
            "hi": bf((1.2 + 0.4 * np.random.random(T)) * u),
            "w": bf(np.random.standard_normal((C, F)) / np.sqrt(C)),
            "r": bf((1.0 + 0.5 * np.random.random(F)) / np.sqrt(C))}


def reference(delta, v_words, v_scales, gain, x, lo, hi, w, r):
    back = mxq(f64(delta), 1, "e4m3") @ unpack4(v_words, v_scales)
    e = back * f64(gain)
    xc = np.minimum(np.maximum(f64(x), f64(lo)[:, None]), f64(hi)[:, None])
    dw = mxq(xc, 0, "e4m3").T @ mxq(e, 0, "e5m2")
    inside = np.abs(f64(w)) <= f64(r)
    return dw * inside

@@ -1,0 +1,345 @@
+from contextlib import ExitStack
+
+import concourse.mybir as mybir
+from concourse.masks import make_identity
+
+T, O, F, C = 1024, 2048, 1024, 1024
+FLOPS = 2 * T * O * F + 2 * T * F * C
+
+F32 = mybir.dt.float32
+BF16 = mybir.dt.bfloat16
+I32 = mybir.dt.int32
+U32 = mybir.dt.uint32
+U8 = mybir.dt.uint8
+E4M3 = mybir.dt.float8_e4m3fn_x4
+E5M2 = mybir.dt.float8_e5m2_x4
+E2M1 = mybir.dt.float4_e2m1fn_x4
+OP = mybir.AluOpType
+ACT = mybir.ActivationFunctionType
+
+P = 128
+KG = O // 512
+TG = T // 512
+
+
+def tile_straight_through_weight_gradient_s9_kernel(
+    tc, delta, v_words, v_scales, gain, x, lo, hi, w, r, out
+):
+    nc = tc.nc
+    with ExitStack() as ctx:
+        keep = ctx.enter_context(tc.tile_pool(name="keep", bufs=1))
+        stage = ctx.enter_context(tc.tile_pool(name="stage", bufs=3))
+        outs = ctx.enter_context(tc.tile_pool(name="outs", bufs=16))
+        psum = ctx.enter_context(tc.psum_pool(name="psum", bufs=1))
+        ctx.enter_context(tc.manual_schedule())
+
+        vs = keep.tile([P, KG, F], U8, align_bytes=64)
+        nc.vector.memset(vs[:].rearrange("p g n -> p (g n)").bitcast(I32), 0)
+        warm = keep.tile([P, 1], F32)
+        nc.vector.memset(warm[:], 0.0)
+        warm2 = keep.tile([P, 1], F32)
+        nc.scalar.activation(out=warm2[:], in_=warm[:], func=ACT.Abs)
+        ident = keep.tile([P, P], F32)
+        make_identity(nc, ident[:])
+        lo_sb = keep.tile([P, TG, 4], BF16)
+        hi_sb = keep.tile([P, TG, 4], BF16)
+
+        delta_v = delta.rearrange("(g m t) k -> g t m k", m=P, t=4)
+        x_v = x.rearrange("(g p j) c -> g p j c", p=P, j=4)
+        w_v = w.rearrange("(ct p) f -> p ct f", p=P)
+        vw_v = v_words.rearrange("g p b -> p g b")
+        vs_v = v_scales.rearrange("g q n -> q g n").bitcast(I32)
+
+        d_sb = [keep.tile([P, O], BF16, name=f"d_sb{i}") for i in range(8)]
+        vw = [keep.tile([P, KG, F], U8, name=f"vw{h}", align_bytes=64) for h in range(2)]
+        gain_bc = keep.tile([P, F], BF16)
+        r_bc = keep.tile([P, F], BF16)
+        x_sb = [keep.tile([P, 4, C], BF16, name=f"x_sb{g}") for g in range(TG)]
+        w_sb = keep.tile([P, 8, F], BF16)
+
+        def load_d(i, pieces=1):
+            n = O // pieces
+            for k in range(pieces):
+                nc.sync.dma_start(
+                    out=d_sb[i][:, k * n : (k + 1) * n],
+                    in_=delta_v[i // 4, i % 4, :, k * n : (k + 1) * n],
+                )
+
+        def load_vs():
+            for q in range(4):
+                nc.sync.dma_start(
+                    out=vs[32 * q : 32 * q + 4, :, :].bitcast(I32), in_=vs_v[4 * q : 4 * q + 4, :, :]
+                )
+
+        def load_vw(h):
+            nc.sync.dma_start(out=vw[h][:], in_=vw_v[:, :, h * F : (h + 1) * F])
+
+        def load_x(g, a):
+            if True:
+                nc.sync.dma_start(out=x_sb[g][:, 2 * a : 2 * a + 2, :], in_=x_v[g, :, 2 * a : 2 * a + 2, :])
+
+        def load_w(a):
+            nc.sync.dma_start(out=w_sb[:, 2 * a : 2 * a + 2, :], in_=w_v[:, 2 * a : 2 * a + 2, :])
+
+        nc.gpsimd.dma_start(out=lo_sb[:], in_=lo.rearrange("(g p j) -> p g j", p=P, j=4))
+        nc.gpsimd.dma_start(out=hi_sb[:], in_=hi.rearrange("(g p j) -> p g j", p=P, j=4))
+        loads = "d0 d1 d2 vs d3 vh0 d4 x0a d5 x0b gain d6 vh1 d7 x1a x1b w0 r w1 w2 w3"
+        for word in loads.split():
+            if word == "vs":
+                load_vs()
+            elif word == "gain":
+                nc.sync.dma_start(out=gain_bc[:], in_=gain.partition_broadcast(P))
+            elif word == "r":
+                nc.sync.dma_start(out=r_bc[:], in_=r.partition_broadcast(P))
+            elif word[0] == "v":
+                load_vw(int(word[2]))
+            elif word[0] == "x":
+                load_x(int(word[1]), {"a": 0, "b": 1}[word[2]])
+            elif word[0] == "w":
+                load_w(int(word[1]))
+            else:
+                load_d(int(word[1]), 2 if word == "d0" else 1)
+
+        d_codes = [keep.tile([P, 512], U32, name=f"d_codes{i}", align_bytes=64) for i in range(8)]
+        d_scales = [keep.tile([P, 512], U8, name=f"d_scales{i}", align_bytes=64) for i in range(8)]
+        x_grp = [keep.tile([P, C, 4], BF16, name=f"x_grp{g}", align_bytes=64) for g in range(TG)]
+        x_codes = [keep.tile([P, C], U32, name=f"x_codes{g}", align_bytes=64) for g in range(TG)]
+        x_scales = [keep.tile([P, C], U8, name=f"x_scales{g}", align_bytes=64) for g in range(TG)]
+        e_grp = [keep.tile([P, F, 4], BF16, name=f"e_grp{g}", align_bytes=64) for g in range(TG)]
+        e_codes = [keep.tile([P, F], U32, name=f"e_codes{g}", align_bytes=64) for g in range(TG)]
+        e_scales = [keep.tile([P, F], U8, name=f"e_scales{g}", align_bytes=64) for g in range(TG)]
+        mask = keep.tile([P, 8, F], BF16)
+
+        def bank(n):
+            return psum.tile([P, 512], F32, name=f"bank{n}", tag=f"bank{n}")
+
+        tbanks = {}
+        mbanks = {}
+        d_grp = {}
+        d_perm = {}
+
+        def R_(i):
+            perm = keep.tile([P, O // 2], F32, name=f"d_perm{i}")
+            nc.vector.tensor_copy(
+                out=perm[:].rearrange("p (g u w) -> p g u w", g=KG, u=2),
+                in_=d_sb[i][:].bitcast(F32).rearrange("p (g w u) -> p g u w", g=KG, u=2),
+            )
+            d_perm[i] = perm
+
+        def T_(i, b):
+            words = d_sb[i][:].bitcast(F32)
+            if True:
+                ps = bank((i % 2) * 2 + b)
+                tbanks[(i, b)] = ps
+                for s in range(2):
+                    for u in range(2):
+                        k0 = 256 * (2 * b + s)
+                        q = 2 * s + u
+                        if i in d_perm:
+                            src = d_perm[i][:, k0 + u * P : k0 + (u + 1) * P]
+                        else:
+                            src = words[:, k0 + u : k0 + 256 : 2]
+                        nc.tensor.transpose(ps[:, q * P : (q + 1) * P], src, ident[:])
+
+        def C_(i, b):
+            if b == 0:
+                grp = stage.tile([P, KG, P, 4], BF16, name="d_grp", align_bytes=64)
+                d_grp[i] = grp
+            grp = d_grp[i]
+            gw = grp[:].rearrange("p g r t -> p (g r t)").bitcast(F32)
+            gw = gw.rearrange("p (g r u) -> p g r u", g=KG, u=2)
+            if True:
+                nc.scalar.copy(
+                    out=gw[:, 2 * b : 2 * b + 2, :, :],
+                    in_=tbanks[(i, b)][:].rearrange("p (s u r) -> p s r u", s=2, u=2),
+                )
+
+        def Q_(i):
+            nc.vector.quantize_mx(
+                out=d_codes[i][:].bitcast(E4M3),
+                scales=d_scales[i][:],
+                in_=d_grp[i][:].rearrange("p g r t -> p (g r t)"),
+            )
+
+        def mx1(i, fc, ps):
+            t = i % 4
+            for g in range(KG):
+                nc.tensor.matmul_mx(
+                    out=ps[:, t * P : (t + 1) * P],
+                    lhsT=d_codes[i][:, g * P : (g + 1) * P].bitcast(E4M3),
+                    lhsT_scale=d_scales[i][:, g * P : (g + 1) * P],
+                    rhs=vw[fc // 4][:, g, 256 * (fc % 4) : 256 * (fc % 4) + 256].bitcast(E2M1),
+                    rhs_scale=vs[:, g, P * fc : P * fc + P],
+                    start=(g == 0),
+                    stop=(g == KG - 1),
+                )
+
+        def M_(i, fc):
+            if i == 0:
+                mbanks[(0, fc)] = bank(4 + fc)
+            mx1(i, fc, mbanks[(0, fc)])
+
+        def B_(G, fc):
+            mbanks[(G, fc)] = bank(4 + fc % 4)
+            for t in range(4):
+                mx1(4 * G + t, fc, mbanks[(G, fc)])
+
+        def G_(G, fc):
+            nc.vector.tensor_tensor(
+                out=e_grp[G][:, fc * P : (fc + 1) * P, :],
+                in0=mbanks[(G, fc)][:].rearrange("p (t n) -> p n t", t=4),
+                in1=gain_bc[:, fc * P : (fc + 1) * P].unsqueeze(2).to_broadcast([P, P, 4]),
+                op=OP.mult,
+            )
+
+        def QE_(G, f0, n):
+            nc.vector.quantize_mx(
+                out=e_codes[G][:, f0 : f0 + n].bitcast(E5M2),
+                scales=e_scales[G][:, f0 : f0 + n],
+                in_=e_grp[G][:, f0 : f0 + n, :].rearrange("p n t -> p (n t)"),
+            )
+
+        def CL_(G, j):
+            nc.vector.tensor_scalar(
+                out=x_sb[G][:, j, :],
+                in0=x_sb[G][:, j, :],
+                scalar1=lo_sb[:, G, j : j + 1],
+                scalar2=hi_sb[:, G, j : j + 1],
+                op0=OP.max,
+                op1=OP.min,
+            )
+
+        def I_(G, c0, n, eng):
+            o = x_grp[G][:, c0 : c0 + n, :]
+            i = x_sb[G][:, :, c0 : c0 + n].rearrange("p j c -> p c j")
+            if eng == "s":
+                nc.scalar.copy(
+                    out=o.rearrange("p (c i) j -> p c j i", i=4),
+                    in_=x_sb[G][:, :, c0 : c0 + n].rearrange("p j (c i) -> p c j i", i=4),
+                )
+            else:
+                nc.vector.tensor_copy(out=o, in_=i)
+
+        def QX_(G, c0, n):
+            nc.vector.quantize_mx(
+                out=x_codes[G][:, c0 : c0 + n].bitcast(E4M3),
+                scales=x_scales[G][:, c0 : c0 + n],
+                in_=x_grp[G][:, c0 : c0 + n, :].rearrange("p c j -> p (c j)"),
+            )
+
+        def A_(a):
+            s = w_sb[:, 2 * a : 2 * a + 2, :]
+            if a == 1:
+                bits = s.rearrange("p c f -> p (c f)").bitcast(I32)
+                nc.vector.tensor_scalar(
+                    out=bits, in0=bits, scalar1=0x7FFF7FFF, scalar2=None, op0=OP.bitwise_and
+                )
+            else:
+                nc.scalar.activation(out=s, in_=s, func=ACT.Abs)
+
+        def K_(a):
+            nc.vector.tensor_tensor(
+                out=mask[:, 2 * a : 2 * a + 2, :],
+                in0=w_sb[:, 2 * a : 2 * a + 2, :],
+                in1=r_bc[:].unsqueeze(1).to_broadcast([P, 2, F]),
+                op=OP.is_le,
+            )
+
+        obanks = {}
+        counter = {"n": 0}
+
+        def S2_(ct, h):
+            ps = bank(counter["n"] % 8)
+            counter["n"] += 1
+            obanks[(ct, h)] = ps
+            for G in range(TG):
+                nc.tensor.matmul_mx(
+                    out=ps[:],
+                    lhsT=x_codes[G][:, ct * P : (ct + 1) * P].bitcast(E4M3),
+                    lhsT_scale=x_scales[G][:, ct * P : (ct + 1) * P],
+                    rhs=e_codes[G][:, h * 512 : (h + 1) * 512].bitcast(E5M2),
+                    rhs_scale=e_scales[G][:, h * 512 : (h + 1) * 512],
+                    start=(G == 0),
+                    stop=(G == TG - 1),
+                )
+
+        def O_(ct, h, eng="v", pieces=1):
+            res = outs.tile([P, 512], F32, name="res")
+            n = 512 // pieces
+            for k in range(pieces):
+                sl = slice(k * n, (k + 1) * n)
+                m = mask[:, ct, h * 512 + k * n : h * 512 + (k + 1) * n]
+                if eng == "v":
+                    nc.vector.tensor_tensor(out=res[:, sl], in0=obanks[(ct, h)][:, sl], in1=m, op=OP.mult)
+                else:
+                    nc.scalar.copy(out=res[:, sl], in_=obanks[(ct, h)][:, sl])
+                    nc.gpsimd.tensor_tensor(out=res[:, sl], in0=res[:, sl], in1=m, op=OP.mult)
+            return res
+
+        def D_(ct, h, res, pieces=1):
+            n = 512 // pieces
+            for k in range(pieces):
+                nc.sync.dma_start(
+                    out=out[ct * P : (ct + 1) * P, h * 512 + k * n : h * 512 + (k + 1) * n],
+                    in_=res[:, k * n : (k + 1) * n],
+                )
+
+        res = {}
+
+        def P_(ct, h):
+            res[(ct, h)] = O_(ct, h, "s")
+
+        def E_(G, k):
+            if G == 0 or k == 0:
+                QE_(G, 512 * k, 512)
+            else:
+                QE_(1, 256 + 256 * k, 256)
+
+        steps = """T00 C00 T01 C01 Q0 T10 C10 T11 C11 Q1 T20 C20 T21 C21 Q2 R4 T30 C30 T31 C31 Q3 L00 L01 R5 M00
+        M01 M02 M03 T40 C40 T41 C41 Q4 L02 L03 M10 I01 M20 M30 G00 M11 M21 M31 G01 I00 M12 M22 M32
+        G02 M13 M23 M33 G03 X00 T50 C50 T51 C51 Q5 E00 T60 C60 T61 C61 I02 B04 G04 Q6 L10 L11 L12 L13
+        T70 C70 T71 C71 I03 A0 I10 I11 I12 I13 A2 A3 B05 G05 Q7 X01 B06 G06 A1 B07 G07 K0 K1 B10 G10
+        E01 B11 G11 X10 B12 G12 B13 G13 B14 G14 E10 B15 G15 X11 E11 K2 B16 G16 S00 O00 D00 S10 P10
+        O10 B17 G17 S20 O20 E12 D20 S30 P30 O30 S40 O40 D40 D10 S50 O50 D50 S01 O01 D01 S11 O11 K3
+        D11 D30 S21 P21 O21 S31 O31 D31 S41 O41 D41 D21 S51 O51 D51 S60 O60 D60 S70 O70 D70 S61 P61
+        O61 D61 S71 O71 D71"""
+        last = "71"
+        on_v = set("I00".split())
+        for word in steps.split():
+            kind, a = word[0], int(word[1])
+            b = int(word[2]) if len(word) > 2 else 0
+            if kind == "T":
+                T_(a, b)
+            elif kind == "C":
+                C_(a, b)
+            elif kind == "R":
+                R_(a)
+            elif kind == "Q":
+                Q_(a)
+            elif kind == "M":
+                M_(a, b)
+            elif kind == "B":
+                B_(a, b)
+            elif kind == "G":
+                G_(a, b)
+            elif kind == "E":
+                E_(a, b)
+            elif kind == "L":
+                CL_(a, b)
+            elif kind == "I":
+                I_(a, 256 * b, 256, "v" if word in on_v else "s")
+            elif kind == "X":
+                QX_(a, 512 * b, 512)
+            elif kind == "A":
+                A_(a)
+            elif kind == "K":
+                K_(a)
+            elif kind == "S":
+                S2_(a, b)
+            elif kind == "P":
+                P_(a, b)
+            elif kind == "O":
+                if (a, b) not in res:
+                    res[(a, b)] = O_(a, b, "v", 2 if word[1:] == last else 1)
+            else:
+                D_(a, b, res[(a, b)], 2 if word[1:] == last else 1)

@@ -20,6 +20,10 @@ ACT = mybir.ActivationFunctionType
 P = 128
 KG = O // 512
 TG = T // 512
+TILES = T // P
+CT = C // P
+HALF = 512
+BANKS = 8
 
 
 def tile_straight_through_weight_gradient_s9_kernel(
@@ -29,18 +33,17 @@ def tile_straight_through_weight_gradient_s9_kernel(
     with ExitStack() as ctx:
         keep = ctx.enter_context(tc.tile_pool(name="keep", bufs=1))
         stage = ctx.enter_context(tc.tile_pool(name="stage", bufs=3))
-        outs = ctx.enter_context(tc.tile_pool(name="outs", bufs=16))
+        outs = ctx.enter_context(tc.tile_pool(name="outs", bufs=10))
         psum = ctx.enter_context(tc.psum_pool(name="psum", bufs=1))
         ctx.enter_context(tc.manual_schedule())
 
-        vs = keep.tile([P, KG, F], U8, align_bytes=64)
-        nc.vector.memset(vs[:].rearrange("p g n -> p (g n)").bitcast(I32), 0)
-        warm = keep.tile([P, 1], F32)
-        nc.vector.memset(warm[:], 0.0)
-        warm2 = keep.tile([P, 1], F32)
-        nc.scalar.activation(out=warm2[:], in_=warm[:], func=ACT.Abs)
+        vs = [keep.tile([P, KG, HALF], U8, name=f"vs{h}", align_bytes=64) for h in range(2)]
+        for h in range(2):
+            nc.vector.memset(vs[h][:].rearrange("p g n -> p (g n)").bitcast(I32), 0)
         ident = keep.tile([P, P], F32)
         make_identity(nc, ident[:])
+        gain_col = keep.tile([P, F // P], BF16)
+        r_col = keep.tile([P, 4, 2], BF16)
         lo_sb = keep.tile([P, TG, 4], BF16)
         hi_sb = keep.tile([P, TG, 4], BF16)
 
@@ -50,296 +53,335 @@ def tile_straight_through_weight_gradient_s9_kernel(
         vw_v = v_words.rearrange("g p b -> p g b")
         vs_v = v_scales.rearrange("g q n -> q g n").bitcast(I32)
 
-        d_sb = [keep.tile([P, O], BF16, name=f"d_sb{i}") for i in range(8)]
+        d_first = [keep.tile([P, O // 2], BF16, name=f"d_first{b}") for b in range(2)]
+        d_sb = [None] + [keep.tile([P, O], BF16, name=f"d_sb{i}") for i in range(1, TILES)]
         vw = [keep.tile([P, KG, F], U8, name=f"vw{h}", align_bytes=64) for h in range(2)]
         gain_bc = keep.tile([P, F], BF16)
-        r_bc = keep.tile([P, F], BF16)
         x_sb = [keep.tile([P, 4, C], BF16, name=f"x_sb{g}") for g in range(TG)]
-        w_sb = keep.tile([P, 8, F], BF16)
+        w_sb = [keep.tile([P, 2, F], BF16, name=f"w_sb{a}") for a in range(CT // 2)]
 
-        def load_d(i, pieces=1):
-            n = O // pieces
-            for k in range(pieces):
-                nc.sync.dma_start(
-                    out=d_sb[i][:, k * n : (k + 1) * n],
-                    in_=delta_v[i // 4, i % 4, :, k * n : (k + 1) * n],
-                )
+        def load_delta(i):
+            rows = delta_v[i // 4, i % 4]
+            if i == 0:
+                for b in range(2):
+                    nc.sync.dma_start(out=d_first[b][:], in_=rows[:, b * O // 2 : (b + 1) * O // 2])
+            else:
+                nc.sync.dma_start(out=d_sb[i][:], in_=rows)
 
-        def load_vs():
+        def load_v(h):
             for q in range(4):
                 nc.sync.dma_start(
-                    out=vs[32 * q : 32 * q + 4, :, :].bitcast(I32), in_=vs_v[4 * q : 4 * q + 4, :, :]
+                    out=vs[h][32 * q : 32 * q + 4, :, :].bitcast(I32),
+                    in_=vs_v[4 * q : 4 * q + 4, :, h * P : (h + 1) * P],
                 )
-
-        def load_vw(h):
             nc.sync.dma_start(out=vw[h][:], in_=vw_v[:, :, h * F : (h + 1) * F])
 
         def load_x(g, a):
-            if True:
-                nc.sync.dma_start(out=x_sb[g][:, 2 * a : 2 * a + 2, :], in_=x_v[g, :, 2 * a : 2 * a + 2, :])
+            nc.sync.dma_start(out=x_sb[g][:, 2 * a : 2 * a + 2, :], in_=x_v[g, :, 2 * a : 2 * a + 2, :])
 
         def load_w(a):
-            nc.sync.dma_start(out=w_sb[:, 2 * a : 2 * a + 2, :], in_=w_v[:, 2 * a : 2 * a + 2, :])
+            nc.sync.dma_start(out=w_sb[a][:], in_=w_v[:, 2 * a : 2 * a + 2, :])
 
+        nc.scalar.dma_start(out=gain_col[:], in_=gain.rearrange("(p c) -> p c", p=P))
+        nc.scalar.dma_start(out=r_col[:], in_=r.rearrange("(c p e) -> p c e", p=P, e=2))
         nc.gpsimd.dma_start(out=lo_sb[:], in_=lo.rearrange("(g p j) -> p g j", p=P, j=4))
         nc.gpsimd.dma_start(out=hi_sb[:], in_=hi.rearrange("(g p j) -> p g j", p=P, j=4))
-        loads = "d0 d1 d2 vs d3 vh0 d4 x0a d5 x0b gain d6 vh1 d7 x1a x1b w0 r w1 w2 w3"
-        for word in loads.split():
-            if word == "vs":
-                load_vs()
-            elif word == "gain":
-                nc.sync.dma_start(out=gain_bc[:], in_=gain.partition_broadcast(P))
-            elif word == "r":
-                nc.sync.dma_start(out=r_bc[:], in_=r.partition_broadcast(P))
-            elif word[0] == "v":
-                load_vw(int(word[2]))
-            elif word[0] == "x":
-                load_x(int(word[1]), {"a": 0, "b": 1}[word[2]])
-            elif word[0] == "w":
-                load_w(int(word[1]))
-            else:
-                load_d(int(word[1]), 2 if word == "d0" else 1)
+        load_delta(0)
+        load_delta(1)
+        load_delta(2)
+        load_v(0)
+        load_delta(3)
+        load_delta(4)
+        load_x(0, 0)
+        load_x(0, 1)
+        load_delta(5)
+        load_delta(6)
+        load_v(1)
+        load_delta(7)
+        load_x(1, 0)
+        load_x(1, 1)
+        load_w(0)
+        load_w(1)
+        load_w(2)
+        load_w(3)
 
-        d_codes = [keep.tile([P, 512], U32, name=f"d_codes{i}", align_bytes=64) for i in range(8)]
-        d_scales = [keep.tile([P, 512], U8, name=f"d_scales{i}", align_bytes=64) for i in range(8)]
+        d_codes = [keep.tile([P, 512], U32, name=f"d_codes{i}", align_bytes=64) for i in range(TILES)]
+        d_scales = [keep.tile([P, 512], U8, name=f"d_scales{i}", align_bytes=64) for i in range(TILES)]
         x_grp = [keep.tile([P, C, 4], BF16, name=f"x_grp{g}", align_bytes=64) for g in range(TG)]
         x_codes = [keep.tile([P, C], U32, name=f"x_codes{g}", align_bytes=64) for g in range(TG)]
         x_scales = [keep.tile([P, C], U8, name=f"x_scales{g}", align_bytes=64) for g in range(TG)]
         e_grp = [keep.tile([P, F, 4], BF16, name=f"e_grp{g}", align_bytes=64) for g in range(TG)]
         e_codes = [keep.tile([P, F], U32, name=f"e_codes{g}", align_bytes=64) for g in range(TG)]
         e_scales = [keep.tile([P, F], U8, name=f"e_scales{g}", align_bytes=64) for g in range(TG)]
-        mask = keep.tile([P, 8, F], BF16)
+        mask = keep.tile([P, CT, F], BF16)
 
         def bank(n):
             return psum.tile([P, 512], F32, name=f"bank{n}", tag=f"bank{n}")
 
-        tbanks = {}
-        mbanks = {}
+        d_sorted = {}
         d_grp = {}
-        d_perm = {}
+        e_bank = {}
+        o_bank = {}
 
-        def R_(i):
-            perm = keep.tile([P, O // 2], F32, name=f"d_perm{i}")
+        def sort_words(i):
+            d_sorted[i] = stage.tile([P, O // 2], F32, name="d_sorted", bufs=4)
             nc.vector.tensor_copy(
-                out=perm[:].rearrange("p (g u w) -> p g u w", g=KG, u=2),
-                in_=d_sb[i][:].bitcast(F32).rearrange("p (g w u) -> p g u w", g=KG, u=2),
+                out=d_sorted[i][:].rearrange("p (g u m) -> p g u m", g=KG, u=2),
+                in_=d_sb[i][:].bitcast(F32).rearrange("p (g m u) -> p g u m", g=KG, u=2),
             )
-            d_perm[i] = perm
 
-        def T_(i, b):
-            words = d_sb[i][:].bitcast(F32)
-            if True:
-                ps = bank((i % 2) * 2 + b)
-                tbanks[(i, b)] = ps
-                for s in range(2):
-                    for u in range(2):
-                        k0 = 256 * (2 * b + s)
-                        q = 2 * s + u
-                        if i in d_perm:
-                            src = d_perm[i][:, k0 + u * P : k0 + (u + 1) * P]
-                        else:
-                            src = words[:, k0 + u : k0 + 256 : 2]
-                        nc.tensor.transpose(ps[:, q * P : (q + 1) * P], src, ident[:])
+        t_bank = {}
 
-        def C_(i, b):
+        def turn_half(i, b, n):
+            t_bank[(i, b)] = ps = bank(n)
+            for q in range(4):
+                g, u = q // 2, q % 2
+                if i == 0:
+                    src = d_first[b][:].bitcast(F32)[:, 256 * g + u : 256 * (g + 1) : 2]
+                elif i not in d_sorted:
+                    src = d_sb[i][:].bitcast(F32)[:, 256 * (2 * b + g) + u : 256 * (2 * b + g + 1) : 2]
+                else:
+                    src = d_sorted[i][:, (4 * b + q) * P : (4 * b + q + 1) * P]
+                nc.tensor.transpose(ps[:, q * P : (q + 1) * P], src, ident[:])
+
+        def turn(i, n):
+            for b in range(2):
+                turn_half(i, b, n + b)
+                pair_words(i, b)
+
+        def pair_words(i, b):
             if b == 0:
-                grp = stage.tile([P, KG, P, 4], BF16, name="d_grp", align_bytes=64)
-                d_grp[i] = grp
-            grp = d_grp[i]
-            gw = grp[:].rearrange("p g r t -> p (g r t)").bitcast(F32)
-            gw = gw.rearrange("p (g r u) -> p g r u", g=KG, u=2)
-            if True:
-                nc.scalar.copy(
-                    out=gw[:, 2 * b : 2 * b + 2, :, :],
-                    in_=tbanks[(i, b)][:].rearrange("p (s u r) -> p s r u", s=2, u=2),
-                )
+                d_grp[i] = stage.tile([P, KG, P, 4], BF16, name="d_grp", align_bytes=64)
+            words = d_grp[i][:].rearrange("p g m t -> p (g m t)").bitcast(F32)
+            words = words.rearrange("p (g m u) -> p g m u", g=KG, u=2)
+            nc.scalar.copy(
+                out=words[:, 2 * b : 2 * b + 2, :, :],
+                in_=t_bank[(i, b)][:].rearrange("p (g u m) -> p g m u", g=2, u=2),
+            )
 
-        def Q_(i):
+        s_bank = {}
+
+        def spread_turn(which, n):
+            s_bank[which] = ps = bank(n)
+            words = {"g": gain_col[:], "r": r_col[:].rearrange("p c e -> p (c e)")}[which].bitcast(F32)
+            for c in range(4):
+                nc.tensor.transpose(ps[:, c * P : (c + 1) * P], words[:, c : c + 1].to_broadcast([P, P]), ident[:])
+
+        def spread_copy(which):
+            nc.scalar.copy(
+                out=gain_bc[:].bitcast(F32).rearrange("p (m c) -> p m c", c=4),
+                in_=s_bank[which][:].rearrange("p (c m) -> p m c", c=4),
+            )
+
+        def quantise_delta(i):
             nc.vector.quantize_mx(
                 out=d_codes[i][:].bitcast(E4M3),
                 scales=d_scales[i][:],
-                in_=d_grp[i][:].rearrange("p g r t -> p (g r t)"),
+                in_=d_grp[i][:].rearrange("p g m t -> p (g m t)"),
             )
 
-        def mx1(i, fc, ps):
-            t = i % 4
+        def first_product(i, fc):
+            t, h, n0 = i % 4, fc // 4, P * (fc % 4)
             for g in range(KG):
                 nc.tensor.matmul_mx(
-                    out=ps[:, t * P : (t + 1) * P],
+                    out=e_bank[(i // 4, fc)][:, t * P : (t + 1) * P],
                     lhsT=d_codes[i][:, g * P : (g + 1) * P].bitcast(E4M3),
                     lhsT_scale=d_scales[i][:, g * P : (g + 1) * P],
-                    rhs=vw[fc // 4][:, g, 256 * (fc % 4) : 256 * (fc % 4) + 256].bitcast(E2M1),
-                    rhs_scale=vs[:, g, P * fc : P * fc + P],
+                    rhs=vw[h][:, g, 2 * n0 : 2 * n0 + 2 * P].bitcast(E2M1),
+                    rhs_scale=vs[h][:, g, n0 : n0 + P],
                     start=(g == 0),
                     stop=(g == KG - 1),
                 )
 
-        def M_(i, fc):
-            if i == 0:
-                mbanks[(0, fc)] = bank(4 + fc)
-            mx1(i, fc, mbanks[(0, fc)])
-
-        def B_(G, fc):
-            mbanks[(G, fc)] = bank(4 + fc % 4)
-            for t in range(4):
-                mx1(4 * G + t, fc, mbanks[(G, fc)])
-
-        def G_(G, fc):
+        def apply_gain(g, fc):
             nc.vector.tensor_tensor(
-                out=e_grp[G][:, fc * P : (fc + 1) * P, :],
-                in0=mbanks[(G, fc)][:].rearrange("p (t n) -> p n t", t=4),
+                out=e_grp[g][:, fc * P : (fc + 1) * P, :],
+                in0=e_bank[(g, fc)][:].rearrange("p (t n) -> p n t", t=4),
                 in1=gain_bc[:, fc * P : (fc + 1) * P].unsqueeze(2).to_broadcast([P, P, 4]),
                 op=OP.mult,
             )
 
-        def QE_(G, f0, n):
+        def quantise_e(g, f0, n):
             nc.vector.quantize_mx(
-                out=e_codes[G][:, f0 : f0 + n].bitcast(E5M2),
-                scales=e_scales[G][:, f0 : f0 + n],
-                in_=e_grp[G][:, f0 : f0 + n, :].rearrange("p n t -> p (n t)"),
+                out=e_codes[g][:, f0 : f0 + n].bitcast(E5M2),
+                scales=e_scales[g][:, f0 : f0 + n],
+                in_=e_grp[g][:, f0 : f0 + n, :].rearrange("p n t -> p (n t)"),
             )
 
-        def CL_(G, j):
-            nc.vector.tensor_scalar(
-                out=x_sb[G][:, j, :],
-                in0=x_sb[G][:, j, :],
-                scalar1=lo_sb[:, G, j : j + 1],
-                scalar2=hi_sb[:, G, j : j + 1],
-                op0=OP.max,
-                op1=OP.min,
-            )
-
-        def I_(G, c0, n, eng):
-            o = x_grp[G][:, c0 : c0 + n, :]
-            i = x_sb[G][:, :, c0 : c0 + n].rearrange("p j c -> p c j")
-            if eng == "s":
-                nc.scalar.copy(
-                    out=o.rearrange("p (c i) j -> p c j i", i=4),
-                    in_=x_sb[G][:, :, c0 : c0 + n].rearrange("p j (c i) -> p c j i", i=4),
-                )
-            else:
-                nc.vector.tensor_copy(out=o, in_=i)
-
-        def QX_(G, c0, n):
-            nc.vector.quantize_mx(
-                out=x_codes[G][:, c0 : c0 + n].bitcast(E4M3),
-                scales=x_scales[G][:, c0 : c0 + n],
-                in_=x_grp[G][:, c0 : c0 + n, :].rearrange("p c j -> p (c j)"),
-            )
-
-        def A_(a):
-            s = w_sb[:, 2 * a : 2 * a + 2, :]
-            if a == 1:
-                bits = s.rearrange("p c f -> p (c f)").bitcast(I32)
+        def clip(g, a):
+            for j in (2 * a, 2 * a + 1):
                 nc.vector.tensor_scalar(
-                    out=bits, in0=bits, scalar1=0x7FFF7FFF, scalar2=None, op0=OP.bitwise_and
+                    out=x_sb[g][:, j, :],
+                    in0=x_sb[g][:, j, :],
+                    scalar1=lo_sb[:, g, j : j + 1],
+                    scalar2=hi_sb[:, g, j : j + 1],
+                    op0=OP.max,
+                    op1=OP.min,
                 )
-            else:
-                nc.scalar.activation(out=s, in_=s, func=ACT.Abs)
 
-        def K_(a):
+        def interleave(piece):
+            g, c0 = piece // 4, 256 * (piece % 4)
+            nc.scalar.copy(
+                out=x_grp[g][:, c0 : c0 + 256, :].rearrange("p (c i) j -> p c j i", i=4),
+                in_=x_sb[g][:, :, c0 : c0 + 256].rearrange("p j (c i) -> p c j i", i=4),
+            )
+
+        def quantise_x(g, k):
+            cols = slice(512 * k, 512 * (k + 1))
+            nc.vector.quantize_mx(
+                out=x_codes[g][:, cols].bitcast(E4M3),
+                scales=x_scales[g][:, cols],
+                in_=x_grp[g][:, cols, :].rearrange("p c j -> p (c j)"),
+            )
+
+        def abs_w(a, h):
+            part = w_sb[a][:, :, h * HALF : (h + 1) * HALF]
+            nc.scalar.activation(out=part, in_=part, func=ACT.Abs)
+
+        def abs_w_bits(a):
+            bits = w_sb[a][:].rearrange("p c f -> p (c f)").bitcast(I32)
+            nc.vector.tensor_scalar(out=bits, in0=bits, scalar1=0x7FFF7FFF, scalar2=None, op0=OP.bitwise_and)
+
+        def compare(a, h):
+            cols = slice(h * HALF, (h + 1) * HALF)
             nc.vector.tensor_tensor(
-                out=mask[:, 2 * a : 2 * a + 2, :],
-                in0=w_sb[:, 2 * a : 2 * a + 2, :],
-                in1=r_bc[:].unsqueeze(1).to_broadcast([P, 2, F]),
+                out=mask[:, 2 * a : 2 * a + 2, cols],
+                in0=w_sb[a][:, :, cols],
+                in1=s_bank["r"][:].bitcast(BF16)[:, cols].unsqueeze(1).to_broadcast([P, 2, HALF]),
                 op=OP.is_le,
             )
 
-        obanks = {}
-        counter = {"n": 0}
-
-        def S2_(ct, h):
-            ps = bank(counter["n"] % 8)
-            counter["n"] += 1
-            obanks[(ct, h)] = ps
-            for G in range(TG):
+        def second_product(unit, n):
+            h, ct = unit // CT, unit % CT
+            o_bank[unit] = bank(n)
+            for g in range(TG):
                 nc.tensor.matmul_mx(
-                    out=ps[:],
-                    lhsT=x_codes[G][:, ct * P : (ct + 1) * P].bitcast(E4M3),
-                    lhsT_scale=x_scales[G][:, ct * P : (ct + 1) * P],
-                    rhs=e_codes[G][:, h * 512 : (h + 1) * 512].bitcast(E5M2),
-                    rhs_scale=e_scales[G][:, h * 512 : (h + 1) * 512],
-                    start=(G == 0),
-                    stop=(G == TG - 1),
+                    out=o_bank[unit][:],
+                    lhsT=x_codes[g][:, ct * P : (ct + 1) * P].bitcast(E4M3),
+                    lhsT_scale=x_scales[g][:, ct * P : (ct + 1) * P],
+                    rhs=e_codes[g][:, h * HALF : (h + 1) * HALF].bitcast(E5M2),
+                    rhs_scale=e_scales[g][:, h * HALF : (h + 1) * HALF],
+                    start=(g == 0),
+                    stop=(g == TG - 1),
                 )
 
-        def O_(ct, h, eng="v", pieces=1):
-            res = outs.tile([P, 512], F32, name="res")
-            n = 512 // pieces
-            for k in range(pieces):
-                sl = slice(k * n, (k + 1) * n)
-                m = mask[:, ct, h * 512 + k * n : h * 512 + (k + 1) * n]
-                if eng == "v":
-                    nc.vector.tensor_tensor(out=res[:, sl], in0=obanks[(ct, h)][:, sl], in1=m, op=OP.mult)
-                else:
-                    nc.scalar.copy(out=res[:, sl], in_=obanks[(ct, h)][:, sl])
-                    nc.gpsimd.tensor_tensor(out=res[:, sl], in0=res[:, sl], in1=m, op=OP.mult)
-            return res
+        def finish(unit):
+            h, ct = unit // CT, unit % CT
+            res[unit] = outs.tile([P, HALF], F32, name="res")
+            nc.vector.tensor_tensor(out=res[unit][:], in0=o_bank[unit][:], in1=mask[:, ct, h * HALF : (h + 1) * HALF], op=OP.mult)
 
-        def D_(ct, h, res, pieces=1):
-            n = 512 // pieces
-            for k in range(pieces):
-                nc.sync.dma_start(
-                    out=out[ct * P : (ct + 1) * P, h * 512 + k * n : h * 512 + (k + 1) * n],
-                    in_=res[:, k * n : (k + 1) * n],
-                )
+        def copy_out(unit):
+            res[unit] = outs.tile([P, HALF], F32, name="res")
+            nc.scalar.copy(out=res[unit][:], in_=o_bank[unit][:])
+
+        def pool_mask(unit):
+            h, ct = unit // CT, unit % CT
+            nc.gpsimd.tensor_tensor(out=res[unit][:], in0=res[unit][:], in1=mask[:, ct, h * HALF : (h + 1) * HALF], op=OP.mult)
+
+        def store(unit):
+            h, ct = unit // CT, unit % CT
+            nc.sync.dma_start(out=out[ct * P : (ct + 1) * P, h * HALF : (h + 1) * HALF], in_=res[unit][:])
 
         res = {}
 
-        def P_(ct, h):
-            res[(ct, h)] = O_(ct, h, "s")
+        for i in range(3):
+            turn(i, 2 * i + (i > 0))
+            if i == 0:
+                spread_turn("g", 2)
+            quantise_delta(i)
+        spread_copy("g")
+        for fc in range(4):
+            e_bank[(0, fc)] = bank(4 + fc)
+        sort_words(3)
+        sort_words(4)
+        clip(0, 0)
+        clip(0, 1)
+        for pair in range(2):
+            for i in (2 * pair, 2 * pair + 1):
+                for fc in range(4):
+                    first_product(i, fc)
+            turn(2 * pair + 3, 0)
+            turn(2 * pair + 4, 2)
+            if pair == 0:
+                quantise_delta(3)
+                sort_words(5)
+                quantise_delta(4)
+                sort_words(6)
+                interleave(0)
+                interleave(1)
+        for fc in range(4):
+            apply_gain(0, fc)
+        quantise_delta(5)
+        quantise_e(0, 0, HALF)
+        interleave(2)
 
-        def E_(G, k):
-            if G == 0 or k == 0:
-                QE_(G, 512 * k, 512)
-            else:
-                QE_(1, 256 + 256 * k, 256)
+        def chunk(g, fc, n):
+            e_bank[(g, fc)] = bank(n)
+            for t in range(4):
+                first_product(4 * g + t, fc)
+            apply_gain(g, fc)
 
-        steps = """T00 C00 T01 C01 Q0 T10 C10 T11 C11 Q1 T20 C20 T21 C21 Q2 R4 T30 C30 T31 C31 Q3 L00 L01 R5 M00
-        M01 M02 M03 T40 C40 T41 C41 Q4 L02 L03 M10 I01 M20 M30 G00 M11 M21 M31 G01 I00 M12 M22 M32
-        G02 M13 M23 M33 G03 X00 T50 C50 T51 C51 Q5 E00 T60 C60 T61 C61 I02 B04 G04 Q6 L10 L11 L12 L13
-        T70 C70 T71 C71 I03 A0 I10 I11 I12 I13 A2 A3 B05 G05 Q7 X01 B06 G06 A1 B07 G07 K0 K1 B10 G10
-        E01 B11 G11 X10 B12 G12 B13 G13 B14 G14 E10 B15 G15 X11 E11 K2 B16 G16 S00 O00 D00 S10 P10
-        O10 B17 G17 S20 O20 E12 D20 S30 P30 O30 S40 O40 D40 D10 S50 O50 D50 S01 O01 D01 S11 O11 K3
-        D11 D30 S21 P21 O21 S31 O31 D31 S41 O41 D41 D21 S51 O51 D51 S60 O60 D60 S70 O70 D70 S61 P61
-        O61 D61 S71 O71 D71"""
-        last = "71"
-        on_v = set("I00".split())
-        for word in steps.split():
-            kind, a = word[0], int(word[1])
-            b = int(word[2]) if len(word) > 2 else 0
-            if kind == "T":
-                T_(a, b)
-            elif kind == "C":
-                C_(a, b)
-            elif kind == "R":
-                R_(a)
-            elif kind == "Q":
-                Q_(a)
-            elif kind == "M":
-                M_(a, b)
-            elif kind == "B":
-                B_(a, b)
-            elif kind == "G":
-                G_(a, b)
-            elif kind == "E":
-                E_(a, b)
-            elif kind == "L":
-                CL_(a, b)
-            elif kind == "I":
-                I_(a, 256 * b, 256, "v" if word in on_v else "s")
-            elif kind == "X":
-                QX_(a, 512 * b, 512)
-            elif kind == "A":
-                A_(a)
-            elif kind == "K":
-                K_(a)
-            elif kind == "S":
-                S2_(a, b)
-            elif kind == "P":
-                P_(a, b)
-            elif kind == "O":
-                if (a, b) not in res:
-                    res[(a, b)] = O_(a, b, "v", 2 if word[1:] == last else 1)
+        chunk(0, 4, 4)
+        quantise_delta(6)
+        quantise_x(0, 0)
+        chunk(0, 5, 5)
+        turn(7, 0)
+        spread_turn("r", 7)
+        clip(1, 0)
+        clip(1, 1)
+        quantise_delta(7)
+        for piece in (3, 4, 5):
+            interleave(piece)
+        chunk(0, 6, 6)
+        quantise_x(0, 1)
+        chunk(0, 7, 2)
+        abs_w_bits(0)
+        chunk(1, 0, 3)
+        quantise_e(0, HALF, HALF)
+        compare(0, 0)
+        abs_w(1, 0)
+        abs_w(2, 0)
+        chunk(1, 1, 4)
+        quantise_x(1, 0)
+        compare(0, 1)
+        interleave(6)
+        interleave(7)
+        chunk(1, 2, 5)
+        compare(1, 0)
+        chunk(1, 3, 0)
+        compare(2, 0)
+        quantise_e(1, 0, HALF)
+        abs_w(3, 0)
+        abs_w(1, 1)
+        chunk(1, 4, 1)
+        quantise_x(1, 1)
+        chunk(1, 5, 6)
+        compare(3, 0)
+        quantise_e(1, HALF, 256)
+        chunk(1, 6, 2)
+        quantise_e(1, HALF + 256, P)
+        second_product(0, 3)
+        copy_out(0)
+        pool_mask(0)
+        store(0)
+        abs_w(2, 1)
+        abs_w(3, 1)
+        chunk(1, 7, 4)
+        banks = (5, 0, 1, 6, 2, 3, 4)
+        late = None
+        for unit in range(1, 2 * CT):
+            second_product(unit, banks[(unit - 1) % 7])
+            if unit % 3 == 0 and unit < 15:
+                copy_out(unit)
+                pool_mask(unit)
+                late = unit
             else:
-                D_(a, b, res[(a, b)], 2 if word[1:] == last else 1)
+                finish(unit)
+                store(unit)
+                if late is not None:
+                    store(late)
+                    late = None
+            if unit == 1:
+                quantise_e(1, HALF + 384, P)
+            if unit in (4, 7, 10):
+                compare((unit - 1) // 3, 1)

@@ -304,9 +304,7 @@ def tile_straight_through_weight_gradient_s9_kernel(
             turn(2 * pair + 4, 2)
             if pair == 0:
                 quantise_delta(3)
-                sort_words(5)
                 quantise_delta(4)
-                sort_words(6)
                 interleave(0)
                 interleave(1)
         for fc in range(4):

@@ -33,7 +33,7 @@ def tile_straight_through_weight_gradient_s9_kernel(
     with ExitStack() as ctx:
         keep = ctx.enter_context(tc.tile_pool(name="keep", bufs=1))
         stage = ctx.enter_context(tc.tile_pool(name="stage", bufs=3))
-        outs = ctx.enter_context(tc.tile_pool(name="outs", bufs=10))
+        outs = ctx.enter_context(tc.tile_pool(name="outs", bufs=8))
         psum = ctx.enter_context(tc.psum_pool(name="psum", bufs=1))
         ctx.enter_context(tc.manual_schedule())
 
@@ -43,7 +43,11 @@ def tile_straight_through_weight_gradient_s9_kernel(
         ident = keep.tile([P, P], F32)
         make_identity(nc, ident[:])
         gain_col = keep.tile([P, F // P], BF16)
-        r_col = keep.tile([P, 4, 2], BF16)
+        r_col = keep.tile([P, F // P], BF16)
+        gain_rows = keep.tile([F // P, P], BF16)
+        gain_pad = keep.tile([P, P], F32)
+        nc.vector.memset(gain_pad[:], 0.0)
+        gain_part = keep.tile([P, F // P], F32)
         lo_sb = keep.tile([P, TG, 4], BF16)
         hi_sb = keep.tile([P, TG, 4], BF16)
 
@@ -82,8 +86,8 @@ def tile_straight_through_weight_gradient_s9_kernel(
         def load_w(a):
             nc.sync.dma_start(out=w_sb[a][:], in_=w_v[:, 2 * a : 2 * a + 2, :])
 
+        nc.scalar.dma_start(out=gain_rows[:], in_=gain.rearrange("(c p) -> c p", p=P))
         nc.scalar.dma_start(out=gain_col[:], in_=gain.rearrange("(p c) -> p c", p=P))
-        nc.scalar.dma_start(out=r_col[:], in_=r.rearrange("(c p e) -> p c e", p=P, e=2))
         nc.gpsimd.dma_start(out=lo_sb[:], in_=lo.rearrange("(g p j) -> p g j", p=P, j=4))
         nc.gpsimd.dma_start(out=hi_sb[:], in_=hi.rearrange("(g p j) -> p g j", p=P, j=4))
         load_delta(0)
@@ -96,8 +100,9 @@ def tile_straight_through_weight_gradient_s9_kernel(
         load_x(0, 1)
         load_delta(5)
         load_delta(6)
-        load_v(1)
         load_delta(7)
+        load_v(1)
+        nc.sync.dma_start(out=r_col[:], in_=r.rearrange("(p c) -> p c", p=P))
         load_x(1, 0)
         load_x(1, 1)
         load_w(0)
@@ -105,8 +110,11 @@ def tile_straight_through_weight_gradient_s9_kernel(
         load_w(2)
         load_w(3)
 
-        d_codes = [keep.tile([P, 512], U32, name=f"d_codes{i}", align_bytes=64) for i in range(TILES)]
-        d_scales = [keep.tile([P, 512], U8, name=f"d_scales{i}", align_bytes=64) for i in range(TILES)]
+        d_codes = [keep.tile([P, 512], U32, name=f"d_codes{i}", align_bytes=64) for i in range(4)]
+        d_scales = [keep.tile([P, 512], U8, name=f"d_scales{i}", align_bytes=64) for i in range(4)]
+        late_grp = keep.tile([P, KG, 4, P, 4], BF16, align_bytes=64)
+        late_codes = keep.tile([P, KG, 512], U32, align_bytes=64)
+        late_scales = keep.tile([P, KG, 512], U8, align_bytes=64)
         x_grp = [keep.tile([P, C, 4], BF16, name=f"x_grp{g}", align_bytes=64) for g in range(TG)]
         x_codes = [keep.tile([P, C], U32, name=f"x_codes{g}", align_bytes=64) for g in range(TG)]
         x_scales = [keep.tile([P, C], U8, name=f"x_scales{g}", align_bytes=64) for g in range(TG)]
@@ -124,7 +132,7 @@ def tile_straight_through_weight_gradient_s9_kernel(
         o_bank = {}
 
         def sort_words(i):
-            d_sorted[i] = stage.tile([P, O // 2], F32, name="d_sorted", bufs=4)
+            d_sorted[i] = stage.tile([P, O // 2], F32, name="d_sorted", bufs=2)
             nc.vector.tensor_copy(
                 out=d_sorted[i][:].rearrange("p (g u m) -> p g u m", g=KG, u=2),
                 in_=d_sb[i][:].bitcast(F32).rearrange("p (g m u) -> p g u m", g=KG, u=2),
@@ -150,10 +158,14 @@ def tile_straight_through_weight_gradient_s9_kernel(
                 pair_words(i, b)
 
         def pair_words(i, b):
-            if b == 0:
-                d_grp[i] = stage.tile([P, KG, P, 4], BF16, name="d_grp", align_bytes=64)
-            words = d_grp[i][:].rearrange("p g m t -> p (g m t)").bitcast(F32)
-            words = words.rearrange("p (g m u) -> p g m u", g=KG, u=2)
+            if i >= 4:
+                words = late_grp[:, :, i - 4, :, :].rearrange("p g m t -> p g (m t)").bitcast(F32)
+                words = words.rearrange("p g (m u) -> p g m u", u=2)
+            else:
+                if b == 0:
+                    d_grp[i] = stage.tile([P, KG, P, 4], BF16, name="d_grp", align_bytes=64)
+                words = d_grp[i][:].rearrange("p g m t -> p (g m t)").bitcast(F32)
+                words = words.rearrange("p (g m u) -> p g m u", g=KG, u=2)
             nc.scalar.copy(
                 out=words[:, 2 * b : 2 * b + 2, :, :],
                 in_=t_bank[(i, b)][:].rearrange("p (g u m) -> p g m u", g=2, u=2),
@@ -163,14 +175,14 @@ def tile_straight_through_weight_gradient_s9_kernel(
 
         def spread_turn(which, n):
             s_bank[which] = ps = bank(n)
-            words = {"g": gain_col[:], "r": r_col[:].rearrange("p c e -> p (c e)")}[which].bitcast(F32)
+            words = {"g": gain_col, "r": r_col}[which][:].bitcast(F32)
             for c in range(4):
-                nc.tensor.transpose(ps[:, c * P : (c + 1) * P], words[:, c : c + 1].to_broadcast([P, P]), ident[:])
+                nc.tensor.transpose(ps[:, c::4], words[:, c : c + 1].to_broadcast([P, P]), ident[:])
 
         def spread_copy(which):
             nc.scalar.copy(
-                out=gain_bc[:].bitcast(F32).rearrange("p (m c) -> p m c", c=4),
-                in_=s_bank[which][:].rearrange("p (c m) -> p m c", c=4),
+                out=gain_bc[:].bitcast(F32),
+                in_=s_bank[which][:],
             )
 
         def quantise_delta(i):
@@ -180,13 +192,67 @@ def tile_straight_through_weight_gradient_s9_kernel(
                 in_=d_grp[i][:].rearrange("p g m t -> p (g m t)"),
             )
 
+        def quantise_late(g):
+            nc.vector.quantize_mx(
+                out=late_codes[:, g, :].bitcast(E4M3),
+                scales=late_scales[:, g, :],
+                in_=late_grp[:, g, :, :, :].rearrange("p t m j -> p (t m j)"),
+            )
+
+        e_rows = {}
+
+        def turned_product(fc, n):
+            h, n0 = fc // 4, P * (fc % 4)
+            ps = bank(n)
+            for g in range(KG):
+                nc.tensor.matmul_mx(
+                    out=ps[:],
+                    lhsT=vw[h][:, g, 2 * n0 : 2 * n0 + 2 * P].bitcast(E2M1),
+                    lhsT_scale=vs[h][:, g, n0 : n0 + P],
+                    rhs=late_codes[:, g, :].bitcast(E4M3),
+                    rhs_scale=late_scales[:, g, :],
+                    start=(g == 0),
+                    stop=(g == KG - 1),
+                )
+            e_rows[fc] = stage.tile([P, 2, P, 2], BF16, name="e_rows", bufs=6)
+            nc.scalar.activation(
+                out=e_rows[fc][:],
+                in_=ps[:].rearrange("p (u e m) -> p u m e", u=2, e=2),
+                func=ACT.Copy,
+                scale=gain_part[:, fc : fc + 1],
+            )
+
+        b_bank = {}
+
+        def turn_back(fc0, n):
+            b_bank[fc0] = ps = bank(n)
+            for q in range(4):
+                words = e_rows[fc0 + q // 2][:, q % 2, :, :].rearrange("p m e -> p (m e)").bitcast(F32)
+                nc.tensor.transpose(ps[:, q * P : (q + 1) * P], words, ident[:])
+
+        def pair_back(fc0):
+            words = e_grp[1][:, fc0 * P : (fc0 + 2) * P, :].rearrange("p n t -> p (n t)").bitcast(F32)
+            nc.scalar.copy(
+                out=words.rearrange("p (c n u) -> p c n u", c=2, u=2),
+                in_=b_bank[fc0][:].rearrange("p (c u n) -> p c n u", c=2, u=2),
+            )
+
+        def gain_to_partitions(n):
+            ps = bank(n)
+            nc.tensor.transpose(ps[:, 0:P], gain_pad[:], ident[:])
+            nc.scalar.copy(out=gain_part[:], in_=ps[:, 0 : F // P])
+
         def first_product(i, fc):
             t, h, n0 = i % 4, fc // 4, P * (fc % 4)
             for g in range(KG):
+                if i < 4:
+                    codes, scales = d_codes[i][:, g * P : (g + 1) * P], d_scales[i][:, g * P : (g + 1) * P]
+                else:
+                    codes, scales = late_codes[:, g, t * P : (t + 1) * P], late_scales[:, g, t * P : (t + 1) * P]
                 nc.tensor.matmul_mx(
                     out=e_bank[(i // 4, fc)][:, t * P : (t + 1) * P],
-                    lhsT=d_codes[i][:, g * P : (g + 1) * P].bitcast(E4M3),
-                    lhsT_scale=d_scales[i][:, g * P : (g + 1) * P],
+                    lhsT=codes.bitcast(E4M3),
+                    lhsT_scale=scales,
                     rhs=vw[h][:, g, 2 * n0 : 2 * n0 + 2 * P].bitcast(E2M1),
                     rhs_scale=vs[h][:, g, n0 : n0 + P],
                     start=(g == 0),
@@ -222,6 +288,13 @@ def tile_straight_through_weight_gradient_s9_kernel(
         def interleave(piece):
             g, c0 = piece // 4, 256 * (piece % 4)
             nc.scalar.copy(
+                out=x_grp[g][:, c0 : c0 + 256, :].rearrange("p (c i) j -> p c j i", i=4),
+                in_=x_sb[g][:, :, c0 : c0 + 256].rearrange("p j (c i) -> p c j i", i=4),
+            )
+
+        def interleave_v(piece):
+            g, c0 = piece // 4, 256 * (piece % 4)
+            nc.vector.tensor_copy(
                 out=x_grp[g][:, c0 : c0 + 256, :].rearrange("p (c i) j -> p c j i", i=4),
                 in_=x_sb[g][:, :, c0 : c0 + 256].rearrange("p j (c i) -> p c j i", i=4),
             )
@@ -284,88 +357,99 @@ def tile_straight_through_weight_gradient_s9_kernel(
 
         res = {}
 
-        for i in range(3):
-            turn(i, 2 * i + (i > 0))
-            if i == 0:
-                spread_turn("g", 2)
-            quantise_delta(i)
-        spread_copy("g")
-        for fc in range(4):
-            e_bank[(0, fc)] = bank(4 + fc)
-        sort_words(3)
-        sort_words(4)
-        clip(0, 0)
-        clip(0, 1)
-        for pair in range(2):
-            for i in (2 * pair, 2 * pair + 1):
-                for fc in range(4):
-                    first_product(i, fc)
-            turn(2 * pair + 3, 0)
-            turn(2 * pair + 4, 2)
-            if pair == 0:
-                quantise_delta(3)
-                quantise_delta(4)
-                interleave(0)
-                interleave(1)
-        for fc in range(4):
-            apply_gain(0, fc)
-        quantise_delta(5)
-        quantise_e(0, 0, HALF)
-        interleave(2)
-
         def chunk(g, fc, n):
             e_bank[(g, fc)] = bank(n)
             for t in range(4):
                 first_product(4 * g + t, fc)
             apply_gain(g, fc)
 
-        chunk(0, 4, 4)
-        quantise_delta(6)
+        nc.scalar.activation(out=gain_pad[0 : F // P, :], in_=gain_rows[:], func=ACT.Copy)
+        for i in range(3):
+            turn(i, 2 * i + (i > 0))
+            if i == 0:
+                spread_turn("g", 2)
+            quantise_delta(i)
+        spread_copy("g")
+        gain_to_partitions(0)
+        for fc in range(4):
+            e_bank[(0, fc)] = bank(4 + fc)
+        sort_words(3)
+        sort_words(4)
+        clip(0, 0)
+        clip(0, 1)
+        for i in (0, 1):
+            for fc in range(4):
+                first_product(i, fc)
+        turn(3, 0)
+        turn(4, 2)
+        quantise_delta(3)
+        sort_words(5)
+        interleave(0)
+        interleave(1)
+        for i in (2, 3):
+            for fc in range(4):
+                first_product(i, fc)
+        apply_gain(0, 0)
+        sort_words(6)
+        turn(5, 0)
+        turn(6, 2)
+        apply_gain(0, 1)
+        turn(7, 4)
+        apply_gain(0, 2)
+        apply_gain(0, 3)
         quantise_x(0, 0)
-        chunk(0, 5, 5)
-        turn(7, 0)
-        spread_turn("r", 7)
+        quantise_e(0, 0, HALF)
         clip(1, 0)
+        quantise_late(0)
+        quantise_late(1)
+        interleave(2)
+        chunk(0, 4, 6)
         clip(1, 1)
-        quantise_delta(7)
-        for piece in (3, 4, 5):
-            interleave(piece)
-        chunk(0, 6, 6)
-        quantise_x(0, 1)
-        chunk(0, 7, 2)
+        quantise_late(2)
+        quantise_late(3)
+        interleave(4)
+        interleave(5)
+        chunk(0, 5, 0)
+        spread_turn("r", 7)
         abs_w_bits(0)
-        chunk(1, 0, 3)
-        quantise_e(0, HALF, HALF)
+        chunk(0, 6, 1)
+        interleave(3)
         compare(0, 0)
-        abs_w(1, 0)
-        abs_w(2, 0)
-        chunk(1, 1, 4)
+        chunk(0, 7, 2)
+        abs_w_bits(1)
+        quantise_e(0, HALF, HALF)
+        turned_product(0, 3)
         quantise_x(1, 0)
         compare(0, 1)
-        interleave(6)
-        interleave(7)
-        chunk(1, 2, 5)
+        turned_product(1, 4)
+        quantise_x(0, 1)
         compare(1, 0)
-        chunk(1, 3, 0)
+        turned_product(2, 5)
+        abs_w_bits(2)
+        compare(1, 1)
+        turned_product(3, 6)
         compare(2, 0)
+        turned_product(4, 0)
+        turn_back(0, 1)
+        turn_back(2, 2)
+        pair_back(0)
+        pair_back(2)
+        compare(2, 1)
+        turned_product(5, 3)
+        interleave(6)
         quantise_e(1, 0, HALF)
+        chunk(1, 6, 4)
+        turn_back(4, 5)
+        pair_back(4)
+        interleave(7)
         abs_w(3, 0)
-        abs_w(1, 1)
-        chunk(1, 4, 1)
-        quantise_x(1, 1)
-        chunk(1, 5, 6)
-        compare(3, 0)
-        quantise_e(1, HALF, 256)
-        chunk(1, 6, 2)
         quantise_e(1, HALF + 256, P)
-        second_product(0, 3)
-        copy_out(0)
-        pool_mask(0)
+        second_product(0, 6)
+        finish(0)
         store(0)
-        abs_w(2, 1)
-        abs_w(3, 1)
-        chunk(1, 7, 4)
-        banks = (5, 0, 1, 6, 2, 3, 4)
+        quantise_e(1, HALF, 256)
+        chunk(1, 7, 0)
+        banks = (1, 2, 3, 4, 5, 6, 0)
         late = None
         for unit in range(1, 2 * CT):
             second_product(unit, banks[(unit - 1) % 7])
@@ -380,6 +464,12 @@ def tile_straight_through_weight_gradient_s9_kernel(
                     store(late)
                     late = None
             if unit == 1:
+                quantise_x(1, 1)
+            if unit == 2:
                 quantise_e(1, HALF + 384, P)
-            if unit in (4, 7, 10):
-                compare((unit - 1) // 3, 1)
+            if unit == 4:
+                compare(3, 0)
+            if unit == 6:
+                abs_w(3, 1)
+            if unit == 10:
+                compare(3, 1)

@@ -18,12 +18,15 @@ OP = mybir.AluOpType
 ACT = mybir.ActivationFunctionType
 
 P = 128
-KG = O // 512
-TG = T // 512
+PASSES = O // 512
+GROUPS = T // 512
 TILES = T // P
-CT = C // P
+CHUNKS = F // P
+ROW_TILES = C // P
 HALF = 512
 BANKS = 8
+SPLIT = (0, 3)
+POOLED = (5, 9)
 
 
 def tile_straight_through_weight_gradient_s9_kernel(
@@ -32,77 +35,74 @@ def tile_straight_through_weight_gradient_s9_kernel(
     nc = tc.nc
     with ExitStack() as ctx:
         keep = ctx.enter_context(tc.tile_pool(name="keep", bufs=1))
-        stage = ctx.enter_context(tc.tile_pool(name="stage", bufs=3))
-        outs = ctx.enter_context(tc.tile_pool(name="outs", bufs=8))
+        stage = ctx.enter_context(tc.tile_pool(name="stage", bufs=2))
+        outs = ctx.enter_context(tc.tile_pool(name="outs", bufs=2 * ROW_TILES))
         psum = ctx.enter_context(tc.psum_pool(name="psum", bufs=1))
         ctx.enter_context(tc.manual_schedule())
 
-        vs = [keep.tile([P, KG, HALF], U8, name=f"vs{h}", align_bytes=64) for h in range(2)]
+        v_planes = [keep.tile([P, PASSES, HALF], U8, name=f"v_planes{h}", align_bytes=64) for h in range(2)]
         for h in range(2):
-            nc.vector.memset(vs[h][:].rearrange("p g n -> p (g n)").bitcast(I32), 0)
-        ident = keep.tile([P, P], F32)
-        make_identity(nc, ident[:])
-        gain_col = keep.tile([P, F // P], BF16)
-        r_col = keep.tile([P, F // P], BF16)
-        gain_rows = keep.tile([F // P, P], BF16)
-        gain_pad = keep.tile([P, P], F32)
+            nc.vector.memset(v_planes[h][:].rearrange("p g n -> p (g n)").bitcast(I32), 0)
+        gain_pad = keep.tile([P, P], F32, name="gain_pad")
         nc.vector.memset(gain_pad[:], 0.0)
-        gain_part = keep.tile([P, F // P], F32)
-        lo_sb = keep.tile([P, TG, 4], BF16)
-        hi_sb = keep.tile([P, TG, 4], BF16)
+        ident = keep.tile([P, P], F32, name="ident")
+        make_identity(nc, ident[:])
 
-        delta_v = delta.rearrange("(g m t) k -> g t m k", m=P, t=4)
+        gain_rows = keep.tile([CHUNKS, P], BF16, name="gain_rows")
+        gain_part = keep.tile([P, CHUNKS], F32, name="gain_part")
+        r_col = keep.tile([P, F // P], BF16, name="r_col")
+        r_all = keep.tile([P, F], BF16, name="r_all")
+        lo_sb = keep.tile([P, GROUPS, 4], BF16, name="lo_sb")
+        hi_sb = keep.tile([P, GROUPS, 4], BF16, name="hi_sb")
+        d_sb = [[keep.tile([P, O // 2], BF16, name=f"d_sb{i}_{b}") for b in range(2)] if i in SPLIT else keep.tile([P, O], BF16, name=f"d_sb{i}") for i in range(TILES)]
+        v_codes = [[keep.tile([P, 2, F], U8, name=f"v_codes{h}_{b}", align_bytes=64) for b in range(2)] for h in range(2)]
+        x_sb = [[keep.tile([P, 4, HALF], BF16, name=f"x_sb{g}_{a}") for a in range(2)] for g in range(GROUPS)]
+        w_sb = [keep.tile([P, 2, F], BF16, name=f"w_sb{a}") for a in range(ROW_TILES // 2)]
+
         x_v = x.rearrange("(g p j) c -> g p j c", p=P, j=4)
         w_v = w.rearrange("(ct p) f -> p ct f", p=P)
-        vw_v = v_words.rearrange("g p b -> p g b")
-        vs_v = v_scales.rearrange("g q n -> q g n").bitcast(I32)
-
-        d_first = [keep.tile([P, O // 2], BF16, name=f"d_first{b}") for b in range(2)]
-        d_sb = [None] + [keep.tile([P, O], BF16, name=f"d_sb{i}") for i in range(1, TILES)]
-        vw = [keep.tile([P, KG, F], U8, name=f"vw{h}", align_bytes=64) for h in range(2)]
-        gain_bc = keep.tile([P, F], BF16)
-        x_sb = [keep.tile([P, 4, C], BF16, name=f"x_sb{g}") for g in range(TG)]
-        w_sb = [keep.tile([P, 2, F], BF16, name=f"w_sb{a}") for a in range(CT // 2)]
+        words_v = v_words.rearrange("g p b -> p g b")
+        scales_v = v_scales.rearrange("g q n -> q g n").bitcast(I32)
 
         def load_delta(i):
-            rows = delta_v[i // 4, i % 4]
-            if i == 0:
+            rows = delta[i * P : (i + 1) * P, :]
+            if i in SPLIT:
                 for b in range(2):
-                    nc.sync.dma_start(out=d_first[b][:], in_=rows[:, b * O // 2 : (b + 1) * O // 2])
+                    nc.sync.dma_start(out=d_sb[i][b][:], in_=rows[:, b * O // 2 : (b + 1) * O // 2])
             else:
                 nc.sync.dma_start(out=d_sb[i][:], in_=rows)
 
         def load_v(h):
             for q in range(4):
                 nc.sync.dma_start(
-                    out=vs[h][32 * q : 32 * q + 4, :, :].bitcast(I32),
-                    in_=vs_v[4 * q : 4 * q + 4, :, h * P : (h + 1) * P],
+                    out=v_planes[h][32 * q : 32 * q + 4, :, :].bitcast(I32),
+                    in_=scales_v[4 * q : 4 * q + 4, :, h * P : (h + 1) * P],
                 )
-            nc.sync.dma_start(out=vw[h][:], in_=vw_v[:, :, h * F : (h + 1) * F])
+            for b in range(2):
+                nc.sync.dma_start(out=v_codes[h][b][:], in_=words_v[:, 2 * b : 2 * b + 2, h * F : (h + 1) * F])
 
         def load_x(g, a):
-            nc.sync.dma_start(out=x_sb[g][:, 2 * a : 2 * a + 2, :], in_=x_v[g, :, 2 * a : 2 * a + 2, :])
+            nc.sync.dma_start(out=x_sb[g][a][:], in_=x_v[g, :, :, a * HALF : (a + 1) * HALF])
 
         def load_w(a):
             nc.sync.dma_start(out=w_sb[a][:], in_=w_v[:, 2 * a : 2 * a + 2, :])
 
         nc.scalar.dma_start(out=gain_rows[:], in_=gain.rearrange("(c p) -> c p", p=P))
-        nc.scalar.dma_start(out=gain_col[:], in_=gain.rearrange("(p c) -> p c", p=P))
+        nc.scalar.dma_start(out=r_col[:], in_=r.rearrange("(p c) -> p c", p=P))
         nc.gpsimd.dma_start(out=lo_sb[:], in_=lo.rearrange("(g p j) -> p g j", p=P, j=4))
         nc.gpsimd.dma_start(out=hi_sb[:], in_=hi.rearrange("(g p j) -> p g j", p=P, j=4))
         load_delta(0)
         load_delta(1)
         load_delta(2)
-        load_v(0)
         load_delta(3)
-        load_delta(4)
         load_x(0, 0)
-        load_x(0, 1)
+        load_v(0)
+        load_delta(4)
         load_delta(5)
+        load_x(0, 1)
+        load_v(1)
         load_delta(6)
         load_delta(7)
-        load_v(1)
-        nc.sync.dma_start(out=r_col[:], in_=r.rearrange("(p c) -> p c", p=P))
         load_x(1, 0)
         load_x(1, 1)
         load_w(0)
@@ -110,162 +110,113 @@ def tile_straight_through_weight_gradient_s9_kernel(
         load_w(2)
         load_w(3)
 
-        d_codes = [keep.tile([P, 512], U32, name=f"d_codes{i}", align_bytes=64) for i in range(4)]
-        d_scales = [keep.tile([P, 512], U8, name=f"d_scales{i}", align_bytes=64) for i in range(4)]
-        late_grp = keep.tile([P, KG, 4, P, 4], BF16, align_bytes=64)
-        late_codes = keep.tile([P, KG, 512], U32, align_bytes=64)
-        late_scales = keep.tile([P, KG, 512], U8, align_bytes=64)
-        x_grp = [keep.tile([P, C, 4], BF16, name=f"x_grp{g}", align_bytes=64) for g in range(TG)]
-        x_codes = [keep.tile([P, C], U32, name=f"x_codes{g}", align_bytes=64) for g in range(TG)]
-        x_scales = [keep.tile([P, C], U8, name=f"x_scales{g}", align_bytes=64) for g in range(TG)]
-        e_grp = [keep.tile([P, F, 4], BF16, name=f"e_grp{g}", align_bytes=64) for g in range(TG)]
-        e_codes = [keep.tile([P, F], U32, name=f"e_codes{g}", align_bytes=64) for g in range(TG)]
-        e_scales = [keep.tile([P, F], U8, name=f"e_scales{g}", align_bytes=64) for g in range(TG)]
-        mask = keep.tile([P, CT, F], BF16)
+        d_grp = [keep.tile([P, PASSES, 4, P, 4], BF16, name=f"d_grp{g}", align_bytes=64) for g in range(GROUPS)]
+        d_codes = [keep.tile([P, PASSES, 512], U32, name=f"d_codes{g}", align_bytes=64) for g in range(GROUPS)]
+        d_scales = [keep.tile([P, PASSES, 512], U8, name=f"d_scales{g}", align_bytes=64) for g in range(GROUPS)]
+        x_grp = [keep.tile([P, C, 4], BF16, name=f"x_grp{g}", align_bytes=64) for g in range(GROUPS)]
+        x_codes = [keep.tile([P, C], U32, name=f"x_codes{g}", align_bytes=64) for g in range(GROUPS)]
+        x_scales = [keep.tile([P, C], U8, name=f"x_scales{g}", align_bytes=64) for g in range(GROUPS)]
+        e_grp = [keep.tile([P, F, 4], BF16, name=f"e_grp{g}", align_bytes=64) for g in range(GROUPS)]
+        e_codes = [keep.tile([P, F], U32, name=f"e_codes{g}", align_bytes=64) for g in range(GROUPS)]
+        e_scales = [keep.tile([P, F], U8, name=f"e_scales{g}", align_bytes=64) for g in range(GROUPS)]
 
         def bank(n):
             return psum.tile([P, 512], F32, name=f"bank{n}", tag=f"bank{n}")
 
-        d_sorted = {}
-        d_grp = {}
-        e_bank = {}
-        o_bank = {}
+        d_sorted, t_bank, y_bank, b_bank, o_bank, e_rows, res = {}, {}, {}, {}, {}, {}, {}
 
         def sort_words(i):
-            d_sorted[i] = stage.tile([P, O // 2], F32, name="d_sorted", bufs=2)
+            d_sorted[i] = stage.tile([P, O // 2], F32, name="d_sorted")
             nc.vector.tensor_copy(
-                out=d_sorted[i][:].rearrange("p (g u m) -> p g u m", g=KG, u=2),
-                in_=d_sb[i][:].bitcast(F32).rearrange("p (g m u) -> p g u m", g=KG, u=2),
+                out=d_sorted[i][:].rearrange("p (g u m i) -> p g m u i", g=PASSES, u=2, i=2),
+                in_=d_sb[i][:].bitcast(F32).rearrange("p (g m i u) -> p g m u i", g=PASSES, u=2, i=2),
             )
 
-        t_bank = {}
-
-        def turn_half(i, b, n):
+        def turn(i, b, n):
             t_bank[(i, b)] = ps = bank(n)
             for q in range(4):
                 g, u = q // 2, q % 2
-                if i == 0:
-                    src = d_first[b][:].bitcast(F32)[:, 256 * g + u : 256 * (g + 1) : 2]
-                elif i not in d_sorted:
-                    src = d_sb[i][:].bitcast(F32)[:, 256 * (2 * b + g) + u : 256 * (2 * b + g + 1) : 2]
-                else:
+                if i in SPLIT:
+                    src = d_sb[i][b][:].bitcast(F32)[:, 256 * g + u : 256 * (g + 1) : 2]
+                elif i in d_sorted:
                     src = d_sorted[i][:, (4 * b + q) * P : (4 * b + q + 1) * P]
+                else:
+                    src = d_sb[i][:].bitcast(F32)[:, 256 * (2 * b + g) + u : 256 * (2 * b + g + 1) : 2]
                 nc.tensor.transpose(ps[:, q * P : (q + 1) * P], src, ident[:])
 
-        def turn(i, n):
-            for b in range(2):
-                turn_half(i, b, n + b)
-                pair_words(i, b)
-
         def pair_words(i, b):
-            if i >= 4:
-                words = late_grp[:, :, i - 4, :, :].rearrange("p g m t -> p g (m t)").bitcast(F32)
-                words = words.rearrange("p g (m u) -> p g m u", u=2)
-            else:
-                if b == 0:
-                    d_grp[i] = stage.tile([P, KG, P, 4], BF16, name="d_grp", align_bytes=64)
-                words = d_grp[i][:].rearrange("p g m t -> p (g m t)").bitcast(F32)
-                words = words.rearrange("p (g m u) -> p g m u", g=KG, u=2)
+            words = d_grp[i // 4][:, 2 * b : 2 * b + 2, i % 4, :, :].rearrange("p g m t -> p g (m t)").bitcast(F32)
             nc.scalar.copy(
-                out=words[:, 2 * b : 2 * b + 2, :, :],
+                out=words.rearrange("p g (m u) -> p g m u", u=2),
                 in_=t_bank[(i, b)][:].rearrange("p (g u m) -> p g m u", g=2, u=2),
             )
 
-        s_bank = {}
+        def turn_tile(i, n):
+            for b in range(2):
+                turn(i, b, n + b)
+                pair_words(i, b)
 
-        def spread_turn(which, n):
-            s_bank[which] = ps = bank(n)
-            words = {"g": gain_col, "r": r_col}[which][:].bitcast(F32)
-            for c in range(4):
-                nc.tensor.transpose(ps[:, c::4], words[:, c : c + 1].to_broadcast([P, P]), ident[:])
-
-        def spread_copy(which):
-            nc.scalar.copy(
-                out=gain_bc[:].bitcast(F32),
-                in_=s_bank[which][:],
-            )
-
-        def quantise_delta(i):
+        def quantise_delta(k, first, count):
+            g, t = first // 4, first % 4
+            cols = slice(t * P, (t + count) * P)
             nc.vector.quantize_mx(
-                out=d_codes[i][:].bitcast(E4M3),
-                scales=d_scales[i][:],
-                in_=d_grp[i][:].rearrange("p g m t -> p (g m t)"),
+                out=d_codes[g][:, k, cols].bitcast(E4M3),
+                scales=d_scales[g][:, k, cols],
+                in_=d_grp[g][:, k, t : t + count, :, :].rearrange("p t m j -> p (t m j)"),
             )
 
-        def quantise_late(g):
-            nc.vector.quantize_mx(
-                out=late_codes[:, g, :].bitcast(E4M3),
-                scales=late_scales[:, g, :],
-                in_=late_grp[:, g, :, :, :].rearrange("p t m j -> p (t m j)"),
-            )
-
-        e_rows = {}
-
-        def turned_product(fc, n):
+        def first_pass(g, fc, k):
             h, n0 = fc // 4, P * (fc % 4)
-            ps = bank(n)
-            for g in range(KG):
-                nc.tensor.matmul_mx(
-                    out=ps[:],
-                    lhsT=vw[h][:, g, 2 * n0 : 2 * n0 + 2 * P].bitcast(E2M1),
-                    lhsT_scale=vs[h][:, g, n0 : n0 + P],
-                    rhs=late_codes[:, g, :].bitcast(E4M3),
-                    rhs_scale=late_scales[:, g, :],
-                    start=(g == 0),
-                    stop=(g == KG - 1),
-                )
-            e_rows[fc] = stage.tile([P, 2, P, 2], BF16, name="e_rows", bufs=6)
+            nc.tensor.matmul_mx(
+                out=y_bank[(g, fc)][:],
+                lhsT=v_codes[h][k // 2][:, k % 2, 2 * n0 : 2 * n0 + 2 * P].bitcast(E2M1),
+                lhsT_scale=v_planes[h][:, k, n0 : n0 + P],
+                rhs=d_codes[g][:, k, :].bitcast(E4M3),
+                rhs_scale=d_scales[g][:, k, :],
+                start=(k == 0),
+                stop=(k == PASSES - 1),
+            )
+
+        def first_product(g, chunks, banks):
+            for fc, n in zip(chunks, banks):
+                y_bank[(g, fc)] = bank(n)
+            for k in range(PASSES):
+                for fc in chunks:
+                    first_pass(g, fc, k)
+
+        def apply_gain(g, fc):
+            e_rows[(g, fc)] = stage.tile([P, 2, P, 2], BF16, name="e_rows", bufs=10)
             nc.scalar.activation(
-                out=e_rows[fc][:],
-                in_=ps[:].rearrange("p (u e m) -> p u m e", u=2, e=2),
+                out=e_rows[(g, fc)][:],
+                in_=y_bank[(g, fc)][:].rearrange("p (m u e) -> p u m e", u=2, e=2),
                 func=ACT.Copy,
                 scale=gain_part[:, fc : fc + 1],
             )
 
-        b_bank = {}
-
-        def turn_back(fc0, n):
-            b_bank[fc0] = ps = bank(n)
+        def turn_back(g, fc0, n):
+            b_bank[(g, fc0)] = ps = bank(n)
             for q in range(4):
-                words = e_rows[fc0 + q // 2][:, q % 2, :, :].rearrange("p m e -> p (m e)").bitcast(F32)
+                words = e_rows[(g, fc0 + q // 2)][:, q % 2, :, :].rearrange("p m e -> p (m e)").bitcast(F32)
                 nc.tensor.transpose(ps[:, q * P : (q + 1) * P], words, ident[:])
 
-        def pair_back(fc0):
-            words = e_grp[1][:, fc0 * P : (fc0 + 2) * P, :].rearrange("p n t -> p (n t)").bitcast(F32)
-            nc.scalar.copy(
+        def pair_back(g, fc0, copy):
+            words = e_grp[g][:, fc0 * P : (fc0 + 2) * P, :].rearrange("p n t -> p (n t)").bitcast(F32)
+            copy(
                 out=words.rearrange("p (c n u) -> p c n u", c=2, u=2),
-                in_=b_bank[fc0][:].rearrange("p (c u n) -> p c n u", c=2, u=2),
+                in_=b_bank[(g, fc0)][:].rearrange("p (c u n) -> p c n u", c=2, u=2),
             )
 
         def gain_to_partitions(n):
             ps = bank(n)
             nc.tensor.transpose(ps[:, 0:P], gain_pad[:], ident[:])
-            nc.scalar.copy(out=gain_part[:], in_=ps[:, 0 : F // P])
+            nc.scalar.copy(out=gain_part[:], in_=ps[:, 0:CHUNKS])
 
-        def first_product(i, fc):
-            t, h, n0 = i % 4, fc // 4, P * (fc % 4)
-            for g in range(KG):
-                if i < 4:
-                    codes, scales = d_codes[i][:, g * P : (g + 1) * P], d_scales[i][:, g * P : (g + 1) * P]
-                else:
-                    codes, scales = late_codes[:, g, t * P : (t + 1) * P], late_scales[:, g, t * P : (t + 1) * P]
-                nc.tensor.matmul_mx(
-                    out=e_bank[(i // 4, fc)][:, t * P : (t + 1) * P],
-                    lhsT=codes.bitcast(E4M3),
-                    lhsT_scale=scales,
-                    rhs=vw[h][:, g, 2 * n0 : 2 * n0 + 2 * P].bitcast(E2M1),
-                    rhs_scale=vs[h][:, g, n0 : n0 + P],
-                    start=(g == 0),
-                    stop=(g == KG - 1),
-                )
-
-        def apply_gain(g, fc):
-            nc.vector.tensor_tensor(
-                out=e_grp[g][:, fc * P : (fc + 1) * P, :],
-                in0=e_bank[(g, fc)][:].rearrange("p (t n) -> p n t", t=4),
-                in1=gain_bc[:, fc * P : (fc + 1) * P].unsqueeze(2).to_broadcast([P, P, 4]),
-                op=OP.mult,
-            )
+        def spread_r(n):
+            ps = bank(n)
+            words = r_col[:].bitcast(F32)
+            for c in range(4):
+                nc.tensor.transpose(ps[:, c::4], words[:, c : c + 1].to_broadcast([P, P]), ident[:])
+            nc.scalar.copy(out=r_all[:].bitcast(F32), in_=ps[:])
 
         def quantise_e(g, f0, n):
             nc.vector.quantize_mx(
@@ -275,28 +226,21 @@ def tile_straight_through_weight_gradient_s9_kernel(
             )
 
         def clip(g, a):
-            for j in (2 * a, 2 * a + 1):
+            for j in range(4):
                 nc.vector.tensor_scalar(
-                    out=x_sb[g][:, j, :],
-                    in0=x_sb[g][:, j, :],
+                    out=x_sb[g][a][:, j, :],
+                    in0=x_sb[g][a][:, j, :],
                     scalar1=lo_sb[:, g, j : j + 1],
                     scalar2=hi_sb[:, g, j : j + 1],
                     op0=OP.max,
                     op1=OP.min,
                 )
 
-        def interleave(piece):
-            g, c0 = piece // 4, 256 * (piece % 4)
-            nc.scalar.copy(
-                out=x_grp[g][:, c0 : c0 + 256, :].rearrange("p (c i) j -> p c j i", i=4),
-                in_=x_sb[g][:, :, c0 : c0 + 256].rearrange("p j (c i) -> p c j i", i=4),
-            )
-
-        def interleave_v(piece):
-            g, c0 = piece // 4, 256 * (piece % 4)
-            nc.vector.tensor_copy(
-                out=x_grp[g][:, c0 : c0 + 256, :].rearrange("p (c i) j -> p c j i", i=4),
-                in_=x_sb[g][:, :, c0 : c0 + 256].rearrange("p j (c i) -> p c j i", i=4),
+        def interleave(g, k, copy):
+            cols = slice(256 * k, 256 * (k + 1))
+            copy(
+                out=x_grp[g][:, cols, :].rearrange("p (c i) j -> p c j i", i=4),
+                in_=x_sb[g][k // 2][:, :, 256 * (k % 2) : 256 * (k % 2 + 1)].rearrange("p j (c i) -> p c j i", i=4),
             )
 
         def quantise_x(g, k):
@@ -307,27 +251,22 @@ def tile_straight_through_weight_gradient_s9_kernel(
                 in_=x_grp[g][:, cols, :].rearrange("p c j -> p (c j)"),
             )
 
-        def abs_w(a, h):
-            part = w_sb[a][:, :, h * HALF : (h + 1) * HALF]
-            nc.scalar.activation(out=part, in_=part, func=ACT.Abs)
-
-        def abs_w_bits(a):
+        def abs_w(a):
             bits = w_sb[a][:].rearrange("p c f -> p (c f)").bitcast(I32)
             nc.vector.tensor_scalar(out=bits, in0=bits, scalar1=0x7FFF7FFF, scalar2=None, op0=OP.bitwise_and)
 
-        def compare(a, h):
-            cols = slice(h * HALF, (h + 1) * HALF)
+        def compare(a):
             nc.vector.tensor_tensor(
-                out=mask[:, 2 * a : 2 * a + 2, cols],
-                in0=w_sb[a][:, :, cols],
-                in1=s_bank["r"][:].bitcast(BF16)[:, cols].unsqueeze(1).to_broadcast([P, 2, HALF]),
+                out=w_sb[a][:],
+                in0=w_sb[a][:],
+                in1=r_all[:].unsqueeze(1).to_broadcast([P, 2, F]),
                 op=OP.is_le,
             )
 
         def second_product(unit, n):
-            h, ct = unit // CT, unit % CT
+            h, ct = unit // ROW_TILES, unit % ROW_TILES
             o_bank[unit] = bank(n)
-            for g in range(TG):
+            for g in range(GROUPS):
                 nc.tensor.matmul_mx(
                     out=o_bank[unit][:],
                     lhsT=x_codes[g][:, ct * P : (ct + 1) * P].bitcast(E4M3),
@@ -335,141 +274,124 @@ def tile_straight_through_weight_gradient_s9_kernel(
                     rhs=e_codes[g][:, h * HALF : (h + 1) * HALF].bitcast(E5M2),
                     rhs_scale=e_scales[g][:, h * HALF : (h + 1) * HALF],
                     start=(g == 0),
-                    stop=(g == TG - 1),
+                    stop=(g == GROUPS - 1),
                 )
 
-        def finish(unit):
-            h, ct = unit // CT, unit % CT
+        def apply_mask(unit, on_vector):
+            h, ct = unit // ROW_TILES, unit % ROW_TILES
             res[unit] = outs.tile([P, HALF], F32, name="res")
-            nc.vector.tensor_tensor(out=res[unit][:], in0=o_bank[unit][:], in1=mask[:, ct, h * HALF : (h + 1) * HALF], op=OP.mult)
-
-        def copy_out(unit):
-            res[unit] = outs.tile([P, HALF], F32, name="res")
-            nc.scalar.copy(out=res[unit][:], in_=o_bank[unit][:])
-
-        def pool_mask(unit):
-            h, ct = unit // CT, unit % CT
-            nc.gpsimd.tensor_tensor(out=res[unit][:], in0=res[unit][:], in1=mask[:, ct, h * HALF : (h + 1) * HALF], op=OP.mult)
+            keep_mask = w_sb[ct // 2][:, ct % 2, h * HALF : (h + 1) * HALF]
+            if on_vector:
+                nc.vector.tensor_tensor(out=res[unit][:], in0=o_bank[unit][:], in1=keep_mask, op=OP.mult)
+            else:
+                nc.scalar.copy(out=res[unit][:], in_=o_bank[unit][:])
+                nc.gpsimd.tensor_tensor(out=res[unit][:], in0=res[unit][:], in1=keep_mask, op=OP.mult)
 
         def store(unit):
-            h, ct = unit // CT, unit % CT
+            h, ct = unit // ROW_TILES, unit % ROW_TILES
             nc.sync.dma_start(out=out[ct * P : (ct + 1) * P, h * HALF : (h + 1) * HALF], in_=res[unit][:])
 
-        res = {}
+        on_vector, on_scalar = nc.vector.tensor_copy, nc.scalar.copy
 
-        def chunk(g, fc, n):
-            e_bank[(g, fc)] = bank(n)
-            for t in range(4):
-                first_product(4 * g + t, fc)
-            apply_gain(g, fc)
-
-        nc.scalar.activation(out=gain_pad[0 : F // P, :], in_=gain_rows[:], func=ACT.Copy)
-        for i in range(3):
-            turn(i, 2 * i + (i > 0))
-            if i == 0:
-                spread_turn("g", 2)
-            quantise_delta(i)
-        spread_copy("g")
-        gain_to_partitions(0)
-        for fc in range(4):
-            e_bank[(0, fc)] = bank(4 + fc)
-        sort_words(3)
-        sort_words(4)
-        clip(0, 0)
-        clip(0, 1)
-        for i in (0, 1):
-            for fc in range(4):
-                first_product(i, fc)
-        turn(3, 0)
-        turn(4, 2)
-        quantise_delta(3)
-        sort_words(5)
-        interleave(0)
-        interleave(1)
-        for i in (2, 3):
-            for fc in range(4):
-                first_product(i, fc)
+        nc.scalar.activation(out=gain_pad[0:CHUNKS, :], in_=gain_rows[:], func=ACT.Copy)
+        for i in range(4):
+            turn_tile(i, 2 * i % 6)
+            if i == 3:
+                clip(0, 0)
+            if i % 2 == 1:
+                for k in range(PASSES):
+                    quantise_delta(k, i - 1, 2)
+        gain_to_partitions(2)
+        spread_r(3)
+        interleave(0, 0, on_scalar)
+        interleave(0, 1, on_scalar)
+        first_product(0, (0, 1), (4, 5))
         apply_gain(0, 0)
-        sort_words(6)
-        turn(5, 0)
-        turn(6, 2)
         apply_gain(0, 1)
-        turn(7, 4)
-        apply_gain(0, 2)
-        apply_gain(0, 3)
+        sort_words(4)
+        sort_words(5)
         quantise_x(0, 0)
-        quantise_e(0, 0, HALF)
-        clip(1, 0)
-        quantise_late(0)
-        quantise_late(1)
-        interleave(2)
-        chunk(0, 4, 6)
-        clip(1, 1)
-        quantise_late(2)
-        quantise_late(3)
-        interleave(4)
-        interleave(5)
-        chunk(0, 5, 0)
-        spread_turn("r", 7)
-        abs_w_bits(0)
-        chunk(0, 6, 1)
-        interleave(3)
-        compare(0, 0)
-        chunk(0, 7, 2)
-        abs_w_bits(1)
-        quantise_e(0, HALF, HALF)
-        turned_product(0, 3)
-        quantise_x(1, 0)
-        compare(0, 1)
-        turned_product(1, 4)
+        clip(0, 1)
+        for fc in (2, 3):
+            first_product(0, (fc,), (4 + fc,))
+            apply_gain(0, fc)
+        turn_tile(4, 0)
+        turn_tile(5, 2)
+        turn_back(0, 0, 4)
+        turn_back(0, 2, 5)
+        interleave(0, 2, on_vector)
+        interleave(0, 3, on_vector)
+        pair_back(0, 0, on_vector)
+        sort_words(6)
+        pair_back(0, 2, on_vector)
         quantise_x(0, 1)
-        compare(1, 0)
-        turned_product(2, 5)
-        abs_w_bits(2)
-        compare(1, 1)
-        turned_product(3, 6)
-        compare(2, 0)
-        turned_product(4, 0)
-        turn_back(0, 1)
-        turn_back(2, 2)
-        pair_back(0)
-        pair_back(2)
-        compare(2, 1)
-        turned_product(5, 3)
-        interleave(6)
+        for fc in (4, 5):
+            first_product(0, (fc,), (2 + fc,))
+            apply_gain(0, fc)
+        turn_tile(6, 0)
+        turn_tile(7, 2)
+        clip(1, 0)
+        quantise_e(0, 0, HALF)
+        for fc in (6, 7):
+            first_product(0, (fc,), (fc - 2,))
+            apply_gain(0, fc)
+        for k in range(PASSES):
+            quantise_delta(k, 4, 4)
+        clip(1, 1)
+        interleave(1, 0, on_scalar)
+        first_product(1, (0, 1), (6, 7))
+        apply_gain(1, 0)
+        apply_gain(1, 1)
+        abs_w(0)
+        abs_w(1)
+        compare(0)
+        first_product(1, (2,), (0,))
+        apply_gain(1, 2)
+        interleave(1, 1, on_scalar)
+        compare(1)
+        first_product(1, (3,), (1,))
+        apply_gain(1, 3)
+        abs_w(2)
+        quantise_x(1, 0)
+        first_product(1, (4,), (2,))
+        turn_back(1, 0, 3)
+        turn_back(1, 2, 4)
+        turn_back(0, 4, 5)
+        turn_back(0, 6, 6)
+        pair_back(1, 0, on_scalar)
+        pair_back(1, 2, on_scalar)
+        apply_gain(1, 4)
+        compare(2)
+        abs_w(3)
+        first_product(1, (5,), (7,))
+        apply_gain(1, 5)
+        interleave(1, 2, on_scalar)
         quantise_e(1, 0, HALF)
-        chunk(1, 6, 4)
-        turn_back(4, 5)
-        pair_back(4)
-        interleave(7)
-        abs_w(3, 0)
-        quantise_e(1, HALF + 256, P)
-        second_product(0, 6)
-        finish(0)
-        store(0)
-        quantise_e(1, HALF, 256)
-        chunk(1, 7, 0)
-        banks = (1, 2, 3, 4, 5, 6, 0)
-        late = None
-        for unit in range(1, 2 * CT):
-            second_product(unit, banks[(unit - 1) % 7])
-            if unit % 3 == 0 and unit < 15:
-                copy_out(unit)
-                pool_mask(unit)
-                late = unit
-            else:
-                finish(unit)
-                store(unit)
-                if late is not None:
-                    store(late)
-                    late = None
-            if unit == 1:
-                quantise_x(1, 1)
+        compare(3)
+        first_product(1, (6,), (0,))
+        apply_gain(1, 6)
+        pair_back(0, 4, on_scalar)
+        interleave(1, 3, on_vector)
+        banks = (1, 3, 4, 7, 0, 2, 5, 6)
+        for unit in range(2 * ROW_TILES):
+            second_product(unit, banks[unit % BANKS])
+            if unit == 0:
+                first_product(1, (7,), (2,))
+                pair_back(0, 6, on_scalar)
+                apply_gain(1, 7)
             if unit == 2:
-                quantise_e(1, HALF + 384, P)
+                turn_back(1, 4, 5)
+                turn_back(1, 6, 6)
+                pair_back(1, 4, on_scalar)
+                pair_back(1, 6, on_scalar)
+            apply_mask(unit, unit not in POOLED)
+            if unit not in POOLED:
+                store(unit)
+            if unit - 3 in POOLED:
+                store(unit - 3)
+            if unit == 0:
+                quantise_x(1, 1)
+            if unit == 1:
+                quantise_e(0, HALF, HALF)
             if unit == 4:
-                compare(3, 0)
-            if unit == 6:
-                abs_w(3, 1)
-            if unit == 10:
-                compare(3, 1)
+                quantise_e(1, HALF, HALF)

@@ -36,7 +36,7 @@ def tile_straight_through_weight_gradient_s9_kernel(
     with ExitStack() as ctx:
         keep = ctx.enter_context(tc.tile_pool(name="keep", bufs=1))
         stage = ctx.enter_context(tc.tile_pool(name="stage", bufs=2))
-        outs = ctx.enter_context(tc.tile_pool(name="outs", bufs=2 * ROW_TILES))
+        outs = ctx.enter_context(tc.tile_pool(name="outs", bufs=14))
         psum = ctx.enter_context(tc.psum_pool(name="psum", bufs=1))
         ctx.enter_context(tc.manual_schedule())
 
@@ -56,7 +56,8 @@ def tile_straight_through_weight_gradient_s9_kernel(
         hi_sb = keep.tile([P, GROUPS, 4], BF16, name="hi_sb")
         d_sb = [[keep.tile([P, O // 2], BF16, name=f"d_sb{i}_{b}") for b in range(2)] if i in SPLIT else keep.tile([P, O], BF16, name=f"d_sb{i}") for i in range(TILES)]
         v_codes = [[keep.tile([P, 2, F], U8, name=f"v_codes{h}_{b}", align_bytes=64) for b in range(2)] for h in range(2)]
-        x_sb = [[keep.tile([P, 4, HALF], BF16, name=f"x_sb{g}_{a}") for a in range(2)] for g in range(GROUPS)]
+        x_first = [keep.tile([P, 4, HALF], BF16, name=f"x_sb0_{a}") for a in range(2)]
+        x_late = keep.tile([P, 4, C], BF16, name="x_sb1")
         w_sb = [keep.tile([P, 2, F], BF16, name=f"w_sb{a}") for a in range(ROW_TILES // 2)]
 
         x_v = x.rearrange("(g p j) c -> g p j c", p=P, j=4)
@@ -72,17 +73,21 @@ def tile_straight_through_weight_gradient_s9_kernel(
             else:
                 nc.sync.dma_start(out=d_sb[i][:], in_=rows)
 
-        def load_v(h):
+        def load_v_scales(h):
             for q in range(4):
                 nc.sync.dma_start(
                     out=v_planes[h][32 * q : 32 * q + 4, :, :].bitcast(I32),
                     in_=scales_v[4 * q : 4 * q + 4, :, h * P : (h + 1) * P],
                 )
-            for b in range(2):
-                nc.sync.dma_start(out=v_codes[h][b][:], in_=words_v[:, 2 * b : 2 * b + 2, h * F : (h + 1) * F])
+
+        def load_v_codes(h, b):
+            nc.sync.dma_start(out=v_codes[h][b][:], in_=words_v[:, 2 * b : 2 * b + 2, h * F : (h + 1) * F])
 
         def load_x(g, a):
-            nc.sync.dma_start(out=x_sb[g][a][:], in_=x_v[g, :, :, a * HALF : (a + 1) * HALF])
+            if g == 0:
+                nc.sync.dma_start(out=x_first[a][:], in_=x_v[0, :, :, a * HALF : (a + 1) * HALF])
+            else:
+                nc.sync.dma_start(out=x_late[:, 2 * a : 2 * a + 2, :], in_=x_v[1, :, 2 * a : 2 * a + 2, :])
 
         def load_w(a):
             nc.sync.dma_start(out=w_sb[a][:], in_=w_v[:, 2 * a : 2 * a + 2, :])
@@ -96,11 +101,15 @@ def tile_straight_through_weight_gradient_s9_kernel(
         load_delta(2)
         load_delta(3)
         load_x(0, 0)
-        load_v(0)
+        load_v_scales(0)
+        load_v_codes(0, 0)
+        load_v_codes(0, 1)
         load_delta(4)
         load_delta(5)
         load_x(0, 1)
-        load_v(1)
+        load_v_scales(1)
+        load_v_codes(1, 0)
+        load_v_codes(1, 1)
         load_delta(6)
         load_delta(7)
         load_x(1, 0)
@@ -144,9 +153,9 @@ def tile_straight_through_weight_gradient_s9_kernel(
                     src = d_sb[i][:].bitcast(F32)[:, 256 * (2 * b + g) + u : 256 * (2 * b + g + 1) : 2]
                 nc.tensor.transpose(ps[:, q * P : (q + 1) * P], src, ident[:])
 
-        def pair_words(i, b):
+        def pair_words(i, b, copy):
             words = d_grp[i // 4][:, 2 * b : 2 * b + 2, i % 4, :, :].rearrange("p g m t -> p g (m t)").bitcast(F32)
-            nc.scalar.copy(
+            copy(
                 out=words.rearrange("p g (m u) -> p g m u", u=2),
                 in_=t_bank[(i, b)][:].rearrange("p (g u m) -> p g m u", g=2, u=2),
             )
@@ -154,7 +163,7 @@ def tile_straight_through_weight_gradient_s9_kernel(
         def turn_tile(i, n):
             for b in range(2):
                 turn(i, b, n + b)
-                pair_words(i, b)
+                pair_words(i, b, nc.scalar.copy)
 
         def quantise_delta(k, first, count):
             g, t = first // 4, first % 4
@@ -226,10 +235,11 @@ def tile_straight_through_weight_gradient_s9_kernel(
             )
 
         def clip(g, a):
-            for j in range(4):
+            for j in range(4) if g == 0 else (2 * a, 2 * a + 1):
+                row = x_first[a][:, j, :] if g == 0 else x_late[:, j, :]
                 nc.vector.tensor_scalar(
-                    out=x_sb[g][a][:, j, :],
-                    in0=x_sb[g][a][:, j, :],
+                    out=row,
+                    in0=row,
                     scalar1=lo_sb[:, g, j : j + 1],
                     scalar2=hi_sb[:, g, j : j + 1],
                     op0=OP.max,
@@ -240,7 +250,7 @@ def tile_straight_through_weight_gradient_s9_kernel(
             cols = slice(256 * k, 256 * (k + 1))
             copy(
                 out=x_grp[g][:, cols, :].rearrange("p (c i) j -> p c j i", i=4),
-                in_=x_sb[g][k // 2][:, :, 256 * (k % 2) : 256 * (k % 2 + 1)].rearrange("p j (c i) -> p c j i", i=4),
+                in_=(x_first[k // 2][:, :, 256 * (k % 2) : 256 * (k % 2 + 1)] if g == 0 else x_late[:, :, cols]).rearrange("p j (c i) -> p c j i", i=4),
             )
 
         def quantise_x(g, k):
@@ -294,93 +304,105 @@ def tile_straight_through_weight_gradient_s9_kernel(
         on_vector, on_scalar = nc.vector.tensor_copy, nc.scalar.copy
 
         nc.scalar.activation(out=gain_pad[0:CHUNKS, :], in_=gain_rows[:], func=ACT.Copy)
-        for i in range(4):
-            turn_tile(i, 2 * i % 6)
-            if i == 3:
-                clip(0, 0)
-            if i % 2 == 1:
-                for k in range(PASSES):
-                    quantise_delta(k, i - 1, 2)
-        gain_to_partitions(2)
-        spread_r(3)
+        turn_tile(0, 0)
+        gain_to_partitions(4)
+        turn_tile(1, 2)
+        for k in range(2):
+            quantise_delta(k, 0, 2)
+        turn(2, 0, 0)
+        pair_words(2, 0, on_scalar)
+        turn(3, 0, 1)
+        pair_words(3, 0, on_scalar)
+        clip(0, 0)
+        for i in (2, 3):
+            turn(i, 1, i)
+            pair_words(i, 1, on_scalar)
+        for k in range(PASSES):
+            quantise_delta(k, *((2, 2) if k < 2 else (0, 4)))
+        spread_r(0)
         interleave(0, 0, on_scalar)
         interleave(0, 1, on_scalar)
-        first_product(0, (0, 1), (4, 5))
-        apply_gain(0, 0)
-        apply_gain(0, 1)
+        for fc in range(4):
+            y_bank[(0, fc)] = bank(4 + fc)
+        for k in range(2):
+            for fc in range(4):
+                first_pass(0, fc, k)
+        for fc in range(4):
+            for k in range(2, PASSES):
+                first_pass(0, fc, k)
+            apply_gain(0, fc)
         sort_words(4)
         sort_words(5)
-        quantise_x(0, 0)
         clip(0, 1)
-        for fc in (2, 3):
-            first_product(0, (fc,), (4 + fc,))
-            apply_gain(0, fc)
         turn_tile(4, 0)
         turn_tile(5, 2)
         turn_back(0, 0, 4)
         turn_back(0, 2, 5)
+        quantise_x(0, 0)
         interleave(0, 2, on_vector)
-        interleave(0, 3, on_vector)
         pair_back(0, 0, on_vector)
-        sort_words(6)
         pair_back(0, 2, on_vector)
-        quantise_x(0, 1)
+        sort_words(6)
+        for k in range(PASSES):
+            quantise_delta(k, 4, 2)
         for fc in (4, 5):
-            first_product(0, (fc,), (2 + fc,))
+            first_product(0, (fc,), ((3 + fc) % BANKS,))
             apply_gain(0, fc)
-        turn_tile(6, 0)
-        turn_tile(7, 2)
+        turn_tile(6, 1)
+        turn_tile(7, 3)
         clip(1, 0)
-        quantise_e(0, 0, HALF)
+        interleave(0, 3, on_vector)
+        clip(1, 1)
         for fc in (6, 7):
-            first_product(0, (fc,), (fc - 2,))
+            first_product(0, (fc,), (fc - 1,))
             apply_gain(0, fc)
         for k in range(PASSES):
-            quantise_delta(k, 4, 4)
-        clip(1, 1)
+            quantise_delta(k, 6, 2)
         interleave(1, 0, on_scalar)
-        first_product(1, (0, 1), (6, 7))
+        first_product(1, (0, 1), (7, 0))
         apply_gain(1, 0)
         apply_gain(1, 1)
         abs_w(0)
-        abs_w(1)
+        quantise_e(0, 0, HALF)
         compare(0)
-        first_product(1, (2,), (0,))
-        apply_gain(1, 2)
+        abs_w(1)
         interleave(1, 1, on_scalar)
+        first_product(1, (2,), (1,))
+        apply_gain(1, 2)
+        quantise_x(0, 1)
         compare(1)
-        first_product(1, (3,), (1,))
+        first_product(1, (3,), (2,))
         apply_gain(1, 3)
         abs_w(2)
         quantise_x(1, 0)
-        first_product(1, (4,), (2,))
-        turn_back(1, 0, 3)
-        turn_back(1, 2, 4)
-        turn_back(0, 4, 5)
-        turn_back(0, 6, 6)
+        first_product(1, (4,), (3,))
+        turn_back(0, 4, 4)
+        turn_back(0, 6, 5)
+        turn_back(1, 0, 6)
+        turn_back(1, 2, 7)
         pair_back(1, 0, on_scalar)
         pair_back(1, 2, on_scalar)
         apply_gain(1, 4)
         compare(2)
         abs_w(3)
-        first_product(1, (5,), (7,))
+        first_product(1, (5,), (0,))
         apply_gain(1, 5)
         interleave(1, 2, on_scalar)
         quantise_e(1, 0, HALF)
         compare(3)
-        first_product(1, (6,), (0,))
+        first_product(1, (6,), (1,))
         apply_gain(1, 6)
-        pair_back(0, 4, on_scalar)
         interleave(1, 3, on_vector)
-        banks = (1, 3, 4, 7, 0, 2, 5, 6)
+        banks = (2, 7, 3, 0, 4, 5, 1, 6)
         for unit in range(2 * ROW_TILES):
             second_product(unit, banks[unit % BANKS])
             if unit == 0:
-                first_product(1, (7,), (2,))
-                pair_back(0, 6, on_scalar)
+                first_product(1, (7,), (6,))
                 apply_gain(1, 7)
+                pair_back(0, 4, on_scalar)
+                pair_back(0, 6, on_scalar)
             if unit == 2:
-                turn_back(1, 4, 5)
+                turn_back(1, 4, 1)
                 turn_back(1, 6, 6)
                 pair_back(1, 4, on_scalar)
                 pair_back(1, 6, on_scalar)
@@ -391,7 +413,7 @@ def tile_straight_through_weight_gradient_s9_kernel(
                 store(unit - 3)
             if unit == 0:
                 quantise_x(1, 1)
-            if unit == 1:
+            if unit == 2:
                 quantise_e(0, HALF, HALF)
             if unit == 4:
                 quantise_e(1, HALF, HALF)

@@ -44,7 +44,6 @@ def tile_straight_through_weight_gradient_s9_kernel(
         for h in range(2):
             nc.vector.memset(v_planes[h][:].rearrange("p g n -> p (g n)").bitcast(I32), 0)
         gain_pad = keep.tile([P, P], F32, name="gain_pad")
-        nc.vector.memset(gain_pad[:], 0.0)
         ident = keep.tile([P, P], F32, name="ident")
         make_identity(nc, ident[:])
 
@@ -303,9 +302,9 @@ def tile_straight_through_weight_gradient_s9_kernel(
 
         on_vector, on_scalar = nc.vector.tensor_copy, nc.scalar.copy
 
-        nc.scalar.activation(out=gain_pad[0:CHUNKS, :], in_=gain_rows[:], func=ACT.Copy)
+        nc.scalar.activation(out=gain_pad[:], in_=ident[:], func=ACT.Copy, scale=0.0)
         turn_tile(0, 0)
-        gain_to_partitions(4)
+        nc.scalar.activation(out=gain_pad[0:CHUNKS, :], in_=gain_rows[:], func=ACT.Copy)
         turn_tile(1, 2)
         for k in range(2):
             quantise_delta(k, 0, 2)
@@ -319,6 +318,7 @@ def tile_straight_through_weight_gradient_s9_kernel(
             pair_words(i, 1, on_scalar)
         for k in range(PASSES):
             quantise_delta(k, *((2, 2) if k < 2 else (0, 4)))
+        gain_to_partitions(1)
         spread_r(0)
         interleave(0, 0, on_scalar)
         interleave(0, 1, on_scalar)

@@ -21,12 +21,10 @@ P = 128
 PASSES = O // 512
 GROUPS = T // 512
 TILES = T // P
-CHUNKS = F // P
 ROW_TILES = C // P
 HALF = 512
 BANKS = 8
 SPLIT = (0, 3)
-POOLED = (5, 9)
 
 
 def tile_straight_through_weight_gradient_s9_kernel(
@@ -35,28 +33,33 @@ def tile_straight_through_weight_gradient_s9_kernel(
     nc = tc.nc
     with ExitStack() as ctx:
         keep = ctx.enter_context(tc.tile_pool(name="keep", bufs=1))
-        stage = ctx.enter_context(tc.tile_pool(name="stage", bufs=2))
-        outs = ctx.enter_context(tc.tile_pool(name="outs", bufs=14))
+        stage = ctx.enter_context(tc.tile_pool(name="stage", bufs=3))
+        outs = ctx.enter_context(tc.tile_pool(name="outs", bufs=10))
         psum = ctx.enter_context(tc.psum_pool(name="psum", bufs=1))
         ctx.enter_context(tc.manual_schedule())
 
         v_planes = [keep.tile([P, PASSES, HALF], U8, name=f"v_planes{h}", align_bytes=64) for h in range(2)]
         for h in range(2):
             nc.vector.memset(v_planes[h][:].rearrange("p g n -> p (g n)").bitcast(I32), 0)
-        gain_pad = keep.tile([P, P], F32, name="gain_pad")
         ident = keep.tile([P, P], F32, name="ident")
         make_identity(nc, ident[:])
 
-        gain_rows = keep.tile([CHUNKS, P], BF16, name="gain_rows")
-        gain_part = keep.tile([P, CHUNKS], F32, name="gain_part")
+        gain_rows = keep.tile([F // P, P], BF16, name="gain_rows")
+        gain_pad = keep.tile([P, P], F32, name="gain_pad")
+        gain_part = keep.tile([P, F // P], F32, name="gain_part")
         r_col = keep.tile([P, F // P], BF16, name="r_col")
         r_all = keep.tile([P, F], BF16, name="r_all")
         lo_sb = keep.tile([P, GROUPS, 4], BF16, name="lo_sb")
         hi_sb = keep.tile([P, GROUPS, 4], BF16, name="hi_sb")
-        d_sb = [[keep.tile([P, O // 2], BF16, name=f"d_sb{i}_{b}") for b in range(2)] if i in SPLIT else keep.tile([P, O], BF16, name=f"d_sb{i}") for i in range(TILES)]
+        d_sb = [
+            [keep.tile([P, O // 2], BF16, name=f"d_sb{i}_{b}") for b in range(2)]
+            if i in SPLIT
+            else keep.tile([P, O], BF16, name=f"d_sb{i}")
+            for i in range(TILES)
+        ]
         v_codes = [[keep.tile([P, 2, F], U8, name=f"v_codes{h}_{b}", align_bytes=64) for b in range(2)] for h in range(2)]
-        x_first = [keep.tile([P, 4, HALF], BF16, name=f"x_sb0_{a}") for a in range(2)]
-        x_late = keep.tile([P, 4, C], BF16, name="x_sb1")
+        x_first = [keep.tile([P, 4, HALF], BF16, name=f"x_first{a}") for a in range(2)]
+        x_late = keep.tile([P, 4, C], BF16, name="x_late")
         w_sb = [keep.tile([P, 2, F], BF16, name=f"w_sb{a}") for a in range(ROW_TILES // 2)]
 
         x_v = x.rearrange("(g p j) c -> g p j c", p=P, j=4)
@@ -73,10 +76,10 @@ def tile_straight_through_weight_gradient_s9_kernel(
                 nc.sync.dma_start(out=d_sb[i][:], in_=rows)
 
         def load_v_scales(h):
-            for q in range(4):
+            for s in range(4):
                 nc.sync.dma_start(
-                    out=v_planes[h][32 * q : 32 * q + 4, :, :].bitcast(I32),
-                    in_=scales_v[4 * q : 4 * q + 4, :, h * P : (h + 1) * P],
+                    out=v_planes[h][s:P:32, :, :].bitcast(I32),
+                    in_=scales_v[s:16:4, :, h * P : (h + 1) * P],
                 )
 
         def load_v_codes(h, b):
@@ -91,36 +94,15 @@ def tile_straight_through_weight_gradient_s9_kernel(
         def load_w(a):
             nc.sync.dma_start(out=w_sb[a][:], in_=w_v[:, 2 * a : 2 * a + 2, :])
 
-        nc.scalar.dma_start(out=gain_rows[:], in_=gain.rearrange("(c p) -> c p", p=P))
-        nc.scalar.dma_start(out=r_col[:], in_=r.rearrange("(p c) -> p c", p=P))
-        nc.gpsimd.dma_start(out=lo_sb[:], in_=lo.rearrange("(g p j) -> p g j", p=P, j=4))
-        nc.gpsimd.dma_start(out=hi_sb[:], in_=hi.rearrange("(g p j) -> p g j", p=P, j=4))
-        load_delta(0)
-        load_delta(1)
-        load_delta(2)
-        load_delta(3)
-        load_x(0, 0)
-        load_v_scales(0)
-        load_v_codes(0, 0)
-        load_v_codes(0, 1)
-        load_delta(4)
-        load_delta(5)
-        load_x(0, 1)
-        load_v_scales(1)
-        load_v_codes(1, 0)
-        load_v_codes(1, 1)
-        load_delta(6)
-        load_delta(7)
-        load_x(1, 0)
-        load_x(1, 1)
-        load_w(0)
-        load_w(1)
-        load_w(2)
-        load_w(3)
+        d_codes = [keep.tile([P, PASSES * 512], U32, name=f"d_codes{g}", align_bytes=64) for g in range(GROUPS)]
+        d_scales = [keep.tile([P, PASSES * 512], U8, name=f"d_scales{g}", align_bytes=64) for g in range(GROUPS)]
 
         d_grp = [keep.tile([P, PASSES, 4, P, 4], BF16, name=f"d_grp{g}", align_bytes=64) for g in range(GROUPS)]
-        d_codes = [keep.tile([P, PASSES, 512], U32, name=f"d_codes{g}", align_bytes=64) for g in range(GROUPS)]
-        d_scales = [keep.tile([P, PASSES, 512], U8, name=f"d_scales{g}", align_bytes=64) for g in range(GROUPS)]
+
+        def d_cols(i, k, n=1):
+            first = 512 * k + P * (i % 4)
+            return slice(first, first + n * P)
+
         x_grp = [keep.tile([P, C, 4], BF16, name=f"x_grp{g}", align_bytes=64) for g in range(GROUPS)]
         x_codes = [keep.tile([P, C], U32, name=f"x_codes{g}", align_bytes=64) for g in range(GROUPS)]
         x_scales = [keep.tile([P, C], U8, name=f"x_scales{g}", align_bytes=64) for g in range(GROUPS)]
@@ -131,93 +113,8 @@ def tile_straight_through_weight_gradient_s9_kernel(
         def bank(n):
             return psum.tile([P, 512], F32, name=f"bank{n}", tag=f"bank{n}")
 
-        d_sorted, t_bank, y_bank, b_bank, o_bank, e_rows, res = {}, {}, {}, {}, {}, {}, {}
-
-        def sort_words(i):
-            d_sorted[i] = stage.tile([P, O // 2], F32, name="d_sorted")
-            nc.vector.tensor_copy(
-                out=d_sorted[i][:].rearrange("p (g u m i) -> p g m u i", g=PASSES, u=2, i=2),
-                in_=d_sb[i][:].bitcast(F32).rearrange("p (g m i u) -> p g m u i", g=PASSES, u=2, i=2),
-            )
-
-        def turn(i, b, n):
-            t_bank[(i, b)] = ps = bank(n)
-            for q in range(4):
-                g, u = q // 2, q % 2
-                if i in SPLIT:
-                    src = d_sb[i][b][:].bitcast(F32)[:, 256 * g + u : 256 * (g + 1) : 2]
-                elif i in d_sorted:
-                    src = d_sorted[i][:, (4 * b + q) * P : (4 * b + q + 1) * P]
-                else:
-                    src = d_sb[i][:].bitcast(F32)[:, 256 * (2 * b + g) + u : 256 * (2 * b + g + 1) : 2]
-                nc.tensor.transpose(ps[:, q * P : (q + 1) * P], src, ident[:])
-
-        def pair_words(i, b, copy):
-            words = d_grp[i // 4][:, 2 * b : 2 * b + 2, i % 4, :, :].rearrange("p g m t -> p g (m t)").bitcast(F32)
-            copy(
-                out=words.rearrange("p g (m u) -> p g m u", u=2),
-                in_=t_bank[(i, b)][:].rearrange("p (g u m) -> p g m u", g=2, u=2),
-            )
-
-        def turn_tile(i, n):
-            for b in range(2):
-                turn(i, b, n + b)
-                pair_words(i, b, nc.scalar.copy)
-
-        def quantise_delta(k, first, count):
-            g, t = first // 4, first % 4
-            cols = slice(t * P, (t + count) * P)
-            nc.vector.quantize_mx(
-                out=d_codes[g][:, k, cols].bitcast(E4M3),
-                scales=d_scales[g][:, k, cols],
-                in_=d_grp[g][:, k, t : t + count, :, :].rearrange("p t m j -> p (t m j)"),
-            )
-
-        def first_pass(g, fc, k):
-            h, n0 = fc // 4, P * (fc % 4)
-            nc.tensor.matmul_mx(
-                out=y_bank[(g, fc)][:],
-                lhsT=v_codes[h][k // 2][:, k % 2, 2 * n0 : 2 * n0 + 2 * P].bitcast(E2M1),
-                lhsT_scale=v_planes[h][:, k, n0 : n0 + P],
-                rhs=d_codes[g][:, k, :].bitcast(E4M3),
-                rhs_scale=d_scales[g][:, k, :],
-                start=(k == 0),
-                stop=(k == PASSES - 1),
-            )
-
-        def first_product(g, chunks, banks):
-            for fc, n in zip(chunks, banks):
-                y_bank[(g, fc)] = bank(n)
-            for k in range(PASSES):
-                for fc in chunks:
-                    first_pass(g, fc, k)
-
-        def apply_gain(g, fc):
-            e_rows[(g, fc)] = stage.tile([P, 2, P, 2], BF16, name="e_rows", bufs=10)
-            nc.scalar.activation(
-                out=e_rows[(g, fc)][:],
-                in_=y_bank[(g, fc)][:].rearrange("p (m u e) -> p u m e", u=2, e=2),
-                func=ACT.Copy,
-                scale=gain_part[:, fc : fc + 1],
-            )
-
-        def turn_back(g, fc0, n):
-            b_bank[(g, fc0)] = ps = bank(n)
-            for q in range(4):
-                words = e_rows[(g, fc0 + q // 2)][:, q % 2, :, :].rearrange("p m e -> p (m e)").bitcast(F32)
-                nc.tensor.transpose(ps[:, q * P : (q + 1) * P], words, ident[:])
-
-        def pair_back(g, fc0, copy):
-            words = e_grp[g][:, fc0 * P : (fc0 + 2) * P, :].rearrange("p n t -> p (n t)").bitcast(F32)
-            copy(
-                out=words.rearrange("p (c n u) -> p c n u", c=2, u=2),
-                in_=b_bank[(g, fc0)][:].rearrange("p (c u n) -> p c n u", c=2, u=2),
-            )
-
-        def gain_to_partitions(n):
-            ps = bank(n)
-            nc.tensor.transpose(ps[:, 0:P], gain_pad[:], ident[:])
-            nc.scalar.copy(out=gain_part[:], in_=ps[:, 0:CHUNKS])
+        z_bank, e_rows, b_bank = {}, {}, {}
+        d_sorted, o_bank, res = {}, {}, {}
 
         def spread_r(n):
             ps = bank(n)
@@ -226,11 +123,93 @@ def tile_straight_through_weight_gradient_s9_kernel(
                 nc.tensor.transpose(ps[:, c::4], words[:, c : c + 1].to_broadcast([P, P]), ident[:])
             nc.scalar.copy(out=r_all[:].bitcast(F32), in_=ps[:])
 
-        def quantise_e(g, f0, n):
+        def sort_words(i, copy):
+            d_sorted[i] = stage.tile([P, O // 2], F32, name="d_sorted", bufs=4)
+            copy(
+                out=d_sorted[i][:].rearrange("p (g u m i) -> p g m u i", g=PASSES, u=2, i=2),
+                in_=d_sb[i][:].bitcast(F32).rearrange("p (g m i u) -> p g m u i", g=PASSES, u=2, i=2),
+            )
+
+        def turn_half(i, b, n, copy=nc.scalar.copy):
+            ps = bank(n)
+            for q in range(4):
+                k, u = q // 2, q % 2
+                if i in SPLIT:
+                    src = d_sb[i][b][:].bitcast(F32)[:, 256 * k + u : 256 * (k + 1) : 2]
+                elif i in d_sorted:
+                    src = d_sorted[i][:, (4 * b + q) * P : (4 * b + q + 1) * P]
+                else:
+                    src = d_sb[i][:].bitcast(F32)[:, 256 * (2 * b + k) + u : 256 * (2 * b + k + 1) : 2]
+                nc.tensor.transpose(ps[:, q * P : (q + 1) * P], src, ident[:])
+            words = d_grp[i // 4][:, 2 * b : 2 * b + 2, i % 4, :, :].rearrange("p k m t -> p k (m t)").bitcast(F32)
+            copy(
+                out=words.rearrange("p k (m u) -> p k m u", u=2),
+                in_=ps[:].rearrange("p (k u m) -> p k m u", k=2, u=2),
+            )
+
+        def turn(i, n):
+            for b in range(2):
+                turn_half(i, b, n + b)
+
+        def quantise_delta(i, n=1, passes=range(PASSES)):
+            for k in passes:
+                nc.vector.quantize_mx(
+                    out=d_codes[i // 4][:, d_cols(i, k, n)].bitcast(E4M3),
+                    scales=d_scales[i // 4][:, d_cols(i, k, n)],
+                    in_=d_grp[i // 4][:, k, i % 4 : i % 4 + n, :, :].rearrange("p t m j -> p (t m j)"),
+                )
+
+        def first_pass(g, fc, k):
+            h, n0 = fc // 4, P * (fc % 4)
+            nc.tensor.matmul_mx(
+                out=z_bank[(g, fc)][:],
+                lhsT=v_codes[h][k // 2][:, k % 2, 2 * n0 : 2 * (n0 + P)].bitcast(E2M1),
+                lhsT_scale=v_planes[h][:, k, n0 : n0 + P],
+                rhs=d_codes[g][:, 512 * k : 512 * (k + 1)].bitcast(E4M3),
+                rhs_scale=d_scales[g][:, 512 * k : 512 * (k + 1)],
+                start=(k == 0),
+                stop=(k == PASSES - 1),
+            )
+
+        def first_product(g, fc, n):
+            z_bank[(g, fc)] = bank(n)
+            for k in range(PASSES):
+                first_pass(g, fc, k)
+
+        def scale_rows(g, fc):
+            e_rows[(g, fc)] = stage.tile([P, 2, P, 2], BF16, name="e_rows", bufs=10)
+            nc.scalar.activation(
+                out=e_rows[(g, fc)][:],
+                in_=z_bank[(g, fc)][:].rearrange("p (m u e) -> p u m e", u=2, e=2),
+                func=ACT.Copy,
+                scale=gain_part[:, fc : fc + 1],
+            )
+
+        def turn_back(g, fc, n, count=2):
+            b_bank[(g, fc)] = ps = bank(n)
+            for c in range(count):
+                for u in range(2):
+                    words = e_rows[(g, fc + c)][:, u, :, :].rearrange("p m e -> p (m e)").bitcast(F32)
+                    nc.tensor.transpose(ps[:, (2 * c + u) * P : (2 * c + u + 1) * P], words, ident[:])
+
+        def pair_back(g, fc, copy, count=2):
+            words = e_grp[g][:, fc * P : (fc + count) * P, :].rearrange("p n t -> p (n t)").bitcast(F32)
+            copy(
+                out=words.rearrange("p (c n u) -> p c n u", c=count, u=2),
+                in_=b_bank[(g, fc)][:, 0 : 2 * count * P].rearrange("p (c u n) -> p c n u", c=count, u=2),
+            )
+
+        def gain_to_partitions(n):
+            ps = bank(n)
+            nc.tensor.transpose(ps[:, 0:P], gain_pad[:], ident[:])
+            nc.scalar.copy(out=gain_part[:], in_=ps[:, 0 : F // P])
+
+        def quantise_e(g, fc, count):
+            cols = slice(fc * P, (fc + count) * P)
             nc.vector.quantize_mx(
-                out=e_codes[g][:, f0 : f0 + n].bitcast(E5M2),
-                scales=e_scales[g][:, f0 : f0 + n],
-                in_=e_grp[g][:, f0 : f0 + n, :].rearrange("p n t -> p (n t)"),
+                out=e_codes[g][:, cols].bitcast(E5M2),
+                scales=e_scales[g][:, cols],
+                in_=e_grp[g][:, cols, :].rearrange("p n t -> p (n t)"),
             )
 
         def clip(g, a):
@@ -247,9 +226,10 @@ def tile_straight_through_weight_gradient_s9_kernel(
 
         def interleave(g, k, copy):
             cols = slice(256 * k, 256 * (k + 1))
+            rows = x_first[k // 2][:, :, 256 * (k % 2) : 256 * (k % 2 + 1)] if g == 0 else x_late[:, :, cols]
             copy(
                 out=x_grp[g][:, cols, :].rearrange("p (c i) j -> p c j i", i=4),
-                in_=(x_first[k // 2][:, :, 256 * (k % 2) : 256 * (k % 2 + 1)] if g == 0 else x_late[:, :, cols]).rearrange("p j (c i) -> p c j i", i=4),
+                in_=rows.rearrange("p j (c i) -> p c j i", i=4),
             )
 
         def quantise_x(g, k):
@@ -264,11 +244,12 @@ def tile_straight_through_weight_gradient_s9_kernel(
             bits = w_sb[a][:].rearrange("p c f -> p (c f)").bitcast(I32)
             nc.vector.tensor_scalar(out=bits, in0=bits, scalar1=0x7FFF7FFF, scalar2=None, op0=OP.bitwise_and)
 
-        def compare(a):
+        def compare(a, h):
+            cols = slice(h * HALF, (h + 1) * HALF)
             nc.vector.tensor_tensor(
-                out=w_sb[a][:],
-                in0=w_sb[a][:],
-                in1=r_all[:].unsqueeze(1).to_broadcast([P, 2, F]),
+                out=w_sb[a][:, :, cols],
+                in0=w_sb[a][:, :, cols],
+                in1=r_all[:, cols].unsqueeze(1).to_broadcast([P, 2, HALF]),
                 op=OP.is_le,
             )
 
@@ -286,134 +267,179 @@ def tile_straight_through_weight_gradient_s9_kernel(
                     stop=(g == GROUPS - 1),
                 )
 
-        def apply_mask(unit, on_vector):
-            h, ct = unit // ROW_TILES, unit % ROW_TILES
-            res[unit] = outs.tile([P, HALF], F32, name="res")
-            keep_mask = w_sb[ct // 2][:, ct % 2, h * HALF : (h + 1) * HALF]
-            if on_vector:
-                nc.vector.tensor_tensor(out=res[unit][:], in0=o_bank[unit][:], in1=keep_mask, op=OP.mult)
-            else:
-                nc.scalar.copy(out=res[unit][:], in_=o_bank[unit][:])
-                nc.gpsimd.tensor_tensor(out=res[unit][:], in0=res[unit][:], in1=keep_mask, op=OP.mult)
-
         def store(unit):
             h, ct = unit // ROW_TILES, unit % ROW_TILES
             nc.sync.dma_start(out=out[ct * P : (ct + 1) * P, h * HALF : (h + 1) * HALF], in_=res[unit][:])
 
+        def apply_mask(unit):
+            h, ct = unit // ROW_TILES, unit % ROW_TILES
+            res[unit] = outs.tile([P, HALF], F32, name="res")
+            keep_mask = w_sb[ct // 2][:, ct % 2, h * HALF : (h + 1) * HALF]
+            nc.vector.tensor_tensor(out=res[unit][:], in0=o_bank[unit][:], in1=keep_mask, op=OP.mult)
+            store(unit)
+
+        def apply_mask_pooled(unit):
+            h, ct = unit // ROW_TILES, unit % ROW_TILES
+            res[unit] = outs.tile([P, HALF], F32, name="res")
+            keep_mask = w_sb[ct // 2][:, ct % 2, h * HALF : (h + 1) * HALF]
+            nc.scalar.copy(out=res[unit][:], in_=o_bank[unit][:])
+            nc.gpsimd.tensor_tensor(out=res[unit][:], in0=res[unit][:], in1=keep_mask, op=OP.mult)
+
         on_vector, on_scalar = nc.vector.tensor_copy, nc.scalar.copy
 
+        nc.scalar.dma_start(out=r_col[:], in_=r.rearrange("(p c) -> p c", p=P))
+        nc.scalar.dma_start(out=gain_rows[:], in_=gain.rearrange("(c p) -> c p", p=P))
+        nc.gpsimd.dma_start(out=lo_sb[:], in_=lo.rearrange("(g p j) -> p g j", p=P, j=4))
+        nc.gpsimd.dma_start(out=hi_sb[:], in_=hi.rearrange("(g p j) -> p g j", p=P, j=4))
+        for i in range(4):
+            load_delta(i)
+        load_v_scales(0)
+        load_v_codes(0, 0)
+        load_v_codes(0, 1)
+        load_x(0, 0)
+        for i in range(4, TILES):
+            load_delta(i)
+        load_v_scales(1)
+        load_v_codes(1, 0)
+        load_v_codes(1, 1)
+        load_x(1, 0)
+        load_x(1, 1)
+        load_w(0)
+        load_x(0, 1)
+        load_w(1)
+        load_w(2)
+        load_w(3)
+
         nc.scalar.activation(out=gain_pad[:], in_=ident[:], func=ACT.Copy, scale=0.0)
-        turn_tile(0, 0)
-        nc.scalar.activation(out=gain_pad[0:CHUNKS, :], in_=gain_rows[:], func=ACT.Copy)
-        turn_tile(1, 2)
-        for k in range(2):
-            quantise_delta(k, 0, 2)
-        turn(2, 0, 0)
-        pair_words(2, 0, on_scalar)
-        turn(3, 0, 1)
-        pair_words(3, 0, on_scalar)
-        clip(0, 0)
-        for i in (2, 3):
-            turn(i, 1, i)
-            pair_words(i, 1, on_scalar)
-        for k in range(PASSES):
-            quantise_delta(k, *((2, 2) if k < 2 else (0, 4)))
-        gain_to_partitions(1)
-        spread_r(0)
-        interleave(0, 0, on_scalar)
-        interleave(0, 1, on_scalar)
+        spread_r(7)
+        nc.vector.tensor_copy(out=gain_pad[0 : F // P, :], in_=gain_rows[:])
+        turn(0, 0)
+        turn(1, 2)
+        quantise_delta(0, 2)
+        turn_half(2, 0, 0)
+        quantise_delta(2, 1, (0, 1))
+        turn_half(3, 0, 1)
+        quantise_delta(3, 1, (0, 1))
+        turn_half(2, 1, 2)
+        turn_half(3, 1, 3)
+        gain_to_partitions(0)
+        quantise_delta(2, 2, (2, 3))
         for fc in range(4):
-            y_bank[(0, fc)] = bank(4 + fc)
+            z_bank[(0, fc)] = bank(4 + fc)
         for k in range(2):
             for fc in range(4):
                 first_pass(0, fc, k)
+        clip(0, 0)
+        sort_words(4, on_scalar)
+        interleave(0, 0, on_vector)
+        interleave(0, 1, on_vector)
+        sort_words(5, on_vector)
+        quantise_x(0, 0)
+        sort_words(6, on_vector)
+        sort_words(7, on_vector)
         for fc in range(4):
             for k in range(2, PASSES):
                 first_pass(0, fc, k)
-            apply_gain(0, fc)
-        sort_words(4)
-        sort_words(5)
-        clip(0, 1)
-        turn_tile(4, 0)
-        turn_tile(5, 2)
-        turn_back(0, 0, 4)
-        turn_back(0, 2, 5)
-        quantise_x(0, 0)
-        interleave(0, 2, on_vector)
-        pair_back(0, 0, on_vector)
-        pair_back(0, 2, on_vector)
-        sort_words(6)
-        for k in range(PASSES):
-            quantise_delta(k, 4, 2)
-        for fc in (4, 5):
-            first_product(0, (fc,), ((3 + fc) % BANKS,))
-            apply_gain(0, fc)
-        turn_tile(6, 1)
-        turn_tile(7, 3)
+            scale_rows(0, fc)
+        turn(4, 0)
+        turn_half(5, 0, 2)
+        turn_half(5, 1, 3, on_vector)
+        turn_half(6, 0, 4)
+        turn_half(6, 1, 5, on_vector)
+        quantise_delta(4, 2)
+        turn(7, 6)
+        quantise_delta(6, 2)
+        first_product(0, 4, 0)
+        first_product(0, 5, 1)
+        scale_rows(0, 4)
+        first_product(1, 0, 2)
+        scale_rows(0, 5)
         clip(1, 0)
-        interleave(0, 3, on_vector)
         clip(1, 1)
-        for fc in (6, 7):
-            first_product(0, (fc,), (fc - 1,))
-            apply_gain(0, fc)
-        for k in range(PASSES):
-            quantise_delta(k, 6, 2)
+        scale_rows(1, 0)
+        first_product(1, 1, 3)
         interleave(1, 0, on_scalar)
-        first_product(1, (0, 1), (7, 0))
-        apply_gain(1, 0)
-        apply_gain(1, 1)
+        scale_rows(1, 1)
         abs_w(0)
-        quantise_e(0, 0, HALF)
-        compare(0)
-        abs_w(1)
-        interleave(1, 1, on_scalar)
-        first_product(1, (2,), (1,))
-        apply_gain(1, 2)
-        quantise_x(0, 1)
-        compare(1)
-        first_product(1, (3,), (2,))
-        apply_gain(1, 3)
-        abs_w(2)
-        quantise_x(1, 0)
-        first_product(1, (4,), (3,))
-        turn_back(0, 4, 4)
-        turn_back(0, 6, 5)
-        turn_back(1, 0, 6)
-        turn_back(1, 2, 7)
-        pair_back(1, 0, on_scalar)
-        pair_back(1, 2, on_scalar)
-        apply_gain(1, 4)
-        compare(2)
-        abs_w(3)
-        first_product(1, (5,), (0,))
-        apply_gain(1, 5)
+        interleave(1, 1, on_vector)
+        first_product(1, 2, 4)
+        clip(0, 1)
+        scale_rows(1, 2)
+        compare(0, 0)
+        first_product(1, 3, 5)
         interleave(1, 2, on_scalar)
-        quantise_e(1, 0, HALF)
-        compare(3)
-        first_product(1, (6,), (1,))
-        apply_gain(1, 6)
-        interleave(1, 3, on_vector)
-        banks = (2, 7, 3, 0, 4, 5, 1, 6)
-        for unit in range(2 * ROW_TILES):
-            second_product(unit, banks[unit % BANKS])
-            if unit == 0:
-                first_product(1, (7,), (6,))
-                apply_gain(1, 7)
-                pair_back(0, 4, on_scalar)
-                pair_back(0, 6, on_scalar)
-            if unit == 2:
-                turn_back(1, 4, 1)
-                turn_back(1, 6, 6)
-                pair_back(1, 4, on_scalar)
-                pair_back(1, 6, on_scalar)
-            apply_mask(unit, unit not in POOLED)
-            if unit not in POOLED:
-                store(unit)
-            if unit - 3 in POOLED:
-                store(unit - 3)
-            if unit == 0:
-                quantise_x(1, 1)
-            if unit == 2:
-                quantise_e(0, HALF, HALF)
-            if unit == 4:
-                quantise_e(1, HALF, HALF)
+        scale_rows(1, 3)
+        quantise_x(1, 0)
+        turn_back(0, 0, 6)
+        turn_back(0, 2, 7)
+        turn_back(1, 0, 0)
+        turn_back(0, 4, 1)
+        first_product(0, 6, 2)
+        abs_w(1)
+        pair_back(0, 0, on_vector)
+        pair_back(0, 2, on_scalar)
+        pair_back(1, 0, on_scalar)
+        pair_back(0, 4, on_vector)
+        scale_rows(0, 6)
+        first_product(0, 7, 3)
+        compare(1, 0)
+        quantise_e(0, 0, 4)
+        scale_rows(0, 7)
+        first_product(1, 4, 4)
+        abs_w(2)
+        compare(0, 1)
+        turn_back(1, 2, 5)
+        turn_back(0, 6, 6)
+        scale_rows(1, 4)
+        pair_back(1, 2, on_scalar)
+        first_product(1, 5, 7)
+        interleave(1, 3, on_scalar)
+        compare(1, 1)
+        interleave(0, 2, on_vector)
+        abs_w(3)
+        quantise_e(1, 0, 4)
+        scale_rows(1, 5)
+        interleave(0, 3, on_scalar)
+        second_product(0, 0)
+        compare(2, 0)
+        quantise_x(1, 1)
+        apply_mask(0)
+        first_product(1, 6, 1)
+        pair_back(0, 6, on_scalar)
+        scale_rows(1, 6)
+        second_product(1, 2)
+        quantise_x(0, 1)
+        compare(3, 0)
+        second_product(2, 3)
+        apply_mask_pooled(1)
+        quantise_e(0, 4, 4)
+        apply_mask(2)
+        first_product(1, 7, 4)
+        scale_rows(1, 7)
+        second_product(3, 5)
+        apply_mask(3)
+        store(1)
+        second_product(4, 6)
+        compare(2, 1)
+        compare(3, 1)
+        turn_back(1, 4, 7)
+        turn_back(1, 6, 0)
+        pair_back(1, 4, on_scalar)
+        pair_back(1, 6, on_scalar)
+        apply_mask(4)
+        second_product(5, 1)
+        quantise_e(1, 4, 2)
+        second_product(6, 2)
+        second_product(7, 3)
+        quantise_e(1, 6, 2)
+        apply_mask(5)
+        apply_mask_pooled(6)
+        apply_mask(7)
+        for unit in range(8, 16):
+            second_product(unit, (unit - 4) % BANKS)
+            if unit == 9:
+                apply_mask_pooled(unit)
+            else:
+                apply_mask(unit)
+            if unit in (8, 11):
+                store(unit - 2)

@@ -24,7 +24,7 @@ TILES = T // P
 ROW_TILES = C // P
 HALF = 512
 BANKS = 8
-SPLIT = (0, 3)
+SPLIT = (0, 2, 3)
 
 
 def tile_straight_through_weight_gradient_s9_kernel(
@@ -34,7 +34,7 @@ def tile_straight_through_weight_gradient_s9_kernel(
     with ExitStack() as ctx:
         keep = ctx.enter_context(tc.tile_pool(name="keep", bufs=1))
         stage = ctx.enter_context(tc.tile_pool(name="stage", bufs=3))
-        outs = ctx.enter_context(tc.tile_pool(name="outs", bufs=10))
+        outs = ctx.enter_context(tc.tile_pool(name="outs", bufs=14))
         psum = ctx.enter_context(tc.psum_pool(name="psum", bufs=1))
         ctx.enter_context(tc.manual_schedule())
 
@@ -68,12 +68,10 @@ def tile_straight_through_weight_gradient_s9_kernel(
         scales_v = v_scales.rearrange("g q n -> q g n").bitcast(I32)
 
         def load_delta(i):
-            rows = delta[i * P : (i + 1) * P, :]
-            if i in SPLIT:
-                for b in range(2):
-                    nc.sync.dma_start(out=d_sb[i][b][:], in_=rows[:, b * O // 2 : (b + 1) * O // 2])
-            else:
-                nc.sync.dma_start(out=d_sb[i][:], in_=rows)
+            nc.sync.dma_start(out=d_sb[i][:], in_=delta[i * P : (i + 1) * P, :])
+
+        def load_delta_half(i, b):
+            nc.sync.dma_start(out=d_sb[i][b][:], in_=delta[i * P : (i + 1) * P, b * O // 2 : (b + 1) * O // 2])
 
         def load_v_scales(h):
             for s in range(4):
@@ -97,11 +95,6 @@ def tile_straight_through_weight_gradient_s9_kernel(
         d_codes = [keep.tile([P, PASSES * 512], U32, name=f"d_codes{g}", align_bytes=64) for g in range(GROUPS)]
         d_scales = [keep.tile([P, PASSES * 512], U8, name=f"d_scales{g}", align_bytes=64) for g in range(GROUPS)]
 
-        d_grp = [keep.tile([P, PASSES, 4, P, 4], BF16, name=f"d_grp{g}", align_bytes=64) for g in range(GROUPS)]
-
-        def d_cols(i, k, n=1):
-            first = 512 * k + P * (i % 4)
-            return slice(first, first + n * P)
 
         x_grp = [keep.tile([P, C, 4], BF16, name=f"x_grp{g}", align_bytes=64) for g in range(GROUPS)]
         x_codes = [keep.tile([P, C], U32, name=f"x_codes{g}", align_bytes=64) for g in range(GROUPS)]
@@ -114,14 +107,14 @@ def tile_straight_through_weight_gradient_s9_kernel(
             return psum.tile([P, 512], F32, name=f"bank{n}", tag=f"bank{n}")
 
         z_bank, e_rows, b_bank = {}, {}, {}
-        d_sorted, o_bank, res = {}, {}, {}
+        d_sorted, t_bank, d_words, o_bank, res = {}, {}, {}, {}, {}
 
         def spread_r(n):
             ps = bank(n)
             words = r_col[:].bitcast(F32)
             for c in range(4):
                 nc.tensor.transpose(ps[:, c::4], words[:, c : c + 1].to_broadcast([P, P]), ident[:])
-            nc.scalar.copy(out=r_all[:].bitcast(F32), in_=ps[:])
+            nc.vector.tensor_copy(out=r_all[:].bitcast(F32), in_=ps[:])
 
         def sort_words(i, copy):
             d_sorted[i] = stage.tile([P, O // 2], F32, name="d_sorted", bufs=4)
@@ -130,34 +123,34 @@ def tile_straight_through_weight_gradient_s9_kernel(
                 in_=d_sb[i][:].bitcast(F32).rearrange("p (g m i u) -> p g m u i", g=PASSES, u=2, i=2),
             )
 
-        def turn_half(i, b, n, copy=nc.scalar.copy):
-            ps = bank(n)
-            for q in range(4):
-                k, u = q // 2, q % 2
+        def turn(i, k, n=None):
+            if i % 2 == 0:
+                t_bank[(i // 2, k)] = bank(n)
+            for u in range(2):
                 if i in SPLIT:
-                    src = d_sb[i][b][:].bitcast(F32)[:, 256 * k + u : 256 * (k + 1) : 2]
+                    src = d_sb[i][k // 2][:].bitcast(F32)[:, 256 * (k % 2) + u : 256 * (k % 2 + 1) : 2]
                 elif i in d_sorted:
-                    src = d_sorted[i][:, (4 * b + q) * P : (4 * b + q + 1) * P]
+                    src = d_sorted[i][:, (2 * k + u) * P : (2 * k + u + 1) * P]
                 else:
-                    src = d_sb[i][:].bitcast(F32)[:, 256 * (2 * b + k) + u : 256 * (2 * b + k + 1) : 2]
-                nc.tensor.transpose(ps[:, q * P : (q + 1) * P], src, ident[:])
-            words = d_grp[i // 4][:, 2 * b : 2 * b + 2, i % 4, :, :].rearrange("p k m t -> p k (m t)").bitcast(F32)
+                    src = d_sb[i][:].bitcast(F32)[:, 256 * k + u : 256 * (k + 1) : 2]
+                first = (2 * (i % 2) + u) * P
+                nc.tensor.transpose(t_bank[(i // 2, k)][:, first : first + P], src, ident[:])
+
+        def pair_words(pair, k, copy):
+            d_words[(pair, k)] = stage.tile([P, 2 * P, 4], BF16, name="d_words", bufs=8, align_bytes=64)
+            words = d_words[(pair, k)][:].rearrange("p m t -> p (m t)").bitcast(F32)
             copy(
-                out=words.rearrange("p k (m u) -> p k m u", u=2),
-                in_=ps[:].rearrange("p (k u m) -> p k m u", k=2, u=2),
+                out=words.rearrange("p (e m u) -> p e m u", e=2, u=2),
+                in_=t_bank[(pair, k)][:].rearrange("p (e u m) -> p e m u", e=2, u=2),
             )
 
-        def turn(i, n):
-            for b in range(2):
-                turn_half(i, b, n + b)
-
-        def quantise_delta(i, n=1, passes=range(PASSES)):
-            for k in passes:
-                nc.vector.quantize_mx(
-                    out=d_codes[i // 4][:, d_cols(i, k, n)].bitcast(E4M3),
-                    scales=d_scales[i // 4][:, d_cols(i, k, n)],
-                    in_=d_grp[i // 4][:, k, i % 4 : i % 4 + n, :, :].rearrange("p t m j -> p (t m j)"),
-                )
+        def quantise_delta(pair, k):
+            cols = slice(512 * k + 256 * (pair % 2), 512 * k + 256 * (pair % 2 + 1))
+            nc.vector.quantize_mx(
+                out=d_codes[pair // 2][:, cols].bitcast(E4M3),
+                scales=d_scales[pair // 2][:, cols],
+                in_=d_words[(pair, k)][:].rearrange("p m t -> p (m t)"),
+            )
 
         def first_pass(g, fc, k):
             h, n0 = fc // 4, P * (fc % 4)
@@ -177,7 +170,7 @@ def tile_straight_through_weight_gradient_s9_kernel(
                 first_pass(g, fc, k)
 
         def scale_rows(g, fc):
-            e_rows[(g, fc)] = stage.tile([P, 2, P, 2], BF16, name="e_rows", bufs=10)
+            e_rows[(g, fc)] = stage.tile([P, 2, P, 2], BF16, name="e_rows", bufs=12)
             nc.scalar.activation(
                 out=e_rows[(g, fc)][:],
                 in_=z_bank[(g, fc)][:].rearrange("p (m u e) -> p u m e", u=2, e=2),
@@ -253,19 +246,23 @@ def tile_straight_through_weight_gradient_s9_kernel(
                 op=OP.is_le,
             )
 
-        def second_product(unit, n):
+        def second_pass(unit, g, n=None):
             h, ct = unit // ROW_TILES, unit % ROW_TILES
-            o_bank[unit] = bank(n)
-            for g in range(GROUPS):
-                nc.tensor.matmul_mx(
-                    out=o_bank[unit][:],
-                    lhsT=x_codes[g][:, ct * P : (ct + 1) * P].bitcast(E4M3),
-                    lhsT_scale=x_scales[g][:, ct * P : (ct + 1) * P],
-                    rhs=e_codes[g][:, h * HALF : (h + 1) * HALF].bitcast(E5M2),
-                    rhs_scale=e_scales[g][:, h * HALF : (h + 1) * HALF],
-                    start=(g == 0),
-                    stop=(g == GROUPS - 1),
-                )
+            if g == 0:
+                o_bank[unit] = bank(n)
+            nc.tensor.matmul_mx(
+                out=o_bank[unit][:],
+                lhsT=x_codes[g][:, ct * P : (ct + 1) * P].bitcast(E4M3),
+                lhsT_scale=x_scales[g][:, ct * P : (ct + 1) * P],
+                rhs=e_codes[g][:, h * HALF : (h + 1) * HALF].bitcast(E5M2),
+                rhs_scale=e_scales[g][:, h * HALF : (h + 1) * HALF],
+                start=(g == 0),
+                stop=(g == GROUPS - 1),
+            )
+
+        def second_product(unit, n):
+            second_pass(unit, 0, n)
+            second_pass(unit, 1)
 
         def store(unit):
             h, ct = unit // ROW_TILES, unit % ROW_TILES
@@ -291,14 +288,20 @@ def tile_straight_through_weight_gradient_s9_kernel(
         nc.scalar.dma_start(out=gain_rows[:], in_=gain.rearrange("(c p) -> c p", p=P))
         nc.gpsimd.dma_start(out=lo_sb[:], in_=lo.rearrange("(g p j) -> p g j", p=P, j=4))
         nc.gpsimd.dma_start(out=hi_sb[:], in_=hi.rearrange("(g p j) -> p g j", p=P, j=4))
-        for i in range(4):
-            load_delta(i)
+        load_delta_half(0, 0)
+        load_delta_half(0, 1)
+        load_delta(1)
+        for b in range(2):
+            load_delta_half(2, b)
+            load_delta_half(3, b)
         load_v_scales(0)
         load_v_codes(0, 0)
         load_v_codes(0, 1)
+        load_delta(4)
+        load_delta(5)
         load_x(0, 0)
-        for i in range(4, TILES):
-            load_delta(i)
+        load_delta(6)
+        load_delta(7)
         load_v_scales(1)
         load_v_codes(1, 0)
         load_v_codes(1, 1)
@@ -311,135 +314,150 @@ def tile_straight_through_weight_gradient_s9_kernel(
         load_w(3)
 
         nc.scalar.activation(out=gain_pad[:], in_=ident[:], func=ACT.Copy, scale=0.0)
-        spread_r(7)
         nc.vector.tensor_copy(out=gain_pad[0 : F // P, :], in_=gain_rows[:])
-        turn(0, 0)
-        turn(1, 2)
-        quantise_delta(0, 2)
-        turn_half(2, 0, 0)
-        quantise_delta(2, 1, (0, 1))
-        turn_half(3, 0, 1)
-        quantise_delta(3, 1, (0, 1))
-        turn_half(2, 1, 2)
-        turn_half(3, 1, 3)
-        gain_to_partitions(0)
-        quantise_delta(2, 2, (2, 3))
+        for k in range(PASSES):
+            turn(0, k, k)
+        gain_to_partitions(6)
+        for k in range(PASSES):
+            turn(1, k)
+            pair_words(0, k, on_vector if k % 2 else on_scalar)
+        for b in range(2):
+            for i in (2, 3):
+                for k in (2 * b, 2 * b + 1):
+                    turn(i, k, 4 + k)
+        for k in range(PASSES):
+            pair_words(1, k, on_scalar)
+        for k in range(PASSES):
+            quantise_delta(0, k)
+            quantise_delta(1, k)
+        spread_r(3)
         for fc in range(4):
-            z_bank[(0, fc)] = bank(4 + fc)
+            z_bank[(0, fc)] = bank((0, 1, 2, 4)[fc])
         for k in range(2):
             for fc in range(4):
                 first_pass(0, fc, k)
-        clip(0, 0)
         sort_words(4, on_scalar)
-        interleave(0, 0, on_vector)
-        interleave(0, 1, on_vector)
         sort_words(5, on_vector)
-        quantise_x(0, 0)
-        sort_words(6, on_vector)
-        sort_words(7, on_vector)
-        for fc in range(4):
+        for fc in range(2):
             for k in range(2, PASSES):
                 first_pass(0, fc, k)
             scale_rows(0, fc)
-        turn(4, 0)
-        turn_half(5, 0, 2)
-        turn_half(5, 1, 3, on_vector)
-        turn_half(6, 0, 4)
-        turn_half(6, 1, 5, on_vector)
-        quantise_delta(4, 2)
-        turn(7, 6)
-        quantise_delta(6, 2)
-        first_product(0, 4, 0)
-        first_product(0, 5, 1)
+        clip(0, 0)
+        for k in range(PASSES):
+            turn(4, k, (5, 6, 7, 3)[k])
+            turn(5, k)
+            pair_words(2, k, on_scalar)
+        sort_words(6, on_vector)
+        interleave(0, 0, on_vector)
+        interleave(0, 1, on_vector)
+        for fc in range(2, 4):
+            for k in range(2, PASSES):
+                first_pass(0, fc, k)
+            scale_rows(0, fc)
+        for k in range(PASSES):
+            quantise_delta(2, k)
+        for i in (6, 7):
+            for k in range(PASSES):
+                turn(i, k, (0, 1, 5, 6)[k])
+        quantise_x(0, 0)
+        for k in range(PASSES):
+            pair_words(3, k, on_vector if k == 1 else on_scalar)
+        for k in range(PASSES):
+            quantise_delta(3, k)
+        first_product(0, 4, 7)
+        first_product(0, 5, 3)
         scale_rows(0, 4)
         first_product(1, 0, 2)
         scale_rows(0, 5)
         clip(1, 0)
         clip(1, 1)
-        scale_rows(1, 0)
-        first_product(1, 1, 3)
+        first_product(1, 1, 4)
         interleave(1, 0, on_scalar)
-        scale_rows(1, 1)
+        scale_rows(1, 0)
         abs_w(0)
         interleave(1, 1, on_vector)
-        first_product(1, 2, 4)
+        scale_rows(1, 1)
+        first_product(1, 2, 0)
         clip(0, 1)
         scale_rows(1, 2)
         compare(0, 0)
-        first_product(1, 3, 5)
+        first_product(1, 3, 1)
         interleave(1, 2, on_scalar)
         scale_rows(1, 3)
         quantise_x(1, 0)
-        turn_back(0, 0, 6)
-        turn_back(0, 2, 7)
-        turn_back(1, 0, 0)
-        turn_back(0, 4, 1)
         first_product(0, 6, 2)
         abs_w(1)
+        turn_back(0, 0, 5)
+        turn_back(0, 2, 6)
+        turn_back(1, 0, 7)
+        turn_back(1, 2, 3)
+        turn_back(0, 4, 4)
+        compare(1, 0)
+        abs_w(2)
+        scale_rows(0, 6)
         pair_back(0, 0, on_vector)
         pair_back(0, 2, on_scalar)
         pair_back(1, 0, on_scalar)
-        pair_back(0, 4, on_vector)
-        scale_rows(0, 6)
-        first_product(0, 7, 3)
-        compare(1, 0)
+        pair_back(1, 2, on_scalar)
+        pair_back(0, 4, on_scalar)
+        first_product(0, 7, 0)
+        compare(0, 1)
         quantise_e(0, 0, 4)
         scale_rows(0, 7)
-        first_product(1, 4, 4)
-        abs_w(2)
-        compare(0, 1)
-        turn_back(1, 2, 5)
-        turn_back(0, 6, 6)
-        scale_rows(1, 4)
-        pair_back(1, 2, on_scalar)
-        first_product(1, 5, 7)
-        interleave(1, 3, on_scalar)
-        compare(1, 1)
-        interleave(0, 2, on_vector)
+        first_product(1, 4, 1)
         abs_w(3)
         quantise_e(1, 0, 4)
-        scale_rows(1, 5)
-        interleave(0, 3, on_scalar)
-        second_product(0, 0)
+        interleave(1, 3, on_scalar)
+        scale_rows(1, 4)
+        compare(1, 1)
+        second_product(0, 2)
         compare(2, 0)
-        quantise_x(1, 1)
         apply_mask(0)
-        first_product(1, 6, 1)
-        pair_back(0, 6, on_scalar)
-        scale_rows(1, 6)
-        second_product(1, 2)
-        quantise_x(0, 1)
+        first_product(1, 5, 5)
+        interleave(0, 2, on_scalar)
+        scale_rows(1, 5)
+        quantise_x(1, 1)
+        second_product(1, 6)
         compare(3, 0)
-        second_product(2, 3)
-        apply_mask_pooled(1)
-        quantise_e(0, 4, 4)
-        apply_mask(2)
-        first_product(1, 7, 4)
-        scale_rows(1, 7)
-        second_product(3, 5)
-        apply_mask(3)
-        store(1)
-        second_product(4, 6)
+        apply_mask(1)
+        first_product(1, 6, 7)
+        interleave(0, 3, on_scalar)
         compare(2, 1)
-        compare(3, 1)
-        turn_back(1, 4, 7)
-        turn_back(1, 6, 0)
+        second_product(2, 3)
+        quantise_e(0, 4, 2)
+        apply_mask(2)
+        turn_back(0, 6, 4)
+        turn_back(1, 4, 0)
+        scale_rows(1, 6)
+        second_product(3, 2)
+        first_product(1, 7, 1)
+        quantise_x(0, 1)
+        pair_back(0, 6, on_scalar)
         pair_back(1, 4, on_scalar)
-        pair_back(1, 6, on_scalar)
-        apply_mask(4)
-        second_product(5, 1)
+        compare(3, 1)
+        apply_mask(3)
+        scale_rows(1, 7)
+        quantise_e(0, 6, 2)
         quantise_e(1, 4, 2)
-        second_product(6, 2)
-        second_product(7, 3)
-        quantise_e(1, 6, 2)
+        second_product(4, 5)
+        second_product(5, 6)
+        apply_mask(4)
+        turn_back(1, 6, 7, 1)
+        turn_back(1, 7, 3, 1)
+        pair_back(1, 7, on_scalar, 1)
         apply_mask(5)
-        apply_mask_pooled(6)
+        pair_back(1, 6, on_vector, 1)
+        second_product(6, 4)
+        second_product(7, 0)
+        quantise_e(1, 6, 2)
+        apply_mask(6)
         apply_mask(7)
-        for unit in range(8, 16):
-            second_product(unit, (unit - 4) % BANKS)
-            if unit == 9:
-                apply_mask_pooled(unit)
-            else:
-                apply_mask(unit)
-            if unit in (8, 11):
-                store(unit - 2)
+        second_pass(8, 0, 2)
+        second_pass(9, 0, 1)
+        second_pass(8, 1)
+        second_pass(9, 1)
+        apply_mask(8)
+        apply_mask(9)
+        for unit in range(10, 16):
+            second_product(unit, (5, 6, 7, 3, 4, 0)[unit - 10])
+            apply_mask(unit)

@@ -58,8 +58,7 @@ def tile_straight_through_weight_gradient_s9_kernel(
             for i in range(TILES)
         ]
         v_codes = [[keep.tile([P, 2, F], U8, name=f"v_codes{h}_{b}", align_bytes=64) for b in range(2)] for h in range(2)]
-        x_first = [keep.tile([P, 4, HALF], BF16, name=f"x_first{a}") for a in range(2)]
-        x_late = keep.tile([P, 4, C], BF16, name="x_late")
+        x_sb = [keep.tile([P, 4, C], BF16, name=f"x_sb{g}") for g in range(GROUPS)]
         w_sb = [keep.tile([P, 2, F], BF16, name=f"w_sb{a}") for a in range(ROW_TILES // 2)]
 
         x_v = x.rearrange("(g p j) c -> g p j c", p=P, j=4)
@@ -84,10 +83,7 @@ def tile_straight_through_weight_gradient_s9_kernel(
             nc.sync.dma_start(out=v_codes[h][b][:], in_=words_v[:, 2 * b : 2 * b + 2, h * F : (h + 1) * F])
 
         def load_x(g, a):
-            if g == 0:
-                nc.sync.dma_start(out=x_first[a][:], in_=x_v[0, :, :, a * HALF : (a + 1) * HALF])
-            else:
-                nc.sync.dma_start(out=x_late[:, 2 * a : 2 * a + 2, :], in_=x_v[1, :, 2 * a : 2 * a + 2, :])
+            nc.sync.dma_start(out=x_sb[g][:, 2 * a : 2 * a + 2, :], in_=x_v[g, :, 2 * a : 2 * a + 2, :])
 
         def load_w(a):
             nc.sync.dma_start(out=w_sb[a][:], in_=w_v[:, 2 * a : 2 * a + 2, :])
@@ -114,10 +110,10 @@ def tile_straight_through_weight_gradient_s9_kernel(
             words = r_col[:].bitcast(F32)
             for c in range(4):
                 nc.tensor.transpose(ps[:, c::4], words[:, c : c + 1].to_broadcast([P, P]), ident[:])
-            nc.vector.tensor_copy(out=r_all[:].bitcast(F32), in_=ps[:])
+            nc.scalar.copy(out=r_all[:].bitcast(F32), in_=ps[:])
 
         def sort_words(i, copy):
-            d_sorted[i] = stage.tile([P, O // 2], F32, name="d_sorted", bufs=4)
+            d_sorted[i] = stage.tile([P, O // 2], F32, name="d_sorted")
             copy(
                 out=d_sorted[i][:].rearrange("p (g u m i) -> p g m u i", g=PASSES, u=2, i=2),
                 in_=d_sb[i][:].bitcast(F32).rearrange("p (g m i u) -> p g m u i", g=PASSES, u=2, i=2),
@@ -137,19 +133,21 @@ def tile_straight_through_weight_gradient_s9_kernel(
                 nc.tensor.transpose(t_bank[(i // 2, k)][:, first : first + P], src, ident[:])
 
         def pair_words(pair, k, copy):
-            d_words[(pair, k)] = stage.tile([P, 2 * P, 4], BF16, name="d_words", bufs=8, align_bytes=64)
-            words = d_words[(pair, k)][:].rearrange("p m t -> p (m t)").bitcast(F32)
+            g, first = pair // 2, 2 * P * (pair % 2)
+            if pair % 2 == 0:
+                d_words[(g, k)] = stage.tile([P, 512, 4], BF16, name="d_words", bufs=6, align_bytes=64)
+            words = d_words[(g, k)][:, first : first + 2 * P, :].rearrange("p m t -> p (m t)").bitcast(F32)
             copy(
                 out=words.rearrange("p (e m u) -> p e m u", e=2, u=2),
                 in_=t_bank[(pair, k)][:].rearrange("p (e u m) -> p e m u", e=2, u=2),
             )
 
-        def quantise_delta(pair, k):
-            cols = slice(512 * k + 256 * (pair % 2), 512 * k + 256 * (pair % 2 + 1))
+        def quantise_delta(g, k, first=0, count=512):
+            cols = slice(512 * k + first, 512 * k + first + count)
             nc.vector.quantize_mx(
-                out=d_codes[pair // 2][:, cols].bitcast(E4M3),
-                scales=d_scales[pair // 2][:, cols],
-                in_=d_words[(pair, k)][:].rearrange("p m t -> p (m t)"),
+                out=d_codes[g][:, cols].bitcast(E4M3),
+                scales=d_scales[g][:, cols],
+                in_=d_words[(g, k)][:, first : first + count, :].rearrange("p m t -> p (m t)"),
             )
 
         def first_pass(g, fc, k):
@@ -206,27 +204,25 @@ def tile_straight_through_weight_gradient_s9_kernel(
             )
 
         def clip(g, a):
-            for j in range(4) if g == 0 else (2 * a, 2 * a + 1):
-                row = x_first[a][:, j, :] if g == 0 else x_late[:, j, :]
+            for j in (2 * a, 2 * a + 1):
                 nc.vector.tensor_scalar(
-                    out=row,
-                    in0=row,
+                    out=x_sb[g][:, j, :],
+                    in0=x_sb[g][:, j, :],
                     scalar1=lo_sb[:, g, j : j + 1],
                     scalar2=hi_sb[:, g, j : j + 1],
                     op0=OP.max,
                     op1=OP.min,
                 )
 
-        def interleave(g, k, copy):
-            cols = slice(256 * k, 256 * (k + 1))
-            rows = x_first[k // 2][:, :, 256 * (k % 2) : 256 * (k % 2 + 1)] if g == 0 else x_late[:, :, cols]
+        def interleave(g, k, copy, count=1):
+            cols = slice(256 * k, 256 * (k + count))
             copy(
                 out=x_grp[g][:, cols, :].rearrange("p (c i) j -> p c j i", i=4),
-                in_=rows.rearrange("p j (c i) -> p c j i", i=4),
+                in_=x_sb[g][:, :, cols].rearrange("p j (c i) -> p c j i", i=4),
             )
 
-        def quantise_x(g, k):
-            cols = slice(512 * k, 512 * (k + 1))
+        def quantise_x(g, k, count=1):
+            cols = slice(512 * k, 512 * (k + count))
             nc.vector.quantize_mx(
                 out=x_codes[g][:, cols].bitcast(E4M3),
                 scales=x_scales[g][:, cols],
@@ -237,12 +233,11 @@ def tile_straight_through_weight_gradient_s9_kernel(
             bits = w_sb[a][:].rearrange("p c f -> p (c f)").bitcast(I32)
             nc.vector.tensor_scalar(out=bits, in0=bits, scalar1=0x7FFF7FFF, scalar2=None, op0=OP.bitwise_and)
 
-        def compare(a, h):
-            cols = slice(h * HALF, (h + 1) * HALF)
+        def compare(a):
             nc.vector.tensor_tensor(
-                out=w_sb[a][:, :, cols],
-                in0=w_sb[a][:, :, cols],
-                in1=r_all[:, cols].unsqueeze(1).to_broadcast([P, 2, HALF]),
+                out=w_sb[a][:],
+                in0=w_sb[a][:],
+                in1=r_all[:].unsqueeze(1).to_broadcast([P, 2, F]),
                 op=OP.is_le,
             )
 
@@ -284,8 +279,8 @@ def tile_straight_through_weight_gradient_s9_kernel(
 
         on_vector, on_scalar = nc.vector.tensor_copy, nc.scalar.copy
 
-        nc.scalar.dma_start(out=r_col[:], in_=r.rearrange("(p c) -> p c", p=P))
         nc.scalar.dma_start(out=gain_rows[:], in_=gain.rearrange("(c p) -> c p", p=P))
+        nc.scalar.dma_start(out=r_col[:], in_=r.rearrange("(p c) -> p c", p=P))
         nc.gpsimd.dma_start(out=lo_sb[:], in_=lo.rearrange("(g p j) -> p g j", p=P, j=4))
         nc.gpsimd.dma_start(out=hi_sb[:], in_=hi.rearrange("(g p j) -> p g j", p=P, j=4))
         load_delta_half(0, 0)
@@ -300,6 +295,7 @@ def tile_straight_through_weight_gradient_s9_kernel(
         load_delta(4)
         load_delta(5)
         load_x(0, 0)
+        load_x(0, 1)
         load_delta(6)
         load_delta(7)
         load_v_scales(1)
@@ -307,11 +303,8 @@ def tile_straight_through_weight_gradient_s9_kernel(
         load_v_codes(1, 1)
         load_x(1, 0)
         load_x(1, 1)
-        load_w(0)
-        load_x(0, 1)
-        load_w(1)
-        load_w(2)
-        load_w(3)
+        for a in range(4):
+            load_w(a)
 
         nc.scalar.activation(out=gain_pad[:], in_=ident[:], func=ACT.Copy, scale=0.0)
         nc.vector.tensor_copy(out=gain_pad[0 : F // P, :], in_=gain_rows[:])
@@ -329,7 +322,6 @@ def tile_straight_through_weight_gradient_s9_kernel(
             pair_words(1, k, on_scalar)
         for k in range(PASSES):
             quantise_delta(0, k)
-            quantise_delta(1, k)
         spread_r(3)
         for fc in range(4):
             z_bank[(0, fc)] = bank((0, 1, 2, 4)[fc])
@@ -338,126 +330,126 @@ def tile_straight_through_weight_gradient_s9_kernel(
                 first_pass(0, fc, k)
         sort_words(4, on_scalar)
         sort_words(5, on_vector)
+        clip(0, 0)
         for fc in range(2):
             for k in range(2, PASSES):
                 first_pass(0, fc, k)
             scale_rows(0, fc)
-        clip(0, 0)
+        clip(0, 1)
         for k in range(PASSES):
             turn(4, k, (5, 6, 7, 3)[k])
             turn(5, k)
             pair_words(2, k, on_scalar)
         sort_words(6, on_vector)
-        interleave(0, 0, on_vector)
-        interleave(0, 1, on_vector)
+        interleave(0, 0, on_vector, 2)
         for fc in range(2, 4):
             for k in range(2, PASSES):
                 first_pass(0, fc, k)
             scale_rows(0, fc)
         for k in range(PASSES):
-            quantise_delta(2, k)
+            quantise_delta(1, k, 0, 256)
+        interleave(0, 2, on_vector)
         for i in (6, 7):
             for k in range(PASSES):
                 turn(i, k, (0, 1, 5, 6)[k])
-        quantise_x(0, 0)
         for k in range(PASSES):
-            pair_words(3, k, on_vector if k == 1 else on_scalar)
+            pair_words(3, k, on_scalar)
         for k in range(PASSES):
-            quantise_delta(3, k)
+            quantise_delta(1, k, 256, 256)
         first_product(0, 4, 7)
         first_product(0, 5, 3)
         scale_rows(0, 4)
         first_product(1, 0, 2)
         scale_rows(0, 5)
+        interleave(0, 3, on_scalar)
         clip(1, 0)
         clip(1, 1)
         first_product(1, 1, 4)
-        interleave(1, 0, on_scalar)
         scale_rows(1, 0)
-        abs_w(0)
-        interleave(1, 1, on_vector)
+        interleave(1, 0, on_scalar)
+        quantise_x(0, 0, 2)
         scale_rows(1, 1)
         first_product(1, 2, 0)
-        clip(0, 1)
+        abs_w(0)
+        interleave(1, 1, on_scalar)
         scale_rows(1, 2)
-        compare(0, 0)
         first_product(1, 3, 1)
-        interleave(1, 2, on_scalar)
-        scale_rows(1, 3)
-        quantise_x(1, 0)
-        first_product(0, 6, 2)
         abs_w(1)
+        compare(0)
+        scale_rows(1, 3)
+        first_product(0, 6, 2)
+        quantise_x(1, 0)
         turn_back(0, 0, 5)
         turn_back(0, 2, 6)
         turn_back(1, 0, 7)
-        turn_back(1, 2, 3)
         turn_back(0, 4, 4)
-        compare(1, 0)
-        abs_w(2)
+        turn_back(1, 2, 3)
+        compare(1)
         scale_rows(0, 6)
-        pair_back(0, 0, on_vector)
+        pair_back(0, 0, on_scalar)
         pair_back(0, 2, on_scalar)
         pair_back(1, 0, on_scalar)
         pair_back(1, 2, on_scalar)
-        pair_back(0, 4, on_scalar)
         first_product(0, 7, 0)
-        compare(0, 1)
+        abs_w(2)
+        abs_w(3)
         quantise_e(0, 0, 4)
         scale_rows(0, 7)
         first_product(1, 4, 1)
-        abs_w(3)
         quantise_e(1, 0, 4)
-        interleave(1, 3, on_scalar)
+        pair_back(0, 4, on_scalar)
         scale_rows(1, 4)
-        compare(1, 1)
-        second_product(0, 2)
-        compare(2, 0)
-        apply_mask(0)
+        compare(2)
         first_product(1, 5, 5)
-        interleave(0, 2, on_scalar)
+        interleave(1, 2, on_scalar)
+        second_product(0, 2)
         scale_rows(1, 5)
-        quantise_x(1, 1)
+        apply_mask(0)
         second_product(1, 6)
-        compare(3, 0)
+        interleave(1, 3, on_scalar)
+        compare(3)
         apply_mask(1)
         first_product(1, 6, 7)
-        interleave(0, 3, on_scalar)
-        compare(2, 1)
         second_product(2, 3)
         quantise_e(0, 4, 2)
         apply_mask(2)
         turn_back(0, 6, 4)
         turn_back(1, 4, 0)
         scale_rows(1, 6)
-        second_product(3, 2)
-        first_product(1, 7, 1)
-        quantise_x(0, 1)
+        second_product(3, 1)
+        first_product(1, 7, 5)
+        quantise_x(1, 1)
         pair_back(0, 6, on_scalar)
         pair_back(1, 4, on_scalar)
-        compare(3, 1)
         apply_mask(3)
         scale_rows(1, 7)
         quantise_e(0, 6, 2)
         quantise_e(1, 4, 2)
-        second_product(4, 5)
+        second_product(4, 2)
         second_product(5, 6)
         apply_mask(4)
         turn_back(1, 6, 7, 1)
         turn_back(1, 7, 3, 1)
+        pair_back(1, 6, on_scalar, 1)
         pair_back(1, 7, on_scalar, 1)
         apply_mask(5)
-        pair_back(1, 6, on_vector, 1)
         second_product(6, 4)
         second_product(7, 0)
         quantise_e(1, 6, 2)
         apply_mask(6)
-        apply_mask(7)
-        second_pass(8, 0, 2)
-        second_pass(9, 0, 1)
+        apply_mask_pooled(7)
+        second_pass(8, 0, 1)
+        second_pass(9, 0, 5)
         second_pass(8, 1)
         second_pass(9, 1)
         apply_mask(8)
         apply_mask(9)
+        store(7)
         for unit in range(10, 16):
-            second_product(unit, (5, 6, 7, 3, 4, 0)[unit - 10])
-            apply_mask(unit)
+            second_product(unit, (2, 6, 7, 3, 4, 0)[unit - 10])
+            if unit == 11:
+                apply_mask_pooled(unit)
+            else:
+                apply_mask(unit)
+            if unit == 13:
+                store(11)

@@ -58,7 +58,8 @@ def tile_straight_through_weight_gradient_s9_kernel(
             for i in range(TILES)
         ]
         v_codes = [[keep.tile([P, 2, F], U8, name=f"v_codes{h}_{b}", align_bytes=64) for b in range(2)] for h in range(2)]
-        x_sb = [keep.tile([P, 4, C], BF16, name=f"x_sb{g}") for g in range(GROUPS)]
+        x_first = [keep.tile([P, 4, HALF], BF16, name=f"x_first{a}") for a in range(2)]
+        x_late = keep.tile([P, 4, C], BF16, name="x_late")
         w_sb = [keep.tile([P, 2, F], BF16, name=f"w_sb{a}") for a in range(ROW_TILES // 2)]
 
         x_v = x.rearrange("(g p j) c -> g p j c", p=P, j=4)
@@ -83,7 +84,10 @@ def tile_straight_through_weight_gradient_s9_kernel(
             nc.sync.dma_start(out=v_codes[h][b][:], in_=words_v[:, 2 * b : 2 * b + 2, h * F : (h + 1) * F])
 
         def load_x(g, a):
-            nc.sync.dma_start(out=x_sb[g][:, 2 * a : 2 * a + 2, :], in_=x_v[g, :, 2 * a : 2 * a + 2, :])
+            if g == 0:
+                nc.sync.dma_start(out=x_first[a][:], in_=x_v[0, :, :, a * HALF : (a + 1) * HALF])
+            else:
+                nc.sync.dma_start(out=x_late[:, 2 * a : 2 * a + 2, :], in_=x_v[1, :, 2 * a : 2 * a + 2, :])
 
         def load_w(a):
             nc.sync.dma_start(out=w_sb[a][:], in_=w_v[:, 2 * a : 2 * a + 2, :])
@@ -110,7 +114,7 @@ def tile_straight_through_weight_gradient_s9_kernel(
             words = r_col[:].bitcast(F32)
             for c in range(4):
                 nc.tensor.transpose(ps[:, c::4], words[:, c : c + 1].to_broadcast([P, P]), ident[:])
-            nc.scalar.copy(out=r_all[:].bitcast(F32), in_=ps[:])
+            nc.vector.tensor_copy(out=r_all[:].bitcast(F32), in_=ps[:])
 
         def sort_words(i, copy):
             d_sorted[i] = stage.tile([P, O // 2], F32, name="d_sorted")
@@ -135,7 +139,7 @@ def tile_straight_through_weight_gradient_s9_kernel(
         def pair_words(pair, k, copy):
             g, first = pair // 2, 2 * P * (pair % 2)
             if pair % 2 == 0:
-                d_words[(g, k)] = stage.tile([P, 512, 4], BF16, name="d_words", bufs=6, align_bytes=64)
+                d_words[(g, k)] = stage.tile([P, 512, 4], BF16, name="d_words", bufs=5, align_bytes=64)
             words = d_words[(g, k)][:, first : first + 2 * P, :].rearrange("p m t -> p (m t)").bitcast(F32)
             copy(
                 out=words.rearrange("p (e m u) -> p e m u", e=2, u=2),
@@ -168,7 +172,7 @@ def tile_straight_through_weight_gradient_s9_kernel(
                 first_pass(g, fc, k)
 
         def scale_rows(g, fc):
-            e_rows[(g, fc)] = stage.tile([P, 2, P, 2], BF16, name="e_rows", bufs=12)
+            e_rows[(g, fc)] = stage.tile([P, 2, P, 2], BF16, name="e_rows", bufs=13)
             nc.scalar.activation(
                 out=e_rows[(g, fc)][:],
                 in_=z_bank[(g, fc)][:].rearrange("p (m u e) -> p u m e", u=2, e=2),
@@ -204,10 +208,11 @@ def tile_straight_through_weight_gradient_s9_kernel(
             )
 
         def clip(g, a):
-            for j in (2 * a, 2 * a + 1):
+            for j in range(4) if g == 0 else (2 * a, 2 * a + 1):
+                row = x_first[a][:, j, :] if g == 0 else x_late[:, j, :]
                 nc.vector.tensor_scalar(
-                    out=x_sb[g][:, j, :],
-                    in0=x_sb[g][:, j, :],
+                    out=row,
+                    in0=row,
                     scalar1=lo_sb[:, g, j : j + 1],
                     scalar2=hi_sb[:, g, j : j + 1],
                     op0=OP.max,
@@ -216,9 +221,10 @@ def tile_straight_through_weight_gradient_s9_kernel(
 
         def interleave(g, k, copy, count=1):
             cols = slice(256 * k, 256 * (k + count))
+            rows = x_first[k // 2][:, :, 256 * (k % 2) : 256 * (k % 2 + count)] if g == 0 else x_late[:, :, cols]
             copy(
                 out=x_grp[g][:, cols, :].rearrange("p (c i) j -> p c j i", i=4),
-                in_=x_sb[g][:, :, cols].rearrange("p j (c i) -> p c j i", i=4),
+                in_=rows.rearrange("p j (c i) -> p c j i", i=4),
             )
 
         def quantise_x(g, k, count=1):
@@ -279,8 +285,8 @@ def tile_straight_through_weight_gradient_s9_kernel(
 
         on_vector, on_scalar = nc.vector.tensor_copy, nc.scalar.copy
 
-        nc.scalar.dma_start(out=gain_rows[:], in_=gain.rearrange("(c p) -> c p", p=P))
         nc.scalar.dma_start(out=r_col[:], in_=r.rearrange("(p c) -> p c", p=P))
+        nc.scalar.dma_start(out=gain_rows[:], in_=gain.rearrange("(c p) -> c p", p=P))
         nc.gpsimd.dma_start(out=lo_sb[:], in_=lo.rearrange("(g p j) -> p g j", p=P, j=4))
         nc.gpsimd.dma_start(out=hi_sb[:], in_=hi.rearrange("(g p j) -> p g j", p=P, j=4))
         load_delta_half(0, 0)
@@ -292,22 +298,25 @@ def tile_straight_through_weight_gradient_s9_kernel(
         load_v_scales(0)
         load_v_codes(0, 0)
         load_v_codes(0, 1)
+        load_x(0, 0)
         load_delta(4)
         load_delta(5)
-        load_x(0, 0)
-        load_x(0, 1)
-        load_delta(6)
-        load_delta(7)
         load_v_scales(1)
         load_v_codes(1, 0)
         load_v_codes(1, 1)
+        load_x(0, 1)
+        load_delta(6)
+        load_delta(7)
+        load_w(0)
         load_x(1, 0)
         load_x(1, 1)
-        for a in range(4):
-            load_w(a)
+        load_w(1)
+        load_w(2)
+        load_w(3)
 
         nc.scalar.activation(out=gain_pad[:], in_=ident[:], func=ACT.Copy, scale=0.0)
         nc.vector.tensor_copy(out=gain_pad[0 : F // P, :], in_=gain_rows[:])
+        spread_r(7)
         for k in range(PASSES):
             turn(0, k, k)
         gain_to_partitions(6)
@@ -318,138 +327,127 @@ def tile_straight_through_weight_gradient_s9_kernel(
             for i in (2, 3):
                 for k in (2 * b, 2 * b + 1):
                     turn(i, k, 4 + k)
+        quantise_delta(0, 0, 0, 256)
         for k in range(PASSES):
-            pair_words(1, k, on_scalar)
-        for k in range(PASSES):
+            pair_words(1, k, on_vector if k == 1 else on_scalar)
+        quantise_delta(0, 0, 256, 256)
+        for k in range(1, PASSES):
             quantise_delta(0, k)
-        spread_r(3)
         for fc in range(4):
-            z_bank[(0, fc)] = bank((0, 1, 2, 4)[fc])
+            z_bank[(0, fc)] = bank(fc)
         for k in range(2):
             for fc in range(4):
                 first_pass(0, fc, k)
-        sort_words(4, on_scalar)
-        sort_words(5, on_vector)
         clip(0, 0)
-        for fc in range(2):
-            for k in range(2, PASSES):
-                first_pass(0, fc, k)
-            scale_rows(0, fc)
-        clip(0, 1)
-        for k in range(PASSES):
-            turn(4, k, (5, 6, 7, 3)[k])
-            turn(5, k)
-            pair_words(2, k, on_scalar)
-        sort_words(6, on_vector)
+        sort_words(4, on_scalar)
+        sort_words(5, on_scalar)
         interleave(0, 0, on_vector, 2)
-        for fc in range(2, 4):
+        quantise_x(0, 0)
+        for fc in range(4):
             for k in range(2, PASSES):
                 first_pass(0, fc, k)
             scale_rows(0, fc)
+        for k in range(PASSES):
+            turn(4, k, 4 + k)
+            turn(5, k)
+            pair_words(2, k, on_vector if k < 3 else on_scalar)
+        clip(0, 1)
+        first_product(0, 4, 0)
+        for k in range(PASSES):
+            turn(6, k, (4, 5, 1, 6)[k])
+        interleave(0, 2, on_vector, 2)
+        scale_rows(0, 4)
         for k in range(PASSES):
             quantise_delta(1, k, 0, 256)
-        interleave(0, 2, on_vector)
-        for i in (6, 7):
-            for k in range(PASSES):
-                turn(i, k, (0, 1, 5, 6)[k])
+        first_product(0, 5, 2)
+        scale_rows(0, 5)
+        quantise_x(0, 1)
         for k in range(PASSES):
-            pair_words(3, k, on_scalar)
+            turn(7, k)
+            pair_words(3, k, on_vector if k == 1 else on_scalar)
+        first_product(0, 6, 3)
+        abs_w(0)
         for k in range(PASSES):
             quantise_delta(1, k, 256, 256)
-        first_product(0, 4, 7)
-        first_product(0, 5, 3)
-        scale_rows(0, 4)
-        first_product(1, 0, 2)
-        scale_rows(0, 5)
-        interleave(0, 3, on_scalar)
+        first_product(0, 7, 7)
+        scale_rows(0, 6)
         clip(1, 0)
         clip(1, 1)
+        first_product(1, 0, 0)
+        scale_rows(0, 7)
+        compare(0)
+        interleave(1, 0, on_scalar)
         first_product(1, 1, 4)
         scale_rows(1, 0)
-        interleave(1, 0, on_scalar)
-        quantise_x(0, 0, 2)
-        scale_rows(1, 1)
-        first_product(1, 2, 0)
-        abs_w(0)
-        interleave(1, 1, on_scalar)
-        scale_rows(1, 2)
-        first_product(1, 3, 1)
+        interleave(1, 1, on_vector)
         abs_w(1)
-        compare(0)
-        scale_rows(1, 3)
-        first_product(0, 6, 2)
-        quantise_x(1, 0)
         turn_back(0, 0, 5)
-        turn_back(0, 2, 6)
-        turn_back(1, 0, 7)
-        turn_back(0, 4, 4)
-        turn_back(1, 2, 3)
+        turn_back(0, 2, 1)
+        turn_back(0, 4, 6)
+        turn_back(0, 6, 2)
+        scale_rows(1, 1)
+        first_product(1, 2, 3)
         compare(1)
-        scale_rows(0, 6)
         pair_back(0, 0, on_scalar)
+        quantise_x(1, 0)
+        first_product(1, 3, 7)
         pair_back(0, 2, on_scalar)
+        scale_rows(1, 2)
+        pair_back(0, 4, on_vector)
+        abs_w(2)
+        first_product(1, 4, 0)
+        scale_rows(1, 3)
+        quantise_e(0, 0, 4)
+        compare(2)
+        turn_back(1, 0, 4)
+        turn_back(1, 2, 5)
         pair_back(1, 0, on_scalar)
         pair_back(1, 2, on_scalar)
-        first_product(0, 7, 0)
-        abs_w(2)
-        abs_w(3)
-        quantise_e(0, 0, 4)
-        scale_rows(0, 7)
-        first_product(1, 4, 1)
-        quantise_e(1, 0, 4)
-        pair_back(0, 4, on_scalar)
         scale_rows(1, 4)
-        compare(2)
-        first_product(1, 5, 5)
-        interleave(1, 2, on_scalar)
-        second_product(0, 2)
-        scale_rows(1, 5)
-        apply_mask(0)
-        second_product(1, 6)
-        interleave(1, 3, on_scalar)
-        compare(3)
-        apply_mask(1)
-        first_product(1, 6, 7)
-        second_product(2, 3)
-        quantise_e(0, 4, 2)
-        apply_mask(2)
-        turn_back(0, 6, 4)
-        turn_back(1, 4, 0)
-        scale_rows(1, 6)
-        second_product(3, 1)
-        first_product(1, 7, 5)
-        quantise_x(1, 1)
+        first_product(1, 5, 1)
         pair_back(0, 6, on_scalar)
+        abs_w(3)
+        quantise_e(1, 0, 4)
+        first_product(1, 6, 3)
+        scale_rows(1, 5)
+        interleave(1, 2, on_scalar)
+        interleave(1, 3, on_vector)
+        second_product(0, 6)
+        compare(3)
+        second_product(1, 7)
+        scale_rows(1, 6)
+        apply_mask(0)
+        second_product(2, 0)
+        quantise_x(1, 1)
+        apply_mask(1)
+        turn_back(1, 4, 4)
+        second_product(3, 2)
+        apply_mask(2)
+        first_product(1, 7, 1)
         pair_back(1, 4, on_scalar)
+        quantise_e(0, 4, 4)
         apply_mask(3)
         scale_rows(1, 7)
-        quantise_e(0, 6, 2)
         quantise_e(1, 4, 2)
-        second_product(4, 2)
-        second_product(5, 6)
+        second_product(4, 5)
+        second_product(5, 3)
         apply_mask(4)
-        turn_back(1, 6, 7, 1)
-        turn_back(1, 7, 3, 1)
+        turn_back(1, 6, 6, 1)
+        turn_back(1, 7, 7, 1)
         pair_back(1, 6, on_scalar, 1)
         pair_back(1, 7, on_scalar, 1)
         apply_mask(5)
-        second_product(6, 4)
-        second_product(7, 0)
+        second_product(6, 0)
+        second_product(7, 4)
         quantise_e(1, 6, 2)
         apply_mask(6)
-        apply_mask_pooled(7)
-        second_pass(8, 0, 1)
-        second_pass(9, 0, 5)
+        apply_mask(7)
+        second_pass(8, 0, 2)
+        second_pass(9, 0, 1)
         second_pass(8, 1)
         second_pass(9, 1)
         apply_mask(8)
         apply_mask(9)
-        store(7)
         for unit in range(10, 16):
-            second_product(unit, (2, 6, 7, 3, 4, 0)[unit - 10])
-            if unit == 11:
-                apply_mask_pooled(unit)
-            else:
-                apply_mask(unit)
-            if unit == 13:
-                store(11)
+            second_product(unit, (5, 3, 6, 7, 0, 4)[unit - 10])
+            apply_mask(unit)

@@ -24,6 +24,7 @@ TILES = T // P
 ROW_TILES = C // P
 HALF = 512
 BANKS = 8
+LINE = 256
 SPLIT = (0, 2, 3)
 
 
@@ -38,7 +39,7 @@ def tile_straight_through_weight_gradient_s9_kernel(
         psum = ctx.enter_context(tc.psum_pool(name="psum", bufs=1))
         ctx.enter_context(tc.manual_schedule())
 
-        v_planes = [keep.tile([P, PASSES, HALF], U8, name=f"v_planes{h}", align_bytes=64) for h in range(2)]
+        v_planes = [keep.tile([P, PASSES, HALF], U8, name=f"v_planes{h}", align_bytes=LINE) for h in range(2)]
         for h in range(2):
             nc.vector.memset(v_planes[h][:].rearrange("p g n -> p (g n)").bitcast(I32), 0)
         ident = keep.tile([P, P], F32, name="ident")
@@ -52,15 +53,15 @@ def tile_straight_through_weight_gradient_s9_kernel(
         lo_sb = keep.tile([P, GROUPS, 4], BF16, name="lo_sb")
         hi_sb = keep.tile([P, GROUPS, 4], BF16, name="hi_sb")
         d_sb = [
-            [keep.tile([P, O // 2], BF16, name=f"d_sb{i}_{b}") for b in range(2)]
+            [keep.tile([P, O // 2], BF16, name=f"d_sb{i}_{b}", align_bytes=LINE) for b in range(2)]
             if i in SPLIT
-            else keep.tile([P, O], BF16, name=f"d_sb{i}")
+            else keep.tile([P, O], BF16, name=f"d_sb{i}", align_bytes=LINE)
             for i in range(TILES)
         ]
-        v_codes = [[keep.tile([P, 2, F], U8, name=f"v_codes{h}_{b}", align_bytes=64) for b in range(2)] for h in range(2)]
+        v_codes = [[keep.tile([P, 2, F], U8, name=f"v_codes{h}_{b}", align_bytes=LINE) for b in range(2)] for h in range(2)]
         x_first = [keep.tile([P, 4, HALF], BF16, name=f"x_first{a}") for a in range(2)]
         x_late = keep.tile([P, 4, C], BF16, name="x_late")
-        w_sb = [keep.tile([P, 2, F], BF16, name=f"w_sb{a}") for a in range(ROW_TILES // 2)]
+        w_sb = [keep.tile([P, 2, F], BF16, name=f"w_sb{a}", align_bytes=LINE) for a in range(ROW_TILES // 2)]
 
         x_v = x.rearrange("(g p j) c -> g p j c", p=P, j=4)
         w_v = w.rearrange("(ct p) f -> p ct f", p=P)
@@ -92,16 +93,16 @@ def tile_straight_through_weight_gradient_s9_kernel(
         def load_w(a):
             nc.sync.dma_start(out=w_sb[a][:], in_=w_v[:, 2 * a : 2 * a + 2, :])
 
-        d_codes = [keep.tile([P, PASSES * 512], U32, name=f"d_codes{g}", align_bytes=64) for g in range(GROUPS)]
-        d_scales = [keep.tile([P, PASSES * 512], U8, name=f"d_scales{g}", align_bytes=64) for g in range(GROUPS)]
+        d_codes = [keep.tile([P, PASSES * 512], U32, name=f"d_codes{g}", align_bytes=LINE) for g in range(GROUPS)]
+        d_scales = [keep.tile([P, PASSES * 512], U8, name=f"d_scales{g}", align_bytes=LINE) for g in range(GROUPS)]
 
 
-        x_grp = [keep.tile([P, C, 4], BF16, name=f"x_grp{g}", align_bytes=64) for g in range(GROUPS)]
-        x_codes = [keep.tile([P, C], U32, name=f"x_codes{g}", align_bytes=64) for g in range(GROUPS)]
-        x_scales = [keep.tile([P, C], U8, name=f"x_scales{g}", align_bytes=64) for g in range(GROUPS)]
-        e_grp = [keep.tile([P, F, 4], BF16, name=f"e_grp{g}", align_bytes=64) for g in range(GROUPS)]
-        e_codes = [keep.tile([P, F], U32, name=f"e_codes{g}", align_bytes=64) for g in range(GROUPS)]
-        e_scales = [keep.tile([P, F], U8, name=f"e_scales{g}", align_bytes=64) for g in range(GROUPS)]
+        x_grp = [keep.tile([P, C, 4], BF16, name=f"x_grp{g}", align_bytes=LINE) for g in range(GROUPS)]
+        x_codes = [keep.tile([P, C], U32, name=f"x_codes{g}", align_bytes=LINE) for g in range(GROUPS)]
+        x_scales = [keep.tile([P, C], U8, name=f"x_scales{g}", align_bytes=LINE) for g in range(GROUPS)]
+        e_grp = [keep.tile([P, F, 4], BF16, name=f"e_grp{g}", align_bytes=LINE) for g in range(GROUPS)]
+        e_codes = [keep.tile([P, F], U32, name=f"e_codes{g}", align_bytes=LINE) for g in range(GROUPS)]
+        e_scales = [keep.tile([P, F], U8, name=f"e_scales{g}", align_bytes=LINE) for g in range(GROUPS)]
 
         def bank(n):
             return psum.tile([P, 512], F32, name=f"bank{n}", tag=f"bank{n}")
@@ -139,7 +140,7 @@ def tile_straight_through_weight_gradient_s9_kernel(
         def pair_words(pair, k, copy):
             g, first = pair // 2, 2 * P * (pair % 2)
             if pair % 2 == 0:
-                d_words[(g, k)] = stage.tile([P, 512, 4], BF16, name="d_words", bufs=5, align_bytes=64)
+                d_words[(g, k)] = stage.tile([P, 512, 4], BF16, name="d_words", bufs=5, align_bytes=LINE)
             words = d_words[(g, k)][:, first : first + 2 * P, :].rearrange("p m t -> p (m t)").bitcast(F32)
             copy(
                 out=words.rearrange("p (e m u) -> p e m u", e=2, u=2),
@@ -271,14 +272,14 @@ def tile_straight_through_weight_gradient_s9_kernel(
 
         def apply_mask(unit):
             h, ct = unit // ROW_TILES, unit % ROW_TILES
-            res[unit] = outs.tile([P, HALF], F32, name="res")
+            res[unit] = outs.tile([P, HALF], F32, name="res", align_bytes=LINE)
             keep_mask = w_sb[ct // 2][:, ct % 2, h * HALF : (h + 1) * HALF]
             nc.vector.tensor_tensor(out=res[unit][:], in0=o_bank[unit][:], in1=keep_mask, op=OP.mult)
             store(unit)
 
         def apply_mask_pooled(unit):
             h, ct = unit // ROW_TILES, unit % ROW_TILES
-            res[unit] = outs.tile([P, HALF], F32, name="res")
+            res[unit] = outs.tile([P, HALF], F32, name="res", align_bytes=LINE)
             keep_mask = w_sb[ct // 2][:, ct % 2, h * HALF : (h + 1) * HALF]
             nc.scalar.copy(out=res[unit][:], in_=o_bank[unit][:])
             nc.gpsimd.tensor_tensor(out=res[unit][:], in0=res[unit][:], in1=keep_mask, op=OP.mult)
@@ -297,22 +298,21 @@ def tile_straight_through_weight_gradient_s9_kernel(
             load_delta_half(3, b)
         load_v_scales(0)
         load_v_codes(0, 0)
-        load_v_codes(0, 1)
         load_x(0, 0)
+        load_v_codes(0, 1)
         load_delta(4)
         load_delta(5)
         load_v_scales(1)
         load_v_codes(1, 0)
+        load_w(0)
         load_v_codes(1, 1)
-        load_x(0, 1)
         load_delta(6)
         load_delta(7)
-        load_w(0)
+        load_x(0, 1)
         load_x(1, 0)
         load_x(1, 1)
-        load_w(1)
-        load_w(2)
-        load_w(3)
+        for a in range(1, 4):
+            load_w(a)
 
         nc.scalar.activation(out=gain_pad[:], in_=ident[:], func=ACT.Copy, scale=0.0)
         nc.vector.tensor_copy(out=gain_pad[0 : F // P, :], in_=gain_rows[:])
@@ -329,125 +329,127 @@ def tile_straight_through_weight_gradient_s9_kernel(
                     turn(i, k, 4 + k)
         quantise_delta(0, 0, 0, 256)
         for k in range(PASSES):
-            pair_words(1, k, on_vector if k == 1 else on_scalar)
+            pair_words(1, k, on_scalar)
         quantise_delta(0, 0, 256, 256)
-        for k in range(1, PASSES):
-            quantise_delta(0, k)
+        quantise_delta(0, 1)
+        quantise_delta(0, 2)
+        clip(0, 0)
+        quantise_delta(0, 3)
+        interleave(0, 0, on_scalar)
+        interleave(0, 1, on_vector)
         for fc in range(4):
             z_bank[(0, fc)] = bank(fc)
         for k in range(2):
             for fc in range(4):
                 first_pass(0, fc, k)
-        clip(0, 0)
-        sort_words(4, on_scalar)
-        sort_words(5, on_scalar)
-        interleave(0, 0, on_vector, 2)
-        quantise_x(0, 0)
         for fc in range(4):
             for k in range(2, PASSES):
                 first_pass(0, fc, k)
             scale_rows(0, fc)
+        sort_words(4, on_vector)
+        sort_words(5, on_vector)
+        quantise_x(0, 0)
         for k in range(PASSES):
             turn(4, k, 4 + k)
             turn(5, k)
-            pair_words(2, k, on_vector if k < 3 else on_scalar)
-        clip(0, 1)
-        first_product(0, 4, 0)
-        for k in range(PASSES):
-            turn(6, k, (4, 5, 1, 6)[k])
-        interleave(0, 2, on_vector, 2)
-        scale_rows(0, 4)
-        for k in range(PASSES):
-            quantise_delta(1, k, 0, 256)
-        first_product(0, 5, 2)
-        scale_rows(0, 5)
-        quantise_x(0, 1)
-        for k in range(PASSES):
-            turn(7, k)
-            pair_words(3, k, on_vector if k == 1 else on_scalar)
-        first_product(0, 6, 3)
+            pair_words(2, k, on_scalar)
+        turn_back(0, 0, 0)
         abs_w(0)
-        for k in range(PASSES):
-            quantise_delta(1, k, 256, 256)
-        first_product(0, 7, 7)
-        scale_rows(0, 6)
-        clip(1, 0)
-        clip(1, 1)
-        first_product(1, 0, 0)
-        scale_rows(0, 7)
-        compare(0)
-        interleave(1, 0, on_scalar)
-        first_product(1, 1, 4)
-        scale_rows(1, 0)
-        interleave(1, 1, on_vector)
-        abs_w(1)
-        turn_back(0, 0, 5)
-        turn_back(0, 2, 1)
-        turn_back(0, 4, 6)
-        turn_back(0, 6, 2)
-        scale_rows(1, 1)
-        first_product(1, 2, 3)
-        compare(1)
+        quantise_delta(1, 0, 0, 256)
+        for fc in (4, 5):
+            z_bank[(0, fc)] = bank(fc - 3)
+        for b in range(2):
+            for fc in (4, 5):
+                for k in (2 * b, 2 * b + 1):
+                    first_pass(0, fc, k)
         pair_back(0, 0, on_scalar)
-        quantise_x(1, 0)
-        first_product(1, 3, 7)
+        compare(0)
+        sort_words(6, on_vector)
+        scale_rows(0, 4)
+        first_product(0, 6, 3)
+        scale_rows(0, 5)
+        quantise_delta(1, 1, 0, 256)
+        sort_words(7, on_vector)
+        quantise_delta(1, 2, 0, 256)
+        clip(0, 1)
+        quantise_delta(1, 3, 0, 256)
+        scale_rows(0, 6)
+        for i in (6, 7):
+            for k in range(PASSES):
+                turn(i, k, 4 + k)
+        turn_back(0, 2, 0)
+        interleave(0, 2, on_vector)
+        for k in range(PASSES):
+            pair_words(3, k, on_scalar)
+        first_product(0, 7, 1)
+        quantise_delta(1, 0, 256, 256)
+        quantise_delta(1, 1, 256, 256)
+        clip(1, 0)
+        quantise_delta(1, 2, 256, 256)
+        quantise_delta(1, 3, 256, 256)
+        clip(1, 1)
+        interleave(0, 3, on_vector)
         pair_back(0, 2, on_scalar)
-        scale_rows(1, 2)
-        pair_back(0, 4, on_vector)
-        abs_w(2)
-        first_product(1, 4, 0)
-        scale_rows(1, 3)
+        first_product(1, 0, 2)
+        scale_rows(0, 7)
+        interleave(1, 0, on_scalar)
         quantise_e(0, 0, 4)
+        first_product(1, 1, 3)
+        scale_rows(1, 0)
+        quantise_x(0, 1)
+        first_product(1, 2, 4)
+        scale_rows(1, 1)
+        abs_w(1)
+        first_product(1, 3, 5)
+        scale_rows(1, 2)
+        abs_w(2)
+        compare(1)
+        first_product(1, 4, 6)
+        scale_rows(1, 3)
+        interleave(1, 1, on_scalar)
         compare(2)
-        turn_back(1, 0, 4)
-        turn_back(1, 2, 5)
+        quantise_x(1, 0)
+        turn_back(0, 4, 7)
+        turn_back(0, 6, 0)
+        turn_back(1, 0, 1)
+        turn_back(1, 2, 2)
         pair_back(1, 0, on_scalar)
         pair_back(1, 2, on_scalar)
         scale_rows(1, 4)
-        first_product(1, 5, 1)
-        pair_back(0, 6, on_scalar)
         abs_w(3)
-        quantise_e(1, 0, 4)
-        first_product(1, 6, 3)
+        first_product(1, 5, 3)
         scale_rows(1, 5)
         interleave(1, 2, on_scalar)
-        interleave(1, 3, on_vector)
-        second_product(0, 6)
-        compare(3)
-        second_product(1, 7)
+        quantise_e(1, 0, 4)
+        first_product(1, 6, 4)
+        pair_back(0, 4, on_scalar)
         scale_rows(1, 6)
-        apply_mask(0)
-        second_product(2, 0)
-        quantise_x(1, 1)
-        apply_mask(1)
-        turn_back(1, 4, 4)
-        second_product(3, 2)
-        apply_mask(2)
-        first_product(1, 7, 1)
-        pair_back(1, 4, on_scalar)
-        quantise_e(0, 4, 4)
-        apply_mask(3)
+        interleave(1, 3, on_vector)
+        second_product(0, 5)
+        second_product(1, 1)
+        first_product(1, 7, 6)
+        pair_back(0, 6, on_scalar)
         scale_rows(1, 7)
-        quantise_e(1, 4, 2)
-        second_product(4, 5)
-        second_product(5, 3)
-        apply_mask(4)
-        turn_back(1, 6, 6, 1)
-        turn_back(1, 7, 7, 1)
-        pair_back(1, 6, on_scalar, 1)
-        pair_back(1, 7, on_scalar, 1)
-        apply_mask(5)
-        second_product(6, 0)
-        second_product(7, 4)
-        quantise_e(1, 6, 2)
-        apply_mask(6)
-        apply_mask(7)
-        second_pass(8, 0, 2)
-        second_pass(9, 0, 1)
-        second_pass(8, 1)
-        second_pass(9, 1)
-        apply_mask(8)
-        apply_mask(9)
-        for unit in range(10, 16):
-            second_product(unit, (5, 3, 6, 7, 0, 4)[unit - 10])
-            apply_mask(unit)
+        apply_mask(0)
+        apply_mask(1)
+        compare(3)
+        quantise_x(1, 1)
+        second_product(2, 2)
+        second_product(3, 7)
+        quantise_e(0, 4, 4)
+        turn_back(1, 4, 3)
+        turn_back(1, 6, 4)
+        pair_back(1, 4, on_scalar)
+        pair_back(1, 6, on_scalar)
+        apply_mask(2)
+        apply_mask(3)
+        for unit in range(4, 16):
+            second_product(unit, (0, 5, 1, 6, 2, 7, 3, 4)[(unit - 4) % BANKS])
+            if unit in (6, 9,):
+                apply_mask_pooled(unit)
+            else:
+                apply_mask(unit)
+            if unit - 2 in (6, 9,):
+                store(unit - 2)
+            if unit == 4:
+                quantise_e(1, 4, 4)

@@ -20,12 +20,11 @@ ACT = mybir.ActivationFunctionType
 P = 128
 PASSES = O // 512
 GROUPS = T // 512
-TILES = T // P
+STEPS = GROUPS * PASSES
 ROW_TILES = C // P
 HALF = 512
 BANKS = 8
 LINE = 256
-SPLIT = (0, 2, 3)
 
 
 def tile_straight_through_weight_gradient_s9_kernel(
@@ -35,7 +34,7 @@ def tile_straight_through_weight_gradient_s9_kernel(
     with ExitStack() as ctx:
         keep = ctx.enter_context(tc.tile_pool(name="keep", bufs=1))
         stage = ctx.enter_context(tc.tile_pool(name="stage", bufs=3))
-        outs = ctx.enter_context(tc.tile_pool(name="outs", bufs=14))
+        outs = ctx.enter_context(tc.tile_pool(name="outs", bufs=10))
         psum = ctx.enter_context(tc.psum_pool(name="psum", bufs=1))
         ctx.enter_context(tc.manual_schedule())
 
@@ -52,27 +51,25 @@ def tile_straight_through_weight_gradient_s9_kernel(
         r_all = keep.tile([P, F], BF16, name="r_all")
         lo_sb = keep.tile([P, GROUPS, 4], BF16, name="lo_sb")
         hi_sb = keep.tile([P, GROUPS, 4], BF16, name="hi_sb")
-        d_sb = [
-            [keep.tile([P, O // 2], BF16, name=f"d_sb{i}_{b}", align_bytes=LINE) for b in range(2)]
-            if i in SPLIT
-            else keep.tile([P, O], BF16, name=f"d_sb{i}", align_bytes=LINE)
-            for i in range(TILES)
-        ]
-        v_codes = [[keep.tile([P, 2, F], U8, name=f"v_codes{h}_{b}", align_bytes=LINE) for b in range(2)] for h in range(2)]
-        x_first = [keep.tile([P, 4, HALF], BF16, name=f"x_first{a}") for a in range(2)]
-        x_late = keep.tile([P, 4, C], BF16, name="x_late")
+        d_head = [[keep.tile([P, 2 * 512], BF16, name=f"d_head{k}_{a}", align_bytes=LINE) for a in range(2)] for k in range(PASSES)]
+        d_late = [[keep.tile([P, 2 * 1024], BF16, name=f"d_late{b}_{a}", align_bytes=LINE) for a in range(2)] for b in range(2)]
+        v_head = [keep.tile([P, F], U8, name=f"v_head{k}", align_bytes=LINE) for k in range(PASSES)]
+        v_late = [keep.tile([P, 2, F], U8, name=f"v_late{b}", align_bytes=LINE) for b in range(2)]
+        x_sb = [[keep.tile([P, 4, HALF], BF16, name=f"x_sb{g}_{a}", align_bytes=LINE) for a in range(2)] for g in range(GROUPS)]
         w_sb = [keep.tile([P, 2, F], BF16, name=f"w_sb{a}", align_bytes=LINE) for a in range(ROW_TILES // 2)]
 
+        d_v = delta.rearrange("(g i p) (k n) -> g k p i n", p=P, i=4, n=512)
+        d_wide = delta.rearrange("(g i p) (b n) -> g b p i n", p=P, i=4, n=1024)
         x_v = x.rearrange("(g p j) c -> g p j c", p=P, j=4)
         w_v = w.rearrange("(ct p) f -> p ct f", p=P)
         words_v = v_words.rearrange("g p b -> p g b")
         scales_v = v_scales.rearrange("g q n -> q g n").bitcast(I32)
 
-        def load_delta(i):
-            nc.sync.dma_start(out=d_sb[i][:], in_=delta[i * P : (i + 1) * P, :])
+        def load_head(k, a):
+            nc.sync.dma_start(out=d_head[k][a][:].rearrange("p (i n) -> p i n", i=2), in_=d_v[0, k, :, 2 * a : 2 * a + 2, :])
 
-        def load_delta_half(i, b):
-            nc.sync.dma_start(out=d_sb[i][b][:], in_=delta[i * P : (i + 1) * P, b * O // 2 : (b + 1) * O // 2])
+        def load_late(b, a):
+            nc.sync.dma_start(out=d_late[b][a][:].rearrange("p (i n) -> p i n", i=2), in_=d_wide[1, b, :, 2 * a : 2 * a + 2, :])
 
         def load_v_scales(h):
             for s in range(4):
@@ -81,22 +78,20 @@ def tile_straight_through_weight_gradient_s9_kernel(
                     in_=scales_v[s:16:4, :, h * P : (h + 1) * P],
                 )
 
-        def load_v_codes(h, b):
-            nc.sync.dma_start(out=v_codes[h][b][:], in_=words_v[:, 2 * b : 2 * b + 2, h * F : (h + 1) * F])
+        def load_v_head(k):
+            nc.sync.dma_start(out=v_head[k][:], in_=v_words[k, :, 0:F])
+
+        def load_v_late(b):
+            nc.sync.dma_start(out=v_late[b][:], in_=words_v[:, 2 * b : 2 * b + 2, F : 2 * F])
 
         def load_x(g, a):
-            if g == 0:
-                nc.sync.dma_start(out=x_first[a][:], in_=x_v[0, :, :, a * HALF : (a + 1) * HALF])
-            else:
-                nc.sync.dma_start(out=x_late[:, 2 * a : 2 * a + 2, :], in_=x_v[1, :, 2 * a : 2 * a + 2, :])
+            nc.sync.dma_start(out=x_sb[g][a][:], in_=x_v[g, :, :, a * HALF : (a + 1) * HALF])
 
         def load_w(a):
             nc.sync.dma_start(out=w_sb[a][:], in_=w_v[:, 2 * a : 2 * a + 2, :])
 
-        d_codes = [keep.tile([P, PASSES * 512], U32, name=f"d_codes{g}", align_bytes=LINE) for g in range(GROUPS)]
-        d_scales = [keep.tile([P, PASSES * 512], U8, name=f"d_scales{g}", align_bytes=LINE) for g in range(GROUPS)]
-
-
+        d_codes = [keep.tile([P, 512], U32, name=f"d_codes{s}", align_bytes=LINE) for s in range(STEPS)]
+        d_scales = [keep.tile([P, 512], U8, name=f"d_scales{s}", align_bytes=LINE) for s in range(STEPS)]
         x_grp = [keep.tile([P, C, 4], BF16, name=f"x_grp{g}", align_bytes=LINE) for g in range(GROUPS)]
         x_codes = [keep.tile([P, C], U32, name=f"x_codes{g}", align_bytes=LINE) for g in range(GROUPS)]
         x_scales = [keep.tile([P, C], U8, name=f"x_scales{g}", align_bytes=LINE) for g in range(GROUPS)]
@@ -117,88 +112,93 @@ def tile_straight_through_weight_gradient_s9_kernel(
                 nc.tensor.transpose(ps[:, c::4], words[:, c : c + 1].to_broadcast([P, P]), ident[:])
             nc.vector.tensor_copy(out=r_all[:].bitcast(F32), in_=ps[:])
 
-        def sort_words(i, copy):
-            d_sorted[i] = stage.tile([P, O // 2], F32, name="d_sorted")
+        def gain_to_partitions(n):
+            ps = bank(n)
+            nc.tensor.transpose(ps[:, 0:P], gain_pad[:], ident[:])
+            nc.scalar.copy(out=gain_part[:], in_=ps[:, 0 : F // P])
+
+        def raw_words(s, a):
+            if s < PASSES:
+                return d_head[s][a][:].bitcast(F32).rearrange("p (e n) -> p e n", e=2)
+            k = s - PASSES
+            return d_late[k // 2][a][:].bitcast(F32).rearrange("p (e n) -> p e n", e=2)[:, :, 256 * (k % 2) : 256 * (k % 2 + 1)]
+
+        def sort_words(s, a, copy):
+            d_sorted[(s, a)] = stage.tile([P, 512], F32, name="d_sorted", bufs=4)
             copy(
-                out=d_sorted[i][:].rearrange("p (g u m i) -> p g m u i", g=PASSES, u=2, i=2),
-                in_=d_sb[i][:].bitcast(F32).rearrange("p (g m i u) -> p g m u i", g=PASSES, u=2, i=2),
+                out=d_sorted[(s, a)][:].rearrange("p (e u m j) -> p e m u j", e=2, u=2, j=2),
+                in_=raw_words(s, a).rearrange("p e (m j u) -> p e m u j", u=2, j=2),
             )
 
-        def turn(i, k, n=None):
-            if i % 2 == 0:
-                t_bank[(i // 2, k)] = bank(n)
-            for u in range(2):
-                if i in SPLIT:
-                    src = d_sb[i][k // 2][:].bitcast(F32)[:, 256 * (k % 2) + u : 256 * (k % 2 + 1) : 2]
-                elif i in d_sorted:
-                    src = d_sorted[i][:, (2 * k + u) * P : (2 * k + u + 1) * P]
-                else:
-                    src = d_sb[i][:].bitcast(F32)[:, 256 * k + u : 256 * (k + 1) : 2]
-                first = (2 * (i % 2) + u) * P
-                nc.tensor.transpose(t_bank[(i // 2, k)][:, first : first + P], src, ident[:])
+        def turn(s, a, n):
+            t_bank[(s, a)] = ps = bank(n)
+            for e in range(2):
+                for u in range(2):
+                    if (s, a) in d_sorted:
+                        src = d_sorted[(s, a)][:, (2 * e + u) * P : (2 * e + u + 1) * P]
+                    else:
+                        src = raw_words(s, a)[:, e, u:256:2]
+                    nc.tensor.transpose(ps[:, (2 * e + u) * P : (2 * e + u + 1) * P], src, ident[:])
 
-        def pair_words(pair, k, copy):
-            g, first = pair // 2, 2 * P * (pair % 2)
-            if pair % 2 == 0:
-                d_words[(g, k)] = stage.tile([P, 512, 4], BF16, name="d_words", bufs=5, align_bytes=LINE)
-            words = d_words[(g, k)][:, first : first + 2 * P, :].rearrange("p m t -> p (m t)").bitcast(F32)
+        def pair_words(s, a, copy):
+            if a == 0:
+                d_words[s] = stage.tile([P, 512, 4], BF16, name="d_words", align_bytes=LINE)
+            words = d_words[s][:, 256 * a : 256 * (a + 1), :].rearrange("p m t -> p (m t)").bitcast(F32)
             copy(
                 out=words.rearrange("p (e m u) -> p e m u", e=2, u=2),
-                in_=t_bank[(pair, k)][:].rearrange("p (e u m) -> p e m u", e=2, u=2),
+                in_=t_bank[(s, a)][:].rearrange("p (e u m) -> p e m u", e=2, u=2),
             )
 
-        def quantise_delta(g, k, first=0, count=512):
-            cols = slice(512 * k + first, 512 * k + first + count)
+        def quantise_delta(s, first=0, count=2):
+            cols = slice(256 * first, 256 * (first + count))
             nc.vector.quantize_mx(
-                out=d_codes[g][:, cols].bitcast(E4M3),
-                scales=d_scales[g][:, cols],
-                in_=d_words[(g, k)][:, first : first + count, :].rearrange("p m t -> p (m t)"),
+                out=d_codes[s][:, cols].bitcast(E4M3),
+                scales=d_scales[s][:, cols],
+                in_=d_words[s][:, cols, :].rearrange("p m t -> p (m t)"),
             )
 
-        def first_pass(g, fc, k):
+        def first_pass(g, fc, k, n=None):
             h, n0 = fc // 4, P * (fc % 4)
+            if k == 0:
+                z_bank[(g, fc)] = bank(n)
+            codes = v_head[k][:] if h == 0 else v_late[k // 2][:, k % 2, :]
             nc.tensor.matmul_mx(
                 out=z_bank[(g, fc)][:],
-                lhsT=v_codes[h][k // 2][:, k % 2, 2 * n0 : 2 * (n0 + P)].bitcast(E2M1),
+                lhsT=codes[:, 2 * n0 : 2 * (n0 + P)].bitcast(E2M1),
                 lhsT_scale=v_planes[h][:, k, n0 : n0 + P],
-                rhs=d_codes[g][:, 512 * k : 512 * (k + 1)].bitcast(E4M3),
-                rhs_scale=d_scales[g][:, 512 * k : 512 * (k + 1)],
+                rhs=d_codes[PASSES * g + k][:].bitcast(E4M3),
+                rhs_scale=d_scales[PASSES * g + k][:],
                 start=(k == 0),
                 stop=(k == PASSES - 1),
             )
 
         def first_product(g, fc, n):
-            z_bank[(g, fc)] = bank(n)
             for k in range(PASSES):
-                first_pass(g, fc, k)
+                first_pass(g, fc, k, n)
 
-        def scale_rows(g, fc):
-            e_rows[(g, fc)] = stage.tile([P, 2, P, 2], BF16, name="e_rows", bufs=13)
-            nc.scalar.activation(
-                out=e_rows[(g, fc)][:],
-                in_=z_bank[(g, fc)][:].rearrange("p (m u e) -> p u m e", u=2, e=2),
-                func=ACT.Copy,
-                scale=gain_part[:, fc : fc + 1],
-            )
+        def scale_rows(g, fc, on_vector=False):
+            e_rows[(g, fc)] = stage.tile([P, 2, P, 2], BF16, name="e_rows", bufs=10)
+            src = z_bank[(g, fc)][:].rearrange("p (m u e) -> p u m e", u=2, e=2)
+            if on_vector:
+                nc.vector.tensor_scalar(
+                    out=e_rows[(g, fc)][:], in0=src, scalar1=gain_part[:, fc : fc + 1], scalar2=None, op0=OP.mult
+                )
+            else:
+                nc.scalar.activation(out=e_rows[(g, fc)][:], in_=src, func=ACT.Copy, scale=gain_part[:, fc : fc + 1])
 
-        def turn_back(g, fc, n, count=2):
+        def turn_back(g, fc, n):
             b_bank[(g, fc)] = ps = bank(n)
-            for c in range(count):
+            for c in range(2):
                 for u in range(2):
                     words = e_rows[(g, fc + c)][:, u, :, :].rearrange("p m e -> p (m e)").bitcast(F32)
                     nc.tensor.transpose(ps[:, (2 * c + u) * P : (2 * c + u + 1) * P], words, ident[:])
 
-        def pair_back(g, fc, copy, count=2):
-            words = e_grp[g][:, fc * P : (fc + count) * P, :].rearrange("p n t -> p (n t)").bitcast(F32)
+        def pair_back(g, fc, copy):
+            words = e_grp[g][:, fc * P : (fc + 2) * P, :].rearrange("p n t -> p (n t)").bitcast(F32)
             copy(
-                out=words.rearrange("p (c n u) -> p c n u", c=count, u=2),
-                in_=b_bank[(g, fc)][:, 0 : 2 * count * P].rearrange("p (c u n) -> p c n u", c=count, u=2),
+                out=words.rearrange("p (c n u) -> p c n u", c=2, u=2),
+                in_=b_bank[(g, fc)][:].rearrange("p (c u n) -> p c n u", c=2, u=2),
             )
-
-        def gain_to_partitions(n):
-            ps = bank(n)
-            nc.tensor.transpose(ps[:, 0:P], gain_pad[:], ident[:])
-            nc.scalar.copy(out=gain_part[:], in_=ps[:, 0 : F // P])
 
         def quantise_e(g, fc, count):
             cols = slice(fc * P, (fc + count) * P)
@@ -209,27 +209,21 @@ def tile_straight_through_weight_gradient_s9_kernel(
             )
 
         def clip(g, a):
-            for j in range(4) if g == 0 else (2 * a, 2 * a + 1):
-                row = x_first[a][:, j, :] if g == 0 else x_late[:, j, :]
+            for j in range(4):
+                row = x_sb[g][a][:, j, :]
                 nc.vector.tensor_scalar(
-                    out=row,
-                    in0=row,
-                    scalar1=lo_sb[:, g, j : j + 1],
-                    scalar2=hi_sb[:, g, j : j + 1],
-                    op0=OP.max,
-                    op1=OP.min,
+                    out=row, in0=row, scalar1=lo_sb[:, g, j : j + 1], scalar2=hi_sb[:, g, j : j + 1], op0=OP.max, op1=OP.min
                 )
 
-        def interleave(g, k, copy, count=1):
-            cols = slice(256 * k, 256 * (k + count))
-            rows = x_first[k // 2][:, :, 256 * (k % 2) : 256 * (k % 2 + count)] if g == 0 else x_late[:, :, cols]
+        def interleave(g, ct, count, copy):
+            cols = slice(P * ct, P * (ct + count))
             copy(
                 out=x_grp[g][:, cols, :].rearrange("p (c i) j -> p c j i", i=4),
-                in_=rows.rearrange("p j (c i) -> p c j i", i=4),
+                in_=x_sb[g][ct // 4][:, :, P * (ct % 4) : P * (ct % 4 + count)].rearrange("p j (c i) -> p c j i", i=4),
             )
 
-        def quantise_x(g, k, count=1):
-            cols = slice(512 * k, 512 * (k + count))
+        def quantise_x(g, a):
+            cols = slice(512 * a, 512 * (a + 1))
             nc.vector.quantize_mx(
                 out=x_codes[g][:, cols].bitcast(E4M3),
                 scales=x_scales[g][:, cols],
@@ -290,166 +284,204 @@ def tile_straight_through_weight_gradient_s9_kernel(
         nc.scalar.dma_start(out=gain_rows[:], in_=gain.rearrange("(c p) -> c p", p=P))
         nc.gpsimd.dma_start(out=lo_sb[:], in_=lo.rearrange("(g p j) -> p g j", p=P, j=4))
         nc.gpsimd.dma_start(out=hi_sb[:], in_=hi.rearrange("(g p j) -> p g j", p=P, j=4))
-        load_delta_half(0, 0)
-        load_delta_half(0, 1)
-        load_delta(1)
-        for b in range(2):
-            load_delta_half(2, b)
-            load_delta_half(3, b)
+        for k in range(2):
+            load_head(k, 0)
+            load_head(k, 1)
         load_v_scales(0)
-        load_v_codes(0, 0)
-        load_x(0, 0)
-        load_v_codes(0, 1)
-        load_delta(4)
-        load_delta(5)
+        load_v_head(0)
+        for k in range(2, PASSES):
+            load_head(k, 0)
+            load_head(k, 1)
+            load_v_head(k - 1)
+        load_v_head(3)
         load_v_scales(1)
-        load_v_codes(1, 0)
-        load_w(0)
-        load_v_codes(1, 1)
-        load_delta(6)
-        load_delta(7)
-        load_x(0, 1)
+        load_v_late(0)
+        load_x(0, 0)
+        load_v_late(1)
+        load_late(0, 0)
+        load_late(0, 1)
         load_x(1, 0)
+        load_late(1, 0)
+        load_late(1, 1)
+        load_w(0)
+        load_x(0, 1)
+        load_w(1)
         load_x(1, 1)
-        for a in range(1, 4):
-            load_w(a)
+        load_w(2)
+        load_w(3)
 
         nc.scalar.activation(out=gain_pad[:], in_=ident[:], func=ACT.Copy, scale=0.0)
         nc.vector.tensor_copy(out=gain_pad[0 : F // P, :], in_=gain_rows[:])
-        spread_r(7)
-        for k in range(PASSES):
-            turn(0, k, k)
-        gain_to_partitions(6)
-        for k in range(PASSES):
-            turn(1, k)
-            pair_words(0, k, on_vector if k % 2 else on_scalar)
-        for b in range(2):
-            for i in (2, 3):
-                for k in (2 * b, 2 * b + 1):
-                    turn(i, k, 4 + k)
-        quantise_delta(0, 0, 0, 256)
-        for k in range(PASSES):
-            pair_words(1, k, on_scalar)
-        quantise_delta(0, 0, 256, 256)
-        quantise_delta(0, 1)
-        quantise_delta(0, 2)
-        clip(0, 0)
-        quantise_delta(0, 3)
-        interleave(0, 0, on_scalar)
-        interleave(0, 1, on_vector)
+        spread_r(0)
+        turn(0, 0, 4)
+        pair_words(0, 0, on_scalar)
+        turn(0, 1, 5)
+        pair_words(0, 1, on_vector)
+        gain_to_partitions(1)
+        quantise_delta(0, 0, 1)
+        quantise_delta(0, 1, 1)
+        turn(1, 0, 6)
+        pair_words(1, 0, on_scalar)
+        turn(1, 1, 7)
+        pair_words(1, 1, on_vector)
         for fc in range(4):
-            z_bank[(0, fc)] = bank(fc)
+            first_pass(0, fc, 0, fc)
+        sort_words(2, 0, on_vector)
+        quantise_delta(1, 0, 1)
+        sort_words(2, 1, on_vector)
+        quantise_delta(1, 1, 1)
+        for a in range(2):
+            turn(2, a, 4 + a)
+            pair_words(2, a, on_scalar)
+        for fc in range(4):
+            first_pass(0, fc, 1)
+        sort_words(3, 0, on_vector)
+        sort_words(3, 1, on_vector)
+        quantise_delta(2, 0, 1)
+        quantise_delta(2, 1, 1)
+        turn(3, 0, 6)
+        pair_words(3, 0, on_scalar)
+        turn(3, 1, 7)
+        pair_words(3, 1, on_vector)
+        for fc in range(4):
+            first_pass(0, fc, 2)
+        quantise_delta(3, 0, 1)
+        quantise_delta(3, 1, 1)
         for k in range(2):
-            for fc in range(4):
-                first_pass(0, fc, k)
+            first_pass(0, 4, k, 4)
+        clip(0, 0)
         for fc in range(4):
-            for k in range(2, PASSES):
-                first_pass(0, fc, k)
+            first_pass(0, fc, 3)
             scale_rows(0, fc)
-        sort_words(4, on_vector)
-        sort_words(5, on_vector)
-        quantise_x(0, 0)
-        for k in range(PASSES):
-            turn(4, k, 4 + k)
-            turn(5, k)
-            pair_words(2, k, on_scalar)
-        turn_back(0, 0, 0)
-        abs_w(0)
-        quantise_delta(1, 0, 0, 256)
-        for fc in (4, 5):
-            z_bank[(0, fc)] = bank(fc - 3)
-        for b in range(2):
-            for fc in (4, 5):
-                for k in (2 * b, 2 * b + 1):
-                    first_pass(0, fc, k)
-        pair_back(0, 0, on_scalar)
-        compare(0)
-        sort_words(6, on_vector)
+        for k in range(2, 4):
+            first_pass(0, 4, k)
         scale_rows(0, 4)
-        first_product(0, 6, 3)
+        interleave(0, 0, 2, on_vector)
+        first_product(0, 5, 5)
         scale_rows(0, 5)
-        quantise_delta(1, 1, 0, 256)
-        sort_words(7, on_vector)
-        quantise_delta(1, 2, 0, 256)
-        clip(0, 1)
-        quantise_delta(1, 3, 0, 256)
-        scale_rows(0, 6)
-        for i in (6, 7):
-            for k in range(PASSES):
-                turn(i, k, 4 + k)
-        turn_back(0, 2, 0)
-        interleave(0, 2, on_vector)
-        for k in range(PASSES):
-            pair_words(3, k, on_scalar)
-        first_product(0, 7, 1)
-        quantise_delta(1, 0, 256, 256)
-        quantise_delta(1, 1, 256, 256)
+        sort_words(4, 0, on_vector)
+        sort_words(5, 0, on_vector)
+        interleave(0, 2, 2, on_vector)
+        sort_words(4, 1, on_vector)
+        sort_words(5, 1, on_vector)
+        quantise_x(0, 0)
+        turn_back(0, 0, 6)
+        turn_back(0, 2, 7)
+        for a in range(2):
+            turn(4, a, a)
+        pair_back(0, 0, on_scalar)
+        pair_back(0, 2, on_vector)
+        for a in range(2):
+            pair_words(4, a, on_scalar)
         clip(1, 0)
-        quantise_delta(1, 2, 256, 256)
-        quantise_delta(1, 3, 256, 256)
-        clip(1, 1)
-        interleave(0, 3, on_vector)
-        pair_back(0, 2, on_scalar)
-        first_product(1, 0, 2)
-        scale_rows(0, 7)
-        interleave(1, 0, on_scalar)
+        first_product(0, 6, 2)
+        scale_rows(0, 6)
+        quantise_delta(4)
         quantise_e(0, 0, 4)
-        first_product(1, 1, 3)
-        scale_rows(1, 0)
-        quantise_x(0, 1)
-        first_product(1, 2, 4)
-        scale_rows(1, 1)
-        abs_w(1)
-        first_product(1, 3, 5)
-        scale_rows(1, 2)
-        abs_w(2)
-        compare(1)
-        first_product(1, 4, 6)
-        scale_rows(1, 3)
-        interleave(1, 1, on_scalar)
-        compare(2)
+        for a in range(2):
+            turn(5, a, 3 + a)
+            pair_words(5, a, on_scalar)
+        turn_back(0, 4, 5)
+        pair_back(0, 4, on_scalar)
+        interleave(1, 0, 1, on_scalar)
+        sort_words(6, 0, on_vector)
+        sort_words(6, 1, on_vector)
+        sort_words(7, 0, on_vector)
+        for fc in range(4):
+            first_pass(1, fc, 0, (6 + fc) % BANKS)
+        quantise_delta(5)
+        sort_words(7, 1, on_vector)
+        for a in range(2):
+            turn(6, a, 2 + a)
+            pair_words(6, a, on_scalar)
+        interleave(1, 1, 1, on_scalar)
+        abs_w(0)
+        interleave(1, 2, 1, on_vector)
+        quantise_delta(6, 0, 1)
+        interleave(1, 3, 1, on_vector)
+        for fc in range(4):
+            first_pass(1, fc, 1)
+        quantise_delta(6, 1, 1)
+        for a in range(2):
+            turn(7, a, 4 + a)
+            pair_words(7, a, on_scalar)
+        clip(0, 1)
         quantise_x(1, 0)
-        turn_back(0, 4, 7)
-        turn_back(0, 6, 0)
-        turn_back(1, 0, 1)
-        turn_back(1, 2, 2)
+        for fc in range(4):
+            first_pass(1, fc, 2)
+        quantise_delta(7, 0, 1)
+        quantise_delta(7, 1, 1)
+        interleave(0, 4, 2, on_scalar)
+        for k in range(3):
+            first_pass(0, 7, k, 2)
+        for fc in range(4):
+            first_pass(1, fc, 3)
+            scale_rows(1, fc)
+        first_pass(0, 7, 3)
+        compare(0)
+        abs_w(1)
+        clip(1, 1)
+        compare(1)
+        interleave(0, 6, 2, on_vector)
+        abs_w(2)
+        first_product(1, 4, 3)
+        turn_back(1, 0, 4)
+        turn_back(1, 2, 5)
         pair_back(1, 0, on_scalar)
         pair_back(1, 2, on_scalar)
+        scale_rows(0, 7)
         scale_rows(1, 4)
-        abs_w(3)
-        first_product(1, 5, 3)
-        scale_rows(1, 5)
-        interleave(1, 2, on_scalar)
+        quantise_x(0, 1)
+        first_product(1, 5, 6)
         quantise_e(1, 0, 4)
-        first_product(1, 6, 4)
-        pair_back(0, 4, on_scalar)
-        scale_rows(1, 6)
-        interleave(1, 3, on_vector)
-        second_product(0, 5)
-        second_product(1, 1)
-        first_product(1, 7, 6)
-        pair_back(0, 6, on_scalar)
-        scale_rows(1, 7)
+        scale_rows(1, 5)
+        interleave(1, 4, 2, on_scalar)
+        interleave(1, 6, 2, on_scalar)
+        for k in range(2):
+            first_pass(1, 6, k, 7)
+        compare(2)
+        second_pass(0, 0, 0)
+        second_pass(1, 0, 1)
+        second_pass(0, 1)
+        second_pass(1, 1)
         apply_mask(0)
         apply_mask(1)
-        compare(3)
-        quantise_x(1, 1)
-        second_product(2, 2)
-        second_product(3, 7)
-        quantise_e(0, 4, 4)
+        abs_w(3)
+        for unit in (2, 3):
+            second_product(unit, 2 * unit - 2)
+            apply_mask(unit)
+        for k in range(2, 4):
+            first_pass(1, 6, k)
+        scale_rows(1, 6)
+        turn_back(0, 6, 5)
         turn_back(1, 4, 3)
-        turn_back(1, 6, 4)
+        pair_back(0, 6, on_scalar)
+        first_product(1, 7, 6)
+        scale_rows(1, 7)
         pair_back(1, 4, on_scalar)
+        quantise_x(1, 1)
+        compare(3)
+        second_product(4, 0)
+        second_product(5, 1)
+        quantise_e(0, 4, 4)
+        apply_mask(4)
+        quantise_e(1, 4, 2)
+        apply_mask(5)
+        turn_back(1, 6, 2)
         pair_back(1, 6, on_scalar)
-        apply_mask(2)
-        apply_mask(3)
-        for unit in range(4, 16):
-            second_product(unit, (0, 5, 1, 6, 2, 7, 3, 4)[(unit - 4) % BANKS])
-            if unit in (6, 9,):
-                apply_mask_pooled(unit)
-            else:
-                apply_mask(unit)
-            if unit - 2 in (6, 9,):
-                store(unit - 2)
-            if unit == 4:
-                quantise_e(1, 4, 4)
+        second_product(6, 4)
+        second_product(7, 7)
+        quantise_e(1, 6, 2)
+        apply_mask(6)
+        apply_mask(7)
+        second_pass(8, 0, 5)
+        second_pass(9, 0, 3)
+        second_pass(8, 1)
+        second_pass(9, 1)
+        apply_mask_pooled(8)
+        apply_mask(9)
+        for unit in range(10, 16):
+            second_product(unit, (6, 0, 1, 2, 4, 7)[unit - 10])
+            apply_mask(unit)
+            if unit == 10:
+                store(8)

@@ -208,8 +208,8 @@ def tile_straight_through_weight_gradient_s9_kernel(
                 in_=e_grp[g][:, cols, :].rearrange("p n t -> p (n t)"),
             )
 
-        def clip(g, a):
-            for j in range(4):
+        def clip(g, a, rows=range(4)):
+            for j in rows:
                 row = x_sb[g][a][:, j, :]
                 nc.vector.tensor_scalar(
                     out=row, in0=row, scalar1=lo_sb[:, g, j : j + 1], scalar2=hi_sb[:, g, j : j + 1], op0=OP.max, op1=OP.min
@@ -217,6 +217,9 @@ def tile_straight_through_weight_gradient_s9_kernel(
 
         def interleave(g, ct, count, copy):
             cols = slice(P * ct, P * (ct + count))
+            if copy is on_pool:
+                rows = x_sb[g][ct // 4][:, :, P * (ct % 4) : P * (ct % 4 + count)]
+                return copy(out=x_grp[g][:, cols, :], in_=rows.rearrange("p j c -> p c j"))
             copy(
                 out=x_grp[g][:, cols, :].rearrange("p (c i) j -> p c j i", i=4),
                 in_=x_sb[g][ct // 4][:, :, P * (ct % 4) : P * (ct % 4 + count)].rearrange("p j (c i) -> p c j i", i=4),
@@ -234,11 +237,12 @@ def tile_straight_through_weight_gradient_s9_kernel(
             bits = w_sb[a][:].rearrange("p c f -> p (c f)").bitcast(I32)
             nc.vector.tensor_scalar(out=bits, in0=bits, scalar1=0x7FFF7FFF, scalar2=None, op0=OP.bitwise_and)
 
-        def compare(a):
+        def compare(a, first=0, count=2):
+            rows = w_sb[a][:, first : first + count, :]
             nc.vector.tensor_tensor(
-                out=w_sb[a][:],
-                in0=w_sb[a][:],
-                in1=r_all[:].unsqueeze(1).to_broadcast([P, 2, F]),
+                out=rows,
+                in0=rows,
+                in1=r_all[:].unsqueeze(1).to_broadcast([P, count, F]),
                 op=OP.is_le,
             )
 
@@ -277,6 +281,9 @@ def tile_straight_through_weight_gradient_s9_kernel(
             keep_mask = w_sb[ct // 2][:, ct % 2, h * HALF : (h + 1) * HALF]
             nc.scalar.copy(out=res[unit][:], in_=o_bank[unit][:])
             nc.gpsimd.tensor_tensor(out=res[unit][:], in0=res[unit][:], in1=keep_mask, op=OP.mult)
+
+        def on_pool(out, in_):
+            nc.gpsimd.tensor_scalar(out=out, in0=in_, scalar1=1.0, scalar2=0.0, op0=OP.mult, op1=OP.add)
 
         on_vector, on_scalar = nc.vector.tensor_copy, nc.scalar.copy
 
@@ -362,7 +369,6 @@ def tile_straight_through_weight_gradient_s9_kernel(
         sort_words(4, 0, on_vector)
         sort_words(5, 0, on_vector)
         interleave(0, 2, 2, on_vector)
-        sort_words(4, 1, on_vector)
         sort_words(5, 1, on_vector)
         quantise_x(0, 0)
         turn_back(0, 0, 6)
@@ -376,112 +382,111 @@ def tile_straight_through_weight_gradient_s9_kernel(
         clip(1, 0)
         first_product(0, 6, 2)
         scale_rows(0, 6)
-        quantise_delta(4)
         quantise_e(0, 0, 4)
         for a in range(2):
             turn(5, a, 3 + a)
             pair_words(5, a, on_scalar)
         turn_back(0, 4, 5)
         pair_back(0, 4, on_scalar)
-        interleave(1, 0, 1, on_scalar)
         sort_words(6, 0, on_vector)
-        sort_words(6, 1, on_vector)
-        sort_words(7, 0, on_vector)
-        for fc in range(4):
-            first_pass(1, fc, 0, (6 + fc) % BANKS)
-        quantise_delta(5)
-        sort_words(7, 1, on_vector)
+        quantise_delta(4)
+        for k in range(2):
+            first_pass(0, 7, k, 6)
         for a in range(2):
-            turn(6, a, 2 + a)
+            turn(6, a, (7 + a) % BANKS)
             pair_words(6, a, on_scalar)
-        interleave(1, 1, 1, on_scalar)
+        sort_words(7, 0, on_vector)
+        sort_words(7, 1, on_vector)
+        interleave(1, 0, 2, on_vector)
+        for fc in range(4):
+            first_pass(1, fc, 0, 1 + fc)
+        for k in range(2, 4):
+            first_pass(0, 7, k)
+        interleave(1, 2, 1, on_scalar)
+        scale_rows(0, 7)
+        quantise_delta(5)
         abs_w(0)
-        interleave(1, 2, 1, on_vector)
-        quantise_delta(6, 0, 1)
-        interleave(1, 3, 1, on_vector)
-        for fc in range(4):
-            first_pass(1, fc, 1)
-        quantise_delta(6, 1, 1)
-        for a in range(2):
-            turn(7, a, 4 + a)
-            pair_words(7, a, on_scalar)
+        turn(7, 0, 5)
+        pair_words(7, 0, on_scalar)
+        turn(7, 1, 7)
+        pair_words(7, 1, on_scalar)
+        quantise_delta(6)
         clip(0, 1)
-        quantise_x(1, 0)
-        for fc in range(4):
-            first_pass(1, fc, 2)
-        quantise_delta(7, 0, 1)
-        quantise_delta(7, 1, 1)
+        abs_w(1)
+        quantise_e(0, 4, 2)
+        for k in (1, 2):
+            for fc in range(4):
+                first_pass(1, fc, k)
+        quantise_delta(7)
         interleave(0, 4, 2, on_scalar)
-        for k in range(3):
-            first_pass(0, 7, k, 2)
         for fc in range(4):
             first_pass(1, fc, 3)
             scale_rows(1, fc)
-        first_pass(0, 7, 3)
+        interleave(1, 3, 1, on_scalar)
         compare(0)
-        abs_w(1)
-        clip(1, 1)
-        compare(1)
-        interleave(0, 6, 2, on_vector)
         abs_w(2)
-        first_product(1, 4, 3)
-        turn_back(1, 0, 4)
-        turn_back(1, 2, 5)
+        compare(1)
+        abs_w(3)
+        clip(1, 1, range(3))
+        compare(2)
+        quantise_x(1, 0)
+        first_product(1, 4, 0)
+        for k in range(2):
+            first_pass(1, 5, k, 6)
+        turn_back(1, 0, 5)
+        turn_back(1, 2, 7)
         pair_back(1, 0, on_scalar)
         pair_back(1, 2, on_scalar)
-        scale_rows(0, 7)
         scale_rows(1, 4)
-        quantise_x(0, 1)
-        first_product(1, 5, 6)
-        quantise_e(1, 0, 4)
+        for k in range(2, 4):
+            first_pass(1, 5, k)
         scale_rows(1, 5)
-        interleave(1, 4, 2, on_scalar)
+        interleave(0, 6, 2, on_scalar)
+        quantise_e(1, 0, 4)
+        compare(3, 0, 1)
+        first_product(1, 6, 1)
+        clip(1, 1, range(3, 4))
+        interleave(1, 4, 2, on_pool)
         interleave(1, 6, 2, on_scalar)
-        for k in range(2):
-            first_pass(1, 6, k, 7)
-        compare(2)
-        second_pass(0, 0, 0)
-        second_pass(1, 0, 1)
+        scale_rows(1, 6)
+        second_pass(0, 0, 2)
+        second_pass(1, 0, 3)
         second_pass(0, 1)
         second_pass(1, 1)
         apply_mask(0)
         apply_mask(1)
-        abs_w(3)
-        for unit in (2, 3):
-            second_product(unit, 2 * unit - 2)
-            apply_mask(unit)
-        for k in range(2, 4):
-            first_pass(1, 6, k)
-        scale_rows(1, 6)
-        turn_back(0, 6, 5)
-        turn_back(1, 4, 3)
+        second_product(2, 4)
+        apply_mask(2)
+        turn_back(0, 6, 0)
+        turn_back(1, 4, 5)
         pair_back(0, 6, on_scalar)
-        first_product(1, 7, 6)
+        first_product(1, 7, 7)
         scale_rows(1, 7)
         pair_back(1, 4, on_scalar)
+        quantise_x(0, 1)
         quantise_x(1, 1)
-        compare(3)
-        second_product(4, 0)
-        second_product(5, 1)
-        quantise_e(0, 4, 4)
+        compare(3, 1, 1)
+        second_product(3, 6)
+        second_product(4, 1)
+        apply_mask(3)
+        quantise_e(0, 6, 2)
         apply_mask(4)
-        quantise_e(1, 4, 2)
-        apply_mask(5)
         turn_back(1, 6, 2)
         pair_back(1, 6, on_scalar)
+        second_product(5, 3)
         second_product(6, 4)
-        second_product(7, 7)
-        quantise_e(1, 6, 2)
+        second_product(7, 0)
+        apply_mask(5)
+        quantise_e(1, 4, 4)
         apply_mask(6)
-        apply_mask(7)
+        apply_mask_pooled(7)
         second_pass(8, 0, 5)
-        second_pass(9, 0, 3)
+        second_pass(9, 0, 7)
         second_pass(8, 1)
         second_pass(9, 1)
-        apply_mask_pooled(8)
+        apply_mask(8)
         apply_mask(9)
+        store(7)
         for unit in range(10, 16):
-            second_product(unit, (6, 0, 1, 2, 4, 7)[unit - 10])
+            second_product(unit, (6, 1, 2, 3, 4, 0)[unit - 10])
             apply_mask(unit)
-            if unit == 10:
-                store(8)

@@ -367,126 +367,136 @@ def tile_straight_through_weight_gradient_s9_kernel(
         first_product(0, 5, 5)
         scale_rows(0, 5)
         sort_words(4, 0, on_vector)
-        sort_words(5, 0, on_vector)
         interleave(0, 2, 2, on_vector)
+        sort_words(4, 1, on_vector)
+        sort_words(5, 0, on_vector)
         sort_words(5, 1, on_vector)
         quantise_x(0, 0)
-        turn_back(0, 0, 6)
-        turn_back(0, 2, 7)
-        for a in range(2):
-            turn(4, a, a)
+        for k in range(2):
+            first_pass(0, 6, k, 6)
+        turn(4, 0, 7)
+        turn_back(0, 0, 0)
+        turn(4, 1, 1)
+        pair_words(4, 0, on_scalar)
+        pair_words(4, 1, on_scalar)
         pair_back(0, 0, on_scalar)
-        pair_back(0, 2, on_vector)
-        for a in range(2):
-            pair_words(4, a, on_scalar)
         clip(1, 0)
-        first_product(0, 6, 2)
+        for k in range(2, 4):
+            first_pass(0, 6, k)
         scale_rows(0, 6)
-        quantise_e(0, 0, 4)
+        for k in range(2):
+            first_pass(0, 7, k, 2)
+        quantise_delta(4)
+        sort_words(6, 0, on_vector)
+        interleave(1, 0, 2, on_vector)
+        sort_words(6, 1, on_vector)
+        sort_words(7, 0, on_vector)
         for a in range(2):
             turn(5, a, 3 + a)
             pair_words(5, a, on_scalar)
+        turn_back(0, 2, 5)
+        pair_back(0, 2, on_scalar)
+        for fc in range(4):
+            first_pass(1, fc, 0, (6 + fc) % BANKS)
+        quantise_delta(5)
+        sort_words(7, 1, on_vector)
+        abs_w(0)
+        for a in range(2):
+            turn(6, a, 3 + a)
+            pair_words(6, a, on_scalar)
         turn_back(0, 4, 5)
         pair_back(0, 4, on_scalar)
-        sort_words(6, 0, on_vector)
-        quantise_delta(4)
-        for k in range(2):
-            first_pass(0, 7, k, 6)
-        for a in range(2):
-            turn(6, a, (7 + a) % BANKS)
-            pair_words(6, a, on_scalar)
-        sort_words(7, 0, on_vector)
-        sort_words(7, 1, on_vector)
-        interleave(1, 0, 2, on_vector)
+        quantise_e(0, 0, 4)
         for fc in range(4):
-            first_pass(1, fc, 0, 1 + fc)
-        for k in range(2, 4):
-            first_pass(0, 7, k)
-        interleave(1, 2, 1, on_scalar)
-        scale_rows(0, 7)
-        quantise_delta(5)
-        abs_w(0)
-        turn(7, 0, 5)
-        pair_words(7, 0, on_scalar)
-        turn(7, 1, 7)
-        pair_words(7, 1, on_scalar)
+            first_pass(1, fc, 1)
         quantise_delta(6)
         clip(0, 1)
+        interleave(1, 2, 1, on_scalar)
+        for a in range(2):
+            turn(7, a, 3 + a)
+            pair_words(7, a, on_scalar)
         abs_w(1)
-        quantise_e(0, 4, 2)
-        for k in (1, 2):
-            for fc in range(4):
-                first_pass(1, fc, k)
+        compare(0, 0, 1)
+        for fc in range(4):
+            first_pass(1, fc, 2)
         quantise_delta(7)
         interleave(0, 4, 2, on_scalar)
+        for k in range(2, 4):
+            first_pass(0, 7, k)
+        first_pass(1, 4, 0, 5)
         for fc in range(4):
             first_pass(1, fc, 3)
             scale_rows(1, fc)
-        interleave(1, 3, 1, on_scalar)
-        compare(0)
+        interleave(1, 3, 1, on_vector)
+        compare(0, 1, 1)
         abs_w(2)
         compare(1)
-        abs_w(3)
         clip(1, 1, range(3))
-        compare(2)
         quantise_x(1, 0)
-        first_product(1, 4, 0)
+        compare(2)
+        abs_w(3)
+        for k in range(1, 4):
+            first_pass(1, 4, k)
         for k in range(2):
-            first_pass(1, 5, k, 6)
-        turn_back(1, 0, 5)
-        turn_back(1, 2, 7)
+            first_pass(1, 5, k, 3)
+        turn_back(1, 0, 4)
+        turn_back(1, 2, 6)
         pair_back(1, 0, on_scalar)
         pair_back(1, 2, on_scalar)
+        scale_rows(0, 7)
         scale_rows(1, 4)
         for k in range(2, 4):
             first_pass(1, 5, k)
         scale_rows(1, 5)
         interleave(0, 6, 2, on_scalar)
         quantise_e(1, 0, 4)
+        quantise_e(0, 4, 2)
         compare(3, 0, 1)
-        first_product(1, 6, 1)
+        first_product(1, 6, 7)
         clip(1, 1, range(3, 4))
         interleave(1, 4, 2, on_pool)
         interleave(1, 6, 2, on_scalar)
         scale_rows(1, 6)
-        second_pass(0, 0, 2)
-        second_pass(1, 0, 3)
+        second_pass(0, 0, 0)
+        second_pass(1, 0, 1)
         second_pass(0, 1)
         second_pass(1, 1)
         apply_mask(0)
         apply_mask(1)
         second_product(2, 4)
         apply_mask(2)
-        turn_back(0, 6, 0)
+        turn_back(0, 6, 6)
         turn_back(1, 4, 5)
         pair_back(0, 6, on_scalar)
-        first_product(1, 7, 7)
+        first_product(1, 7, 3)
         scale_rows(1, 7)
         pair_back(1, 4, on_scalar)
         quantise_x(0, 1)
         quantise_x(1, 1)
         compare(3, 1, 1)
-        second_product(3, 6)
-        second_product(4, 1)
+        second_product(3, 2)
+        second_product(4, 7)
         apply_mask(3)
         quantise_e(0, 6, 2)
         apply_mask(4)
-        turn_back(1, 6, 2)
+        quantise_e(1, 4, 2)
+        turn_back(1, 6, 0)
         pair_back(1, 6, on_scalar)
-        second_product(5, 3)
+        second_product(5, 1)
         second_product(6, 4)
-        second_product(7, 0)
+        second_product(7, 6)
         apply_mask(5)
-        quantise_e(1, 4, 4)
+        quantise_e(1, 6, 2)
         apply_mask(6)
-        apply_mask_pooled(7)
+        apply_mask(7)
         second_pass(8, 0, 5)
-        second_pass(9, 0, 7)
+        second_pass(9, 0, 3)
         second_pass(8, 1)
         second_pass(9, 1)
-        apply_mask(8)
+        apply_mask_pooled(8)
         apply_mask(9)
-        store(7)
         for unit in range(10, 16):
-            second_product(unit, (6, 1, 2, 3, 4, 0)[unit - 10])
+            second_product(unit, (2, 7, 0, 1, 4, 6)[unit - 10])
             apply_mask(unit)
+            if unit == 10:
+                store(8)

from contextlib import ExitStack

import concourse.mybir as mybir
from concourse.masks import make_identity

T, O, F, C = 1024, 2048, 1024, 1024
FLOPS = 2 * T * O * F + 2 * T * F * C

F32 = mybir.dt.float32
BF16 = mybir.dt.bfloat16
I32 = mybir.dt.int32
U32 = mybir.dt.uint32
U8 = mybir.dt.uint8
E4M3 = mybir.dt.float8_e4m3fn_x4
E5M2 = mybir.dt.float8_e5m2_x4
E2M1 = mybir.dt.float4_e2m1fn_x4
OP = mybir.AluOpType
ACT = mybir.ActivationFunctionType

P = 128
PASSES = O // 512
GROUPS = T // 512
STEPS = GROUPS * PASSES
ROW_TILES = C // P
HALF = 512
BANKS = 8
LINE = 256


def tile_straight_through_weight_gradient_s9_kernel(
    tc, delta, v_words, v_scales, gain, x, lo, hi, w, r, out
):
    nc = tc.nc
    with ExitStack() as ctx:
        keep = ctx.enter_context(tc.tile_pool(name="keep", bufs=1))
        stage = ctx.enter_context(tc.tile_pool(name="stage", bufs=3))
        outs = ctx.enter_context(tc.tile_pool(name="outs", bufs=10))
        psum = ctx.enter_context(tc.psum_pool(name="psum", bufs=1))
        ctx.enter_context(tc.manual_schedule())

        v_planes = [keep.tile([P, PASSES, HALF], U8, name=f"v_planes{h}", align_bytes=LINE) for h in range(2)]
        for h in range(2):
            nc.vector.memset(v_planes[h][:].rearrange("p g n -> p (g n)").bitcast(I32), 0)
        ident = keep.tile([P, P], F32, name="ident")
        make_identity(nc, ident[:])

        gain_rows = keep.tile([F // P, P], BF16, name="gain_rows")
        gain_pad = keep.tile([P, P], F32, name="gain_pad")
        gain_part = keep.tile([P, F // P], F32, name="gain_part")
        r_col = keep.tile([P, F // P], BF16, name="r_col")
        r_all = keep.tile([P, F], BF16, name="r_all")
        lo_sb = keep.tile([P, GROUPS, 4], BF16, name="lo_sb")
        hi_sb = keep.tile([P, GROUPS, 4], BF16, name="hi_sb")
        d_head = [[keep.tile([P, 2 * 512], BF16, name=f"d_head{k}_{a}", align_bytes=LINE) for a in range(2)] for k in range(PASSES)]
        d_late = [[keep.tile([P, 2 * 1024], BF16, name=f"d_late{b}_{a}", align_bytes=LINE) for a in range(2)] for b in range(2)]
        v_head = [keep.tile([P, F], U8, name=f"v_head{k}", align_bytes=LINE) for k in range(PASSES)]
        v_late = [keep.tile([P, 2, F], U8, name=f"v_late{b}", align_bytes=LINE) for b in range(2)]
        x_sb = [[keep.tile([P, 4, HALF], BF16, name=f"x_sb{g}_{a}", align_bytes=LINE) for a in range(2)] for g in range(GROUPS)]
        w_sb = [keep.tile([P, 2, F], BF16, name=f"w_sb{a}", align_bytes=LINE) for a in range(ROW_TILES // 2)]

        d_v = delta.rearrange("(g i p) (k n) -> g k p i n", p=P, i=4, n=512)
        d_wide = delta.rearrange("(g i p) (b n) -> g b p i n", p=P, i=4, n=1024)
        x_v = x.rearrange("(g p j) c -> g p j c", p=P, j=4)
        w_v = w.rearrange("(ct p) f -> p ct f", p=P)
        words_v = v_words.rearrange("g p b -> p g b")
        scales_v = v_scales.rearrange("g q n -> q g n").bitcast(I32)

        def load_head(k, a):
            nc.sync.dma_start(out=d_head[k][a][:].rearrange("p (i n) -> p i n", i=2), in_=d_v[0, k, :, 2 * a : 2 * a + 2, :])

        def load_late(b, a):
            nc.sync.dma_start(out=d_late[b][a][:].rearrange("p (i n) -> p i n", i=2), in_=d_wide[1, b, :, 2 * a : 2 * a + 2, :])

        def load_v_scales(h):
            for s in range(4):
                nc.sync.dma_start(
                    out=v_planes[h][s:P:32, :, :].bitcast(I32),
                    in_=scales_v[s:16:4, :, h * P : (h + 1) * P],
                )

        def load_v_head(k):
            nc.sync.dma_start(out=v_head[k][:], in_=v_words[k, :, 0:F])

        def load_v_late(b):
            nc.sync.dma_start(out=v_late[b][:], in_=words_v[:, 2 * b : 2 * b + 2, F : 2 * F])

        def load_x(g, a):
            nc.sync.dma_start(out=x_sb[g][a][:], in_=x_v[g, :, :, a * HALF : (a + 1) * HALF])

        def load_w(a):
            nc.sync.dma_start(out=w_sb[a][:], in_=w_v[:, 2 * a : 2 * a + 2, :])

        d_codes = [keep.tile([P, 512], U32, name=f"d_codes{s}", align_bytes=LINE) for s in range(STEPS)]
        d_scales = [keep.tile([P, 512], U8, name=f"d_scales{s}", align_bytes=LINE) for s in range(STEPS)]
        x_grp = [keep.tile([P, C, 4], BF16, name=f"x_grp{g}", align_bytes=LINE) for g in range(GROUPS)]
        x_codes = [keep.tile([P, C], U32, name=f"x_codes{g}", align_bytes=LINE) for g in range(GROUPS)]
        x_scales = [keep.tile([P, C], U8, name=f"x_scales{g}", align_bytes=LINE) for g in range(GROUPS)]
        e_grp = [keep.tile([P, F, 4], BF16, name=f"e_grp{g}", align_bytes=LINE) for g in range(GROUPS)]
        e_codes = [keep.tile([P, F], U32, name=f"e_codes{g}", align_bytes=LINE) for g in range(GROUPS)]
        e_scales = [keep.tile([P, F], U8, name=f"e_scales{g}", align_bytes=LINE) for g in range(GROUPS)]

        def bank(n):
            return psum.tile([P, 512], F32, name=f"bank{n}", tag=f"bank{n}")

        z_bank, e_rows, b_bank = {}, {}, {}
        d_sorted, t_bank, d_words, o_bank, res = {}, {}, {}, {}, {}

        def spread_r(n):
            ps = bank(n)
            words = r_col[:].bitcast(F32)
            for c in range(4):
                nc.tensor.transpose(ps[:, c::4], words[:, c : c + 1].to_broadcast([P, P]), ident[:])
            nc.vector.tensor_copy(out=r_all[:].bitcast(F32), in_=ps[:])

        def gain_to_partitions(n):
            ps = bank(n)
            nc.tensor.transpose(ps[:, 0:P], gain_pad[:], ident[:])
            nc.scalar.copy(out=gain_part[:], in_=ps[:, 0 : F // P])

        def raw_words(s, a):
            if s < PASSES:
                return d_head[s][a][:].bitcast(F32).rearrange("p (e n) -> p e n", e=2)
            k = s - PASSES
            return d_late[k // 2][a][:].bitcast(F32).rearrange("p (e n) -> p e n", e=2)[:, :, 256 * (k % 2) : 256 * (k % 2 + 1)]

        def sort_words(s, a, copy):
            d_sorted[(s, a)] = stage.tile([P, 512], F32, name="d_sorted", bufs=4)
            copy(
                out=d_sorted[(s, a)][:].rearrange("p (e u m j) -> p e m u j", e=2, u=2, j=2),
                in_=raw_words(s, a).rearrange("p e (m j u) -> p e m u j", u=2, j=2),
            )

        def turn(s, a, n):
            t_bank[(s, a)] = ps = bank(n)
            for e in range(2):
                for u in range(2):
                    if (s, a) in d_sorted:
                        src = d_sorted[(s, a)][:, (2 * e + u) * P : (2 * e + u + 1) * P]
                    else:
                        src = raw_words(s, a)[:, e, u:256:2]
                    nc.tensor.transpose(ps[:, (2 * e + u) * P : (2 * e + u + 1) * P], src, ident[:])

        def pair_words(s, a, copy):
            if a == 0:
                d_words[s] = stage.tile([P, 512, 4], BF16, name="d_words", align_bytes=LINE)
            words = d_words[s][:, 256 * a : 256 * (a + 1), :].rearrange("p m t -> p (m t)").bitcast(F32)
            copy(
                out=words.rearrange("p (e m u) -> p e m u", e=2, u=2),
                in_=t_bank[(s, a)][:].rearrange("p (e u m) -> p e m u", e=2, u=2),
            )

        def quantise_delta(s, first=0, count=2):
            cols = slice(256 * first, 256 * (first + count))
            nc.vector.quantize_mx(
                out=d_codes[s][:, cols].bitcast(E4M3),
                scales=d_scales[s][:, cols],
                in_=d_words[s][:, cols, :].rearrange("p m t -> p (m t)"),
            )

        def first_pass(g, fc, k, n=None):
            h, n0 = fc // 4, P * (fc % 4)
            if k == 0:
                z_bank[(g, fc)] = bank(n)
            codes = v_head[k][:] if h == 0 else v_late[k // 2][:, k % 2, :]
            nc.tensor.matmul_mx(
                out=z_bank[(g, fc)][:],
                lhsT=codes[:, 2 * n0 : 2 * (n0 + P)].bitcast(E2M1),
                lhsT_scale=v_planes[h][:, k, n0 : n0 + P],
                rhs=d_codes[PASSES * g + k][:].bitcast(E4M3),
                rhs_scale=d_scales[PASSES * g + k][:],
                start=(k == 0),
                stop=(k == PASSES - 1),
            )

        def first_product(g, fc, n):
            for k in range(PASSES):
                first_pass(g, fc, k, n)

        def scale_rows(g, fc, on_vector=False):
            e_rows[(g, fc)] = stage.tile([P, 2, P, 2], BF16, name="e_rows", bufs=10)
            src = z_bank[(g, fc)][:].rearrange("p (m u e) -> p u m e", u=2, e=2)
            if on_vector:
                nc.vector.tensor_scalar(
                    out=e_rows[(g, fc)][:], in0=src, scalar1=gain_part[:, fc : fc + 1], scalar2=None, op0=OP.mult
                )
            else:
                nc.scalar.activation(out=e_rows[(g, fc)][:], in_=src, func=ACT.Copy, scale=gain_part[:, fc : fc + 1])

        def turn_back(g, fc, n):
            b_bank[(g, fc)] = ps = bank(n)
            for c in range(2):
                for u in range(2):
                    words = e_rows[(g, fc + c)][:, u, :, :].rearrange("p m e -> p (m e)").bitcast(F32)
                    nc.tensor.transpose(ps[:, (2 * c + u) * P : (2 * c + u + 1) * P], words, ident[:])

        def pair_back(g, fc, copy):
            words = e_grp[g][:, fc * P : (fc + 2) * P, :].rearrange("p n t -> p (n t)").bitcast(F32)
            copy(
                out=words.rearrange("p (c n u) -> p c n u", c=2, u=2),
                in_=b_bank[(g, fc)][:].rearrange("p (c u n) -> p c n u", c=2, u=2),
            )

        def quantise_e(g, fc, count):
            cols = slice(fc * P, (fc + count) * P)
            nc.vector.quantize_mx(
                out=e_codes[g][:, cols].bitcast(E5M2),
                scales=e_scales[g][:, cols],
                in_=e_grp[g][:, cols, :].rearrange("p n t -> p (n t)"),
            )

        def clip(g, a, rows=range(4)):
            for j in rows:
                row = x_sb[g][a][:, j, :]
                nc.vector.tensor_scalar(
                    out=row, in0=row, scalar1=lo_sb[:, g, j : j + 1], scalar2=hi_sb[:, g, j : j + 1], op0=OP.max, op1=OP.min
                )

        def interleave(g, ct, count, copy):
            cols = slice(P * ct, P * (ct + count))
            if copy is on_pool:
                rows = x_sb[g][ct // 4][:, :, P * (ct % 4) : P * (ct % 4 + count)]
                return copy(out=x_grp[g][:, cols, :], in_=rows.rearrange("p j c -> p c j"))
            copy(
                out=x_grp[g][:, cols, :].rearrange("p (c i) j -> p c j i", i=4),
                in_=x_sb[g][ct // 4][:, :, P * (ct % 4) : P * (ct % 4 + count)].rearrange("p j (c i) -> p c j i", i=4),
            )

        def quantise_x(g, a):
            cols = slice(512 * a, 512 * (a + 1))
            nc.vector.quantize_mx(
                out=x_codes[g][:, cols].bitcast(E4M3),
                scales=x_scales[g][:, cols],
                in_=x_grp[g][:, cols, :].rearrange("p c j -> p (c j)"),
            )

        def abs_w(a):
            bits = w_sb[a][:].rearrange("p c f -> p (c f)").bitcast(I32)
            nc.vector.tensor_scalar(out=bits, in0=bits, scalar1=0x7FFF7FFF, scalar2=None, op0=OP.bitwise_and)

        def compare(a, first=0, count=2):
            rows = w_sb[a][:, first : first + count, :]
            nc.vector.tensor_tensor(
                out=rows,
                in0=rows,
                in1=r_all[:].unsqueeze(1).to_broadcast([P, count, F]),
                op=OP.is_le,
            )

        def second_pass(unit, g, n=None):
            h, ct = unit // ROW_TILES, unit % ROW_TILES
            if g == 0:
                o_bank[unit] = bank(n)
            nc.tensor.matmul_mx(
                out=o_bank[unit][:],
                lhsT=x_codes[g][:, ct * P : (ct + 1) * P].bitcast(E4M3),
                lhsT_scale=x_scales[g][:, ct * P : (ct + 1) * P],
                rhs=e_codes[g][:, h * HALF : (h + 1) * HALF].bitcast(E5M2),
                rhs_scale=e_scales[g][:, h * HALF : (h + 1) * HALF],
                start=(g == 0),
                stop=(g == GROUPS - 1),
            )

        def second_product(unit, n):
            second_pass(unit, 0, n)
            second_pass(unit, 1)

        def store(unit):
            h, ct = unit // ROW_TILES, unit % ROW_TILES
            nc.sync.dma_start(out=out[ct * P : (ct + 1) * P, h * HALF : (h + 1) * HALF], in_=res[unit][:])

        def apply_mask(unit):
            h, ct = unit // ROW_TILES, unit % ROW_TILES
            res[unit] = outs.tile([P, HALF], F32, name="res", align_bytes=LINE)
            keep_mask = w_sb[ct // 2][:, ct % 2, h * HALF : (h + 1) * HALF]
            nc.vector.tensor_tensor(out=res[unit][:], in0=o_bank[unit][:], in1=keep_mask, op=OP.mult)
            store(unit)

        def apply_mask_pooled(unit):
            h, ct = unit // ROW_TILES, unit % ROW_TILES
            res[unit] = outs.tile([P, HALF], F32, name="res", align_bytes=LINE)
            keep_mask = w_sb[ct // 2][:, ct % 2, h * HALF : (h + 1) * HALF]
            nc.scalar.copy(out=res[unit][:], in_=o_bank[unit][:])
            nc.gpsimd.tensor_tensor(out=res[unit][:], in0=res[unit][:], in1=keep_mask, op=OP.mult)

        def on_pool(out, in_):
            nc.gpsimd.tensor_scalar(out=out, in0=in_, scalar1=1.0, scalar2=0.0, op0=OP.mult, op1=OP.add)

        on_vector, on_scalar = nc.vector.tensor_copy, nc.scalar.copy

        nc.scalar.dma_start(out=r_col[:], in_=r.rearrange("(p c) -> p c", p=P))
        nc.scalar.dma_start(out=gain_rows[:], in_=gain.rearrange("(c p) -> c p", p=P))
        nc.gpsimd.dma_start(out=lo_sb[:], in_=lo.rearrange("(g p j) -> p g j", p=P, j=4))
        nc.gpsimd.dma_start(out=hi_sb[:], in_=hi.rearrange("(g p j) -> p g j", p=P, j=4))
        for k in range(2):
            load_head(k, 0)
            load_head(k, 1)
        load_v_scales(0)
        load_v_head(0)
        for k in range(2, PASSES):
            load_head(k, 0)
            load_head(k, 1)
            load_v_head(k - 1)
        load_v_head(3)
        load_v_scales(1)
        load_v_late(0)
        load_x(0, 0)
        load_v_late(1)
        load_late(0, 0)
        load_late(0, 1)
        load_x(1, 0)
        load_late(1, 0)
        load_late(1, 1)
        load_w(0)
        load_x(0, 1)
        load_w(1)
        load_x(1, 1)
        load_w(2)
        load_w(3)

        nc.scalar.activation(out=gain_pad[:], in_=ident[:], func=ACT.Copy, scale=0.0)
        nc.vector.tensor_copy(out=gain_pad[0 : F // P, :], in_=gain_rows[:])
        spread_r(0)
        turn(0, 0, 4)
        pair_words(0, 0, on_scalar)
        turn(0, 1, 5)
        pair_words(0, 1, on_vector)
        gain_to_partitions(1)
        quantise_delta(0, 0, 1)
        quantise_delta(0, 1, 1)
        turn(1, 0, 6)
        pair_words(1, 0, on_scalar)
        turn(1, 1, 7)
        pair_words(1, 1, on_vector)
        for fc in range(4):
            first_pass(0, fc, 0, fc)
        sort_words(2, 0, on_vector)
        quantise_delta(1, 0, 1)
        sort_words(2, 1, on_vector)
        quantise_delta(1, 1, 1)
        for a in range(2):
            turn(2, a, 4 + a)
            pair_words(2, a, on_scalar)
        for fc in range(4):
            first_pass(0, fc, 1)
        sort_words(3, 0, on_vector)
        sort_words(3, 1, on_vector)
        quantise_delta(2, 0, 1)
        quantise_delta(2, 1, 1)
        turn(3, 0, 6)
        pair_words(3, 0, on_scalar)
        turn(3, 1, 7)
        pair_words(3, 1, on_vector)
        for fc in range(4):
            first_pass(0, fc, 2)
        quantise_delta(3, 0, 1)
        quantise_delta(3, 1, 1)
        for k in range(2):
            first_pass(0, 4, k, 4)
        clip(0, 0)
        for fc in range(4):
            first_pass(0, fc, 3)
            scale_rows(0, fc)
        for k in range(2, 4):
            first_pass(0, 4, k)
        scale_rows(0, 4)
        interleave(0, 0, 2, on_vector)
        first_product(0, 5, 5)
        scale_rows(0, 5)
        sort_words(4, 0, on_vector)
        interleave(0, 2, 2, on_vector)
        sort_words(4, 1, on_vector)
        sort_words(5, 0, on_vector)
        sort_words(5, 1, on_vector)
        quantise_x(0, 0)
        for k in range(2):
            first_pass(0, 6, k, 6)
        turn(4, 0, 7)
        turn_back(0, 0, 0)
        turn(4, 1, 1)
        pair_words(4, 0, on_scalar)
        pair_words(4, 1, on_scalar)
        pair_back(0, 0, on_scalar)
        clip(1, 0)
        for k in range(2, 4):
            first_pass(0, 6, k)
        scale_rows(0, 6)
        for k in range(2):
            first_pass(0, 7, k, 2)
        quantise_delta(4)
        sort_words(6, 0, on_vector)
        interleave(1, 0, 2, on_vector)
        sort_words(6, 1, on_vector)
        sort_words(7, 0, on_vector)
        for a in range(2):
            turn(5, a, 3 + a)
            pair_words(5, a, on_scalar)
        turn_back(0, 2, 5)
        pair_back(0, 2, on_scalar)
        for fc in range(4):
            first_pass(1, fc, 0, (6 + fc) % BANKS)
        quantise_delta(5)
        sort_words(7, 1, on_vector)
        abs_w(0)
        for a in range(2):
            turn(6, a, 3 + a)
            pair_words(6, a, on_scalar)
        turn_back(0, 4, 5)
        pair_back(0, 4, on_scalar)
        quantise_e(0, 0, 4)
        for fc in range(4):
            first_pass(1, fc, 1)
        quantise_delta(6)
        clip(0, 1)
        interleave(1, 2, 1, on_scalar)
        for a in range(2):
            turn(7, a, 3 + a)
            pair_words(7, a, on_scalar)
        abs_w(1)
        compare(0, 0, 1)
        for fc in range(4):
            first_pass(1, fc, 2)
        quantise_delta(7)
        interleave(0, 4, 2, on_scalar)
        for k in range(2, 4):
            first_pass(0, 7, k)
        first_pass(1, 4, 0, 5)
        for fc in range(4):
            first_pass(1, fc, 3)
            scale_rows(1, fc)
        interleave(1, 3, 1, on_vector)
        compare(0, 1, 1)
        abs_w(2)
        compare(1)
        clip(1, 1, range(3))
        quantise_x(1, 0)
        compare(2)
        abs_w(3)
        for k in range(1, 4):
            first_pass(1, 4, k)
        for k in range(2):
            first_pass(1, 5, k, 3)
        turn_back(1, 0, 4)
        turn_back(1, 2, 6)
        pair_back(1, 0, on_scalar)
        pair_back(1, 2, on_scalar)
        scale_rows(0, 7)
        scale_rows(1, 4)
        for k in range(2, 4):
            first_pass(1, 5, k)
        scale_rows(1, 5)
        interleave(0, 6, 2, on_scalar)
        quantise_e(1, 0, 4)
        quantise_e(0, 4, 2)
        compare(3, 0, 1)
        first_product(1, 6, 7)
        clip(1, 1, range(3, 4))
        interleave(1, 4, 2, on_pool)
        interleave(1, 6, 2, on_scalar)
        scale_rows(1, 6)
        second_pass(0, 0, 0)
        second_pass(1, 0, 1)
        second_pass(0, 1)
        second_pass(1, 1)
        apply_mask(0)
        apply_mask(1)
        second_product(2, 4)
        apply_mask(2)
        turn_back(0, 6, 6)
        turn_back(1, 4, 5)
        pair_back(0, 6, on_scalar)
        first_product(1, 7, 3)
        scale_rows(1, 7)
        pair_back(1, 4, on_scalar)
        quantise_x(0, 1)
        quantise_x(1, 1)
        compare(3, 1, 1)
        second_product(3, 2)
        second_product(4, 7)
        apply_mask(3)
        quantise_e(0, 6, 2)
        apply_mask(4)
        quantise_e(1, 4, 2)
        turn_back(1, 6, 0)
        pair_back(1, 6, on_scalar)
        second_product(5, 1)
        second_product(6, 4)
        second_product(7, 6)
        apply_mask(5)
        quantise_e(1, 6, 2)
        apply_mask(6)
        apply_mask(7)
        second_pass(8, 0, 5)
        second_pass(9, 0, 3)
        second_pass(8, 1)
        second_pass(9, 1)
        apply_mask_pooled(8)
        apply_mask(9)
        for unit in range(10, 16):
            second_product(unit, (2, 7, 0, 1, 4, 6)[unit - 10])
            apply_mask(unit)
            if unit == 10:
                store(8)
